import numpy as np
import ml_dtypes


def mxq(x, axis, fmt="e4m3"):
    dtype, down = {"e4m3": (ml_dtypes.float8_e4m3fn, 7), "e5m2": (ml_dtypes.float8_e5m2, 14)}[fmt]
    v = np.moveaxis(np.asarray(x, np.float32).astype(ml_dtypes.bfloat16).astype(np.float64), axis, -1)
    blocks = v.reshape(v.shape[:-1] + (-1, 32))
    amax = np.abs(blocks).max(-1, keepdims=True)
    byte = np.maximum(np.where(amax > 0, np.frexp(amax)[1] - 1 + 127, 0) - down, 1)
    scale = np.exp2(byte - 127.0)
    codes = (blocks / scale).astype(np.float32).astype(dtype).astype(np.float64)
    return np.moveaxis((codes * scale).reshape(v.shape), -1, axis)


WIDE = False


def mx_kscale(k):
    if not WIDE:
        return np.ones(k)
    levels = np.array([10, -10, 5, -5, 0])
    if k % 512:
        return np.exp2(np.random.permutation(np.resize(levels, k // 32))).repeat(32)
    a = np.empty((k // 512, 16))
    for p in range(k // 512):
        a[p, :8] = np.random.permutation(np.resize(levels, 8))
        for g in range(8):
            far = levels[np.abs(levels - a[p, g]) >= 10]
            a[p, g + 8] = far[np.random.randint(len(far))]
    return np.exp2(a.ravel()).repeat(32)


def f64(x):
    return np.asarray(x).astype(np.float64)


def striped(idx):
    return np.tile(idx.reshape(-1, 16).T, (8, 1)).astype(np.uint16)


def unstriped(offs):
    return offs[:16].T.reshape(-1).astype(np.int64)


E2M1 = np.array([0.0, 0.5, 1.0, 1.5, 2.0, 3.0, 4.0, 6.0, -0.0, -0.5, -1.0, -1.5, -2.0, -3.0, -4.0, -6.0])


def pack_weight(w, fmt):
    k, n = w.shape
    w = f64(np.asarray(w, np.float32).astype(ml_dtypes.bfloat16)).reshape(k // 32, 32, n)
    amax = np.abs(w).max(1)
    if fmt == "e4m3":
        byte = np.frexp(amax)[1] - 1 + 127 - 7
    else:
        mant, ex = np.frexp(amax / 6.0)
        byte = np.where(mant > 0.5, ex, ex - 1) + 127
    byte = np.clip(np.where(amax > 0, byte, 1), 1, 254)
    scaled = (w * np.exp2(127.0 - byte)[:, None, :]).reshape(k, n).astype(np.float32)
    by_word = np.ascontiguousarray(scaled.reshape(k // 512, 128, 4, n).transpose(0, 1, 3, 2))
    if fmt == "e4m3":
        words = by_word.astype(ml_dtypes.float8_e4m3fn).view(np.uint8)
    else:
        c = by_word.astype(ml_dtypes.float4_e2m1fn).view(np.uint8) & 0xF
        words = (c[..., 0::2] | (c[..., 1::2] << 4)).reshape(k // 512, 128, 2 * n)
    return np.ascontiguousarray(words), np.ascontiguousarray(byte.astype(np.uint8).reshape(k // 512, 16, n))


def unpack_weight(words, scales, fmt):
    g, _, n = scales.shape
    words = np.ascontiguousarray(words).reshape(g, 128, n, -1)
    if fmt == "e4m3":
        vals = words.view(ml_dtypes.float8_e4m3fn).astype(np.float64)
    else:
        nib = np.empty((g, 128, n, 4), np.uint8)
        nib[..., 0::2] = words & 0xF
        nib[..., 1::2] = words >> 4
        vals = E2M1[nib]
    vals = vals * np.repeat(np.exp2(scales.astype(np.float64) - 127.0), 8, axis=1)[..., None]
    return vals.transpose(0, 1, 3, 2).reshape(g * 512, n)


def gelu(v):
    return 0.5 * v * (1.0 + np.tanh(np.sqrt(2.0 / np.pi) * (v + 0.044715 * v**3)))


K, T, S, H, N = 1536, 2048, 1024, 1024, 384

def setup_inputs():
    n = np.random.standard_normal
    s, u = mx_kscale(K)[:, None], mx_kscale(H)[:, None]
    tab_words, tab_scales = pack_weight(n((K, T)) * s, "e4m3")
    offs = striped(np.random.permutation(T)[:S])
    w1 = (n((K, H)) / np.sqrt(K) / s * u.T).astype(np.float32)
    b1 = (0.3 * n(H) * u[:, 0]).astype(np.float32)
    qa_words, qa_scales = pack_weight(n((H, N)) * np.sqrt(2 / H) / u, "e2m1")
    qb = (n((H, N)) * np.sqrt(2 / H) / u).astype(np.float32)
    disc = (1 / (1 + np.exp(-1.5 - 0.7 * n(N)))).astype(np.float32)
    gT = n((N, T)).astype(np.float32)
    return dict(tab_words=tab_words, tab_scales=tab_scales, offs=offs, w1=w1, b1=b1,
                qa_words=qa_words, qa_scales=qa_scales, qb=qb, disc=disc, gT=gT)

def reference(tab_words, tab_scales, offs, w1, b1, qa_words, qa_scales, qb, disc, gT):
    v = unpack_weight(tab_words, tab_scales, "e4m3")[:, unstriped(offs)]
    g = f64(gT)[:, unstriped(offs)]
    h = np.maximum((mxq(f64(w1), 0, "e4m3").T @ v) + f64(b1)[:, None], 0.0)
    hq = mxq(h, 0, "e4m3")
    ya = unpack_weight(qa_words, qa_scales, "e2m1").T @ hq
    yb = mxq(f64(qb), 0, "e4m3").T @ hq
    return g + f64(disc)[:, None] * np.minimum(ya, yb)

@@ -1,0 +1,249 @@
+from contextlib import ExitStack
+
+import concourse.mybir as mybir
+
+K, T, S, H, N = 1536, 2048, 1024, 1024, 384
+FLOPS = 2 * K * H * S + 2 * 2 * H * N * S
+
+F32 = mybir.dt.float32
+BF16 = mybir.dt.bfloat16
+I32 = mybir.dt.int32
+U32 = mybir.dt.uint32
+U16 = mybir.dt.uint16
+U8 = mybir.dt.uint8
+FP8X4 = mybir.dt.float8_e4m3fn_x4
+FP4X4 = mybir.dt.float4_e2m1fn_x4
+RELU = mybir.ActivationFunctionType.Relu
+ALU = mybir.AluOpType
+
+P = 128
+PACK = 4
+K_PASS = P * PACK
+K_PASSES = K // K_PASS
+H_PASSES = H // K_PASS
+COLS = 512
+HALVES = S // COLS
+N_TILES = N // P
+LIST_COLS = COLS // 16
+
+
+def tile_list_twin_critic_targets_kernel(
+    tc, tab_words, tab_scales, offs, w1, b1, qa_words, qa_scales, qb, disc, gT, out
+):
+    nc = tc.nc
+    with ExitStack() as ctx:
+        keep = ctx.enter_context(tc.tile_pool(name="keep", bufs=1))
+        ring = ctx.enter_context(tc.tile_pool(name="ring", bufs=3))
+        psum = ctx.enter_context(tc.psum_pool(name="psum", bufs=8))
+
+        offsets = keep.tile([P, S // 16], U16, name="offsets")
+        nc.sync.dma_start(offsets[:], offs)
+
+        tab_sc = keep.tile([P, T // 4], I32, name="tab_sc", align_bytes=64)
+        qa_sc = keep.tile([P, H_PASSES, N // 4], I32, name="qa_sc", align_bytes=64)
+        warm = keep.tile([P, 8], F32, name="warm")
+        warm2 = keep.tile([P, 8], F32, name="warm2")
+        nc.vector.memset(tab_sc[:], 0)
+        nc.vector.memset(warm[:], 0.0)
+        nc.vector.memset(qa_sc[:], 0)
+        for q in range(4):
+            nc.scalar.dma_start(
+                tab_sc[32 * q : 32 * q + 4 * K_PASSES, :], tab_scales[:, 4 * q : 4 * q + 4, :].bitcast(I32)
+            )
+        bias = keep.tile([P, H_PASSES, PACK], F32, name="bias")
+        nc.scalar.dma_start(bias[:], b1.rearrange("(b p t) -> p b t", p=P, t=PACK))
+        nc.scalar.activation(warm2[:], warm[:], RELU)
+
+        w_raw, tab, qb_raw, rewards = {}, {}, {}, {}
+
+        def load_w(a, b):
+            w_raw[a, b] = keep.tile([P, PACK, K_PASS], F32, name="w_raw_%d_%d" % (a, b))
+            rows = w1[a * K_PASS : (a + 1) * K_PASS, b * K_PASS : (b + 1) * K_PASS]
+            nc.sync.dma_start(w_raw[a, b][:], rows.rearrange("(p j) c -> p j c", j=PACK))
+
+        def load_tab(a):
+            tab[a] = keep.tile([P, T], I32, name="tab_%d" % a, align_bytes=64)
+            nc.sync.dma_start(tab[a][:], tab_words[a].rearrange("p t i -> p (t i)").bitcast(I32))
+
+        for a in range(K_PASSES):
+            load_w(a, 0)
+            load_tab(a)
+        for a in range(K_PASSES):
+            load_w(a, 1)
+        for b in range(H_PASSES):
+            qb_raw[b] = keep.tile([P, PACK, N], F32, name="qb_raw_%d" % b)
+            nc.sync.dma_start(
+                qb_raw[b][:], qb[b * K_PASS : (b + 1) * K_PASS, :].rearrange("(p j) n -> p j n", j=PACK)
+            )
+        discount = keep.tile([P, N_TILES], F32, name="discount")
+        with nc.allow_non_contiguous_dma(reason="one discount a partition"):
+            nc.sync.dma_start(discount[:], disc.rearrange("(i p) -> p i", p=P))
+        for q in range(4):
+            nc.sync.dma_start(
+                qa_sc[32 * q : 32 * q + 4, :, :],
+                qa_scales[:, 4 * q : 4 * q + 4, :].rearrange("b r n -> r b n").bitcast(I32),
+            )
+        qa = keep.tile([P, H_PASSES, N // 2], I32, name="qa", align_bytes=64)
+        nc.sync.dma_start(qa[:], qa_words.rearrange("b p c -> p b c").bitcast(I32))
+        for i in range(N_TILES):
+            rewards[i] = keep.tile([P, T], F32, name="rewards_%d" % i, align_bytes=64)
+            nc.sync.dma_start(rewards[i][:], gT[i * P : (i + 1) * P, :])
+
+        def picks(u):
+            return offsets[:, u * LIST_COLS : (u + 1) * LIST_COLS]
+
+        v_sc, v_codes, w_bf, w_codes, w_sc = {}, {}, {}, {}, {}
+        banks, planes, h_bf, h_codes, h_sc, picked = {}, {}, {}, {}, {}, {}
+
+        def gather_scales(u):
+            v_sc[u] = keep.tile([P, COLS], U8, name="v_sc_%d" % u, align_bytes=64)
+            nc.vector.tensor_copy(v_sc[u][:], tab_sc[:].bitcast(U8).indirect(picks(u)))
+
+        def gather_words(a, u):
+            v_codes[a, u] = keep.tile([P, COLS], U32, name="v_codes_%d_%d" % (a, u), align_bytes=64)
+            nc.vector.tensor_copy(v_codes[a, u][:], tab[a][:].bitcast(U32).indirect(picks(u)))
+
+        def gather_rewards(i, u):
+            picked[i, u] = keep.tile([P, COLS], F32, name="picked_%d_%d" % (i, u))
+            nc.vector.tensor_copy(picked[i, u][:], rewards[i][:].indirect(picks(u)))
+
+        def cast_w(a, b, vector_m):
+            w_bf[a, b] = ring.tile([P, PACK * K_PASS], BF16, name="w_bf", align_bytes=64)
+            dst = w_bf[a, b][:].rearrange("p (t m j) -> p m j t", t=PACK, j=PACK)
+            src = w_raw[a, b][:].rearrange("p j (m t) -> p m j t", t=PACK)
+            if vector_m > 0:
+                nc.vector.tensor_copy(dst[:, 0:vector_m], src[:, 0:vector_m])
+            if vector_m < P:
+                nc.scalar.copy(dst[:, vector_m:P], src[:, vector_m:P])
+
+        def quantize_w(a, b):
+            w_codes[a, b] = keep.tile([P, K_PASS], U32, name="w_codes_%d_%d" % (a, b), align_bytes=64)
+            w_sc[a, b] = keep.tile([P, K_PASS], U8, name="w_sc_%d_%d" % (a, b), align_bytes=64)
+            nc.vector.quantize_mx(out=w_codes[a, b][:].bitcast(FP8X4), scales=w_sc[a, b][:], in_=w_bf[a, b][:])
+
+        def hidden_pass(a, b, u):
+            for t in range(PACK):
+                if a == 0:
+                    banks[b, u, t] = psum.tile([P, COLS], F32, name="bank")
+                cols = slice(t * P, (t + 1) * P)
+                nc.tensor.matmul_mx(
+                    out=banks[b, u, t][:],
+                    lhsT=w_codes[a, b][:, cols].bitcast(FP8X4),
+                    lhsT_scale=w_sc[a, b][:, cols],
+                    rhs=v_codes[a, u][:].bitcast(FP8X4),
+                    rhs_scale=v_sc[u][4 * a : P, :],
+                    start=(a == 0),
+                    stop=(a == K_PASSES - 1),
+                )
+
+        def relu_out(b, u):
+            planes[b, u] = ring.tile([P, PACK, COLS], BF16, name="planes")
+            for t in range(PACK):
+                nc.scalar.activation(planes[b, u][:, t, :], banks[b, u, t][:], RELU, bias=bias[:, b, t : t + 1])
+
+        def interleave_h(b, u):
+            h_bf[b, u] = ring.tile([P, COLS * PACK], BF16, name="h_bf", align_bytes=64, bufs=2)
+            nc.vector.tensor_copy(
+                h_bf[b, u][:].rearrange("p (c i t) -> p c t i", i=4, t=PACK),
+                planes[b, u][:].rearrange("p t (c i) -> p c t i", i=4),
+            )
+
+        def quantize_h(b, u):
+            h_codes[b, u] = keep.tile([P, COLS], U32, name="h_codes_%d_%d" % (b, u), align_bytes=64)
+            h_sc[b, u] = keep.tile([P, COLS], U8, name="h_sc_%d_%d" % (b, u), align_bytes=64)
+            nc.vector.quantize_mx(out=h_codes[b, u][:].bitcast(FP8X4), scales=h_sc[b, u][:], in_=h_bf[b, u][:])
+
+        qb_bf = keep.tile([P, H_PASSES * N * PACK], BF16, name="qb_bf", align_bytes=64)
+        qb_codes = keep.tile([P, H_PASSES * N], U32, name="qb_codes", align_bytes=64)
+        qb_sc = keep.tile([P, H_PASSES * N], U8, name="qb_sc", align_bytes=64)
+
+        def cast_qb(b):
+            dst = qb_bf[:, b * N * PACK : (b + 1) * N * PACK]
+            nc.scalar.copy(
+                dst.rearrange("p (c i t) -> p c t i", i=4, t=PACK),
+                qb_raw[b][:].rearrange("p t (c i) -> p c t i", i=4),
+            )
+
+        def quantize_qb(lo, hi):
+            nc.vector.quantize_mx(
+                out=qb_codes[:, lo:hi].bitcast(FP8X4), scales=qb_sc[:, lo:hi], in_=qb_bf[:, lo * PACK : hi * PACK]
+            )
+
+        def critics(i, u):
+            ya = psum.tile([P, COLS], F32, name="bank")
+            yb = psum.tile([P, COLS], F32, name="bank")
+            for b in range(H_PASSES):
+                nc.tensor.matmul_mx(
+                    out=ya[:],
+                    lhsT=qa[:, b, :].bitcast(U8)[:, 2 * i * P : 2 * (i + 1) * P].bitcast(FP4X4),
+                    lhsT_scale=qa_sc[:, b, :].bitcast(U8)[:, i * P : (i + 1) * P],
+                    rhs=h_codes[b, u][:].bitcast(FP8X4),
+                    rhs_scale=h_sc[b, u][:],
+                    start=(b == 0),
+                    stop=(b == H_PASSES - 1),
+                )
+            for b in range(H_PASSES):
+                cols = slice(b * N + i * P, b * N + (i + 1) * P)
+                nc.tensor.matmul_mx(
+                    out=yb[:],
+                    lhsT=qb_codes[:, cols].bitcast(FP8X4),
+                    lhsT_scale=qb_sc[:, cols],
+                    rhs=h_codes[b, u][:].bitcast(FP8X4),
+                    rhs_scale=h_sc[b, u][:],
+                    start=(b == 0),
+                    stop=(b == H_PASSES - 1),
+                )
+            ya_sb = ring.tile([P, COLS], F32, name="ya_sb")
+            nc.scalar.copy(ya_sb[:], ya[:])
+            least = ring.tile([P, COLS], F32, name="least")
+            nc.vector.tensor_tensor(least[:], yb[:], ya_sb[:], ALU.min)
+            return least
+
+        def finish(i, u, least):
+            target = ring.tile([P, COLS], F32, name="target", bufs=4)
+            nc.vector.scalar_tensor_tensor(
+                target[:], least[:], discount[:, i : i + 1], picked[i, u][:], ALU.mult, ALU.add
+            )
+            nc.sync.dma_start(out[i * P : (i + 1) * P, u * COLS : (u + 1) * COLS], target[:])
+
+        for u in range(HALVES):
+            gather_scales(u)
+        for a in range(K_PASSES):
+            cast_w(a, 0, 0)
+            for u in range(HALVES):
+                gather_words(a, u)
+            quantize_w(a, 0)
+            for u in range(HALVES):
+                hidden_pass(a, 0, u)
+        relu_out(0, 0)
+        cast_w(0, 1, P)
+        relu_out(0, 1)
+        quantize_w(0, 1)
+        interleave_h(0, 0)
+        cast_w(1, 1, 64)
+        quantize_h(0, 0)
+        quantize_w(1, 1)
+        cast_w(2, 1, 64)
+        interleave_h(0, 1)
+        quantize_w(2, 1)
+        quantize_h(0, 1)
+        for u in range(HALVES):
+            for a in range(K_PASSES):
+                hidden_pass(a, 1, u)
+        cast_qb(0)
+        relu_out(1, 0)
+        cast_qb(1)
+        relu_out(1, 1)
+        interleave_h(1, 0)
+        quantize_qb(0, 512)
+        quantize_h(1, 0)
+        quantize_qb(512, 768)
+        interleave_h(1, 1)
+        gather_rewards(0, 0)
+        quantize_h(1, 1)
+        for u in range(HALVES):
+            for i in range(N_TILES):
+                least = critics(i, u)
+                if (i, u) != (0, 0):
+                    gather_rewards(i, u)
+                finish(i, u, least)

@@ -46,10 +46,6 @@ def tile_list_twin_critic_targets_kernel(
         nc.vector.memset(tab_sc[:], 0)
         nc.vector.memset(warm[:], 0.0)
         nc.vector.memset(qa_sc[:], 0)
-        for q in range(4):
-            nc.scalar.dma_start(
-                tab_sc[32 * q : 32 * q + 4 * K_PASSES, :], tab_scales[:, 4 * q : 4 * q + 4, :].bitcast(I32)
-            )
         bias = keep.tile([P, H_PASSES, PACK], F32, name="bias")
         nc.scalar.dma_start(bias[:], b1.rearrange("(b p t) -> p b t", p=P, t=PACK))
         nc.scalar.activation(warm2[:], warm[:], RELU)
@@ -65,64 +61,74 @@ def tile_list_twin_critic_targets_kernel(
             tab[a] = keep.tile([P, T], I32, name="tab_%d" % a, align_bytes=64)
             nc.sync.dma_start(tab[a][:], tab_words[a].rearrange("p t i -> p (t i)").bitcast(I32))
 
-        for a in range(K_PASSES):
-            load_w(a, 0)
-            load_tab(a)
-        for a in range(K_PASSES):
-            load_w(a, 1)
-        for b in range(H_PASSES):
+        def load_tab_scales():
+            for q in range(4):
+                nc.sync.dma_start(
+                    tab_sc[32 * q : 32 * q + 4 * K_PASSES, :], tab_scales[:, 4 * q : 4 * q + 4, :].bitcast(I32)
+                )
+
+        def load_qb(b):
             qb_raw[b] = keep.tile([P, PACK, N], F32, name="qb_raw_%d" % b)
             nc.sync.dma_start(
                 qb_raw[b][:], qb[b * K_PASS : (b + 1) * K_PASS, :].rearrange("(p j) n -> p j n", j=PACK)
             )
+
         discount = keep.tile([P, N_TILES], F32, name="discount")
-        with nc.allow_non_contiguous_dma(reason="one discount a partition"):
-            nc.sync.dma_start(discount[:], disc.rearrange("(i p) -> p i", p=P))
-        for q in range(4):
-            nc.sync.dma_start(
-                qa_sc[32 * q : 32 * q + 4, :, :],
-                qa_scales[:, 4 * q : 4 * q + 4, :].rearrange("b r n -> r b n").bitcast(I32),
-            )
         qa = keep.tile([P, H_PASSES, N // 2], I32, name="qa", align_bytes=64)
-        nc.sync.dma_start(qa[:], qa_words.rearrange("b p c -> p b c").bitcast(I32))
-        for i in range(N_TILES):
+
+        def load_qa():
+            nc.sync.dma_start(qa[:], qa_words.rearrange("b p c -> p b c").bitcast(I32))
+            for q in range(4):
+                nc.sync.dma_start(
+                    qa_sc[32 * q : 32 * q + 4, :, :],
+                    qa_scales[:, 4 * q : 4 * q + 4, :].rearrange("b r n -> r b n").bitcast(I32),
+                )
+            with nc.allow_non_contiguous_dma(reason="one discount a partition"):
+                nc.sync.dma_start(discount[:], disc.rearrange("(i p) -> p i", p=P))
+
+        def load_rewards(i):
             rewards[i] = keep.tile([P, T], F32, name="rewards_%d" % i, align_bytes=64)
             nc.sync.dma_start(rewards[i][:], gT[i * P : (i + 1) * P, :])
 
-        def picks(u):
-            return offsets[:, u * LIST_COLS : (u + 1) * LIST_COLS]
+        w_bf, w_codes, w_sc = {}, {}, {}
+        banks, planes, h_bf, h_codes, h_sc = {}, {}, {}, {}, {}
+        v_sc = keep.tile([P, S], U8, name="v_sc", align_bytes=64)
+        v_codes = [keep.tile([P, S], U32, name="v_codes_%d" % a, align_bytes=64) for a in range(K_PASSES)]
+        picked = [keep.tile([P, S], F32, name="picked_%d" % i) for i in range(N_TILES)]
 
-        v_sc, v_codes, w_bf, w_codes, w_sc = {}, {}, {}, {}, {}
-        banks, planes, h_bf, h_codes, h_sc, picked = {}, {}, {}, {}, {}, {}
+        def gather(dst, window, lo, hi):
+            picks = offsets[:, lo * LIST_COLS : hi * LIST_COLS]
+            nc.vector.tensor_copy(dst[:, lo * COLS : hi * COLS], window.indirect(picks))
 
-        def gather_scales(u):
-            v_sc[u] = keep.tile([P, COLS], U8, name="v_sc_%d" % u, align_bytes=64)
-            nc.vector.tensor_copy(v_sc[u][:], tab_sc[:].bitcast(U8).indirect(picks(u)))
+        def gather_scales(lo, hi):
+            gather(v_sc, tab_sc[:].bitcast(U8), lo, hi)
 
-        def gather_words(a, u):
-            v_codes[a, u] = keep.tile([P, COLS], U32, name="v_codes_%d_%d" % (a, u), align_bytes=64)
-            nc.vector.tensor_copy(v_codes[a, u][:], tab[a][:].bitcast(U32).indirect(picks(u)))
+        def gather_words(a, lo, hi):
+            gather(v_codes[a], tab[a][:].bitcast(U32), lo, hi)
 
-        def gather_rewards(i, u):
-            picked[i, u] = keep.tile([P, COLS], F32, name="picked_%d_%d" % (i, u))
-            nc.vector.tensor_copy(picked[i, u][:], rewards[i][:].indirect(picks(u)))
+        def gather_rewards(i, lo, hi):
+            gather(picked[i], rewards[i][:], lo, hi)
 
-        def cast_w(a, b, vector_m):
-            w_bf[a, b] = ring.tile([P, PACK * K_PASS], BF16, name="w_bf", align_bytes=64)
+        def copy_on(engine, dst, src):
+            if engine == "vector":
+                nc.vector.tensor_copy(dst, src)
+            else:
+                nc.scalar.copy(dst, src)
+
+        def cast_w(a, b, engine, lo, hi):
+            if (a, b) not in w_bf:
+                w_bf[a, b] = ring.tile([P, PACK * K_PASS], BF16, name="w_bf", align_bytes=64)
             dst = w_bf[a, b][:].rearrange("p (t m j) -> p m j t", t=PACK, j=PACK)
             src = w_raw[a, b][:].rearrange("p j (m t) -> p m j t", t=PACK)
-            if vector_m > 0:
-                nc.vector.tensor_copy(dst[:, 0:vector_m], src[:, 0:vector_m])
-            if vector_m < P:
-                nc.scalar.copy(dst[:, vector_m:P], src[:, vector_m:P])
+            copy_on(engine, dst[:, lo:hi], src[:, lo:hi])
 
         def quantize_w(a, b):
             w_codes[a, b] = keep.tile([P, K_PASS], U32, name="w_codes_%d_%d" % (a, b), align_bytes=64)
             w_sc[a, b] = keep.tile([P, K_PASS], U8, name="w_sc_%d_%d" % (a, b), align_bytes=64)
             nc.vector.quantize_mx(out=w_codes[a, b][:].bitcast(FP8X4), scales=w_sc[a, b][:], in_=w_bf[a, b][:])
 
-        def hidden_pass(a, b, u):
-            for t in range(PACK):
+        def hidden_pass(a, b, u, tiles=range(PACK)):
+            for t in tiles:
                 if a == 0:
                     banks[b, u, t] = psum.tile([P, COLS], F32, name="bank")
                 cols = slice(t * P, (t + 1) * P)
@@ -130,23 +136,24 @@ def tile_list_twin_critic_targets_kernel(
                     out=banks[b, u, t][:],
                     lhsT=w_codes[a, b][:, cols].bitcast(FP8X4),
                     lhsT_scale=w_sc[a, b][:, cols],
-                    rhs=v_codes[a, u][:].bitcast(FP8X4),
-                    rhs_scale=v_sc[u][4 * a : P, :],
+                    rhs=v_codes[a][:, u * COLS : (u + 1) * COLS].bitcast(FP8X4),
+                    rhs_scale=v_sc[4 * a : P, u * COLS : (u + 1) * COLS],
                     start=(a == 0),
                     stop=(a == K_PASSES - 1),
                 )
 
-        def relu_out(b, u):
-            planes[b, u] = ring.tile([P, PACK, COLS], BF16, name="planes")
-            for t in range(PACK):
+        def relu_out(b, u, tiles=range(PACK)):
+            if (b, u) not in planes:
+                planes[b, u] = ring.tile([P, PACK, COLS], BF16, name="planes")
+            for t in tiles:
                 nc.scalar.activation(planes[b, u][:, t, :], banks[b, u, t][:], RELU, bias=bias[:, b, t : t + 1])
 
-        def interleave_h(b, u):
-            h_bf[b, u] = ring.tile([P, COLS * PACK], BF16, name="h_bf", align_bytes=64, bufs=2)
-            nc.vector.tensor_copy(
-                h_bf[b, u][:].rearrange("p (c i t) -> p c t i", i=4, t=PACK),
-                planes[b, u][:].rearrange("p t (c i) -> p c t i", i=4),
-            )
+        def interleave_h(b, u, engine, lo, hi):
+            if (b, u) not in h_bf:
+                h_bf[b, u] = ring.tile([P, COLS * PACK], BF16, name="h_bf", align_bytes=64, bufs=2)
+            dst = h_bf[b, u][:].rearrange("p (c i t) -> p c t i", i=4, t=PACK)
+            src = planes[b, u][:].rearrange("p t (c i) -> p c t i", i=4)
+            copy_on(engine, dst[:, lo:hi], src[:, lo:hi])
 
         def quantize_h(b, u):
             h_codes[b, u] = keep.tile([P, COLS], U32, name="h_codes_%d_%d" % (b, u), align_bytes=64)
@@ -157,24 +164,24 @@ def tile_list_twin_critic_targets_kernel(
         qb_codes = keep.tile([P, H_PASSES * N], U32, name="qb_codes", align_bytes=64)
         qb_sc = keep.tile([P, H_PASSES * N], U8, name="qb_sc", align_bytes=64)
 
-        def cast_qb(b):
-            dst = qb_bf[:, b * N * PACK : (b + 1) * N * PACK]
-            nc.scalar.copy(
-                dst.rearrange("p (c i t) -> p c t i", i=4, t=PACK),
-                qb_raw[b][:].rearrange("p t (c i) -> p c t i", i=4),
-            )
+        def cast_qb(b, engine, lo, hi):
+            dst = qb_bf[:, b * N * PACK : (b + 1) * N * PACK].rearrange("p (c i t) -> p c t i", i=4, t=PACK)
+            src = qb_raw[b][:].rearrange("p t (c i) -> p c t i", i=4)
+            copy_on(engine, dst[:, lo:hi], src[:, lo:hi])
 
-        def quantize_qb(lo, hi):
-            nc.vector.quantize_mx(
-                out=qb_codes[:, lo:hi].bitcast(FP8X4), scales=qb_sc[:, lo:hi], in_=qb_bf[:, lo * PACK : hi * PACK]
-            )
+        def quantize_qb(b):
+            for lo, hi in ((b * N, b * N + 256), (b * N + 256, (b + 1) * N)):
+                nc.vector.quantize_mx(
+                    out=qb_codes[:, lo:hi].bitcast(FP8X4), scales=qb_sc[:, lo:hi], in_=qb_bf[:, lo * PACK : hi * PACK]
+                )
 
-        def critics(i, u):
-            ya = psum.tile([P, COLS], F32, name="bank")
-            yb = psum.tile([P, COLS], F32, name="bank")
+        ya, yb, ya_sb, least = {}, {}, {}, {}
+
+        def critic_a(i, u):
+            ya[i, u] = psum.tile([P, COLS], F32, name="bank")
             for b in range(H_PASSES):
                 nc.tensor.matmul_mx(
-                    out=ya[:],
+                    out=ya[i, u][:],
                     lhsT=qa[:, b, :].bitcast(U8)[:, 2 * i * P : 2 * (i + 1) * P].bitcast(FP4X4),
                     lhsT_scale=qa_sc[:, b, :].bitcast(U8)[:, i * P : (i + 1) * P],
                     rhs=h_codes[b, u][:].bitcast(FP8X4),
@@ -182,10 +189,13 @@ def tile_list_twin_critic_targets_kernel(
                     start=(b == 0),
                     stop=(b == H_PASSES - 1),
                 )
+
+        def critic_b(i, u):
+            yb[i, u] = psum.tile([P, COLS], F32, name="bank")
             for b in range(H_PASSES):
                 cols = slice(b * N + i * P, b * N + (i + 1) * P)
                 nc.tensor.matmul_mx(
-                    out=yb[:],
+                    out=yb[i, u][:],
                     lhsT=qb_codes[:, cols].bitcast(FP8X4),
                     lhsT_scale=qb_sc[:, cols],
                     rhs=h_codes[b, u][:].bitcast(FP8X4),
@@ -193,57 +203,170 @@ def tile_list_twin_critic_targets_kernel(
                     start=(b == 0),
                     stop=(b == H_PASSES - 1),
                 )
-            ya_sb = ring.tile([P, COLS], F32, name="ya_sb")
-            nc.scalar.copy(ya_sb[:], ya[:])
-            least = ring.tile([P, COLS], F32, name="least")
-            nc.vector.tensor_tensor(least[:], yb[:], ya_sb[:], ALU.min)
-            return least
 
-        def finish(i, u, least):
+        def copy_a(i, u):
+            ya_sb[i, u] = ring.tile([P, COLS], F32, name="ya_sb")
+            nc.scalar.copy(ya_sb[i, u][:], ya[i, u][:])
+
+        def smaller(i, u):
+            least[i, u] = ring.tile([P, COLS], F32, name="least")
+            nc.vector.tensor_tensor(least[i, u][:], yb[i, u][:], ya_sb[i, u][:], ALU.min)
+
+        def finish(i, u):
             target = ring.tile([P, COLS], F32, name="target", bufs=4)
             nc.vector.scalar_tensor_tensor(
-                target[:], least[:], discount[:, i : i + 1], picked[i, u][:], ALU.mult, ALU.add
+                target[:], least[i, u][:], discount[:, i : i + 1], picked[i][:, u * COLS : (u + 1) * COLS], ALU.mult, ALU.add
             )
             nc.sync.dma_start(out[i * P : (i + 1) * P, u * COLS : (u + 1) * COLS], target[:])
 
-        for u in range(HALVES):
-            gather_scales(u)
-        for a in range(K_PASSES):
-            cast_w(a, 0, 0)
-            for u in range(HALVES):
-                gather_words(a, u)
-            quantize_w(a, 0)
-            for u in range(HALVES):
-                hidden_pass(a, 0, u)
-        relu_out(0, 0)
-        cast_w(0, 1, P)
-        relu_out(0, 1)
+        load_tab(0)
+        load_w(0, 0)
+        load_tab_scales()
+        load_tab(1)
+        load_w(1, 0)
+        load_w(2, 0)
+        load_tab(2)
+        load_w(0, 1)
+        load_w(1, 1)
+        load_w(2, 1)
+        load_qb(0)
+        load_rewards(0)
+        load_qb(1)
+        load_qa()
+        load_rewards(1)
+        load_rewards(2)
+        gather_words(0, 1, 2)
+        gather_words(0, 0, 1)
+        cast_w(0, 0, "scalar", 64, 128)
+        gather_scales(1, 2)
+        cast_w(0, 0, "vector", 0, 64)
+        gather_scales(0, 1)
+        quantize_w(0, 0)
+        gather_words(1, 0, 1)
+        hidden_pass(0, 0, 0, [0])
+        hidden_pass(0, 0, 0, [1])
+        cast_w(1, 0, "scalar", 0, 128)
+        hidden_pass(0, 0, 0, [2])
+        hidden_pass(0, 0, 0, [3])
+        gather_words(1, 1, 2)
+        hidden_pass(0, 0, 1, [0])
+        hidden_pass(0, 0, 1, [1])
+        hidden_pass(0, 0, 1, [2])
+        hidden_pass(0, 0, 1, [3])
+        cast_w(2, 0, "vector", 0, 80)
+        cast_w(2, 0, "scalar", 80, 128)
+        quantize_w(1, 0)
+        quantize_w(2, 0)
+        hidden_pass(1, 0, 1, [0])
+        hidden_pass(1, 0, 1, [1])
+        hidden_pass(1, 0, 1, [2])
+        gather_words(2, 0, 1)
+        hidden_pass(1, 0, 1, [3])
+        hidden_pass(1, 0, 0, [0])
+        hidden_pass(1, 0, 0, [1])
+        hidden_pass(1, 0, 0, [2])
+        gather_words(2, 1, 2)
+        hidden_pass(2, 0, 0, [0])
+        hidden_pass(2, 0, 0, [1])
+        relu_out(0, 0, [0])
+        hidden_pass(2, 0, 0, [2])
+        hidden_pass(1, 0, 0, [3])
+        cast_w(0, 1, "vector", 0, 128)
+        relu_out(0, 0, [1])
+        hidden_pass(2, 0, 0, [3])
+        hidden_pass(2, 0, 1, [0])
+        relu_out(0, 0, [2])
+        hidden_pass(2, 0, 1, [1])
+        hidden_pass(2, 0, 1, [2])
+        hidden_pass(2, 0, 1, [3])
+        relu_out(0, 0, [3])
         quantize_w(0, 1)
-        interleave_h(0, 0)
-        cast_w(1, 1, 64)
-        quantize_h(0, 0)
+        relu_out(0, 1, [0])
+        interleave_h(0, 0, "vector", 0, 128)
+        hidden_pass(0, 1, 0, [0])
+        relu_out(0, 1, [1])
+        hidden_pass(0, 1, 0, [1])
+        hidden_pass(0, 1, 0, [2])
+        hidden_pass(0, 1, 0, [3])
+        relu_out(0, 1, [2])
+        cast_w(1, 1, "vector", 0, 128)
+        hidden_pass(0, 1, 1, [0])
+        hidden_pass(0, 1, 1, [1])
+        relu_out(0, 1, [3])
+        hidden_pass(0, 1, 1, [2])
+        cast_w(2, 1, "scalar", 96, 128)
+        cast_w(2, 1, "vector", 0, 96)
+        hidden_pass(0, 1, 1, [3])
+        interleave_h(0, 1, "scalar", 80, 128)
         quantize_w(1, 1)
-        cast_w(2, 1, 64)
-        interleave_h(0, 1)
+        cast_qb(0, "scalar", 0, 96)
         quantize_w(2, 1)
+        hidden_pass(1, 1, 0, [0])
+        hidden_pass(1, 1, 0, [1])
+        interleave_h(0, 1, "vector", 0, 80)
+        hidden_pass(1, 1, 0, [2])
+        hidden_pass(2, 1, 0, [0])
+        hidden_pass(2, 1, 0, [1])
+        quantize_h(0, 0)
+        hidden_pass(2, 1, 0, [2])
+        relu_out(1, 0, [0])
+        hidden_pass(1, 1, 0, [3])
+        gather_rewards(0, 1, 2)
+        hidden_pass(2, 1, 0, [3])
+        relu_out(1, 0, [1])
+        hidden_pass(1, 1, 1, [0])
+        hidden_pass(2, 1, 1, [0])
+        relu_out(1, 0, [2])
+        hidden_pass(1, 1, 1, [1])
+        hidden_pass(2, 1, 1, [1])
+        quantize_qb(0)
+        cast_qb(1, "scalar", 0, 96)
+        hidden_pass(1, 1, 1, [2])
+        hidden_pass(2, 1, 1, [2])
         quantize_h(0, 1)
-        for u in range(HALVES):
-            for a in range(K_PASSES):
-                hidden_pass(a, 1, u)
-        cast_qb(0)
-        relu_out(1, 0)
-        cast_qb(1)
-        relu_out(1, 1)
-        interleave_h(1, 0)
-        quantize_qb(0, 512)
+        hidden_pass(1, 1, 1, [3])
+        hidden_pass(2, 1, 1, [3])
+        gather_rewards(0, 0, 1)
+        relu_out(1, 0, [3])
+        relu_out(1, 1, [0])
+        quantize_qb(1)
+        interleave_h(1, 0, "scalar", 48, 128)
+        interleave_h(1, 0, "vector", 0, 48)
+        gather_rewards(1, 0, 2)
+        relu_out(1, 1, [1])
+        relu_out(1, 1, [2])
+        relu_out(1, 1, [3])
         quantize_h(1, 0)
-        quantize_qb(512, 768)
-        interleave_h(1, 1)
-        gather_rewards(0, 0)
+        gather_rewards(2, 0, 2)
+        interleave_h(1, 1, "scalar", 0, 128)
+        critic_a(1, 0)
+        critic_b(2, 0)
+        critic_b(1, 0)
+        critic_a(2, 0)
+        copy_a(1, 0)
         quantize_h(1, 1)
-        for u in range(HALVES):
-            for i in range(N_TILES):
-                least = critics(i, u)
-                if (i, u) != (0, 0):
-                    gather_rewards(i, u)
-                finish(i, u, least)
+        critic_a(0, 0)
+        copy_a(2, 0)
+        critic_b(0, 0)
+        smaller(1, 0)
+        copy_a(0, 0)
+        critic_a(0, 1)
+        smaller(2, 0)
+        critic_b(0, 1)
+        copy_a(0, 1)
+        smaller(0, 0)
+        critic_a(1, 1)
+        finish(2, 0)
+        critic_b(1, 1)
+        copy_a(1, 1)
+        finish(0, 0)
+        critic_b(2, 1)
+        smaller(0, 1)
+        critic_a(2, 1)
+        finish(1, 0)
+        copy_a(2, 1)
+        finish(0, 1)
+        smaller(2, 1)
+        smaller(1, 1)
+        finish(2, 1)
+        finish(1, 1)

@@ -53,7 +53,7 @@ def tile_list_twin_critic_targets_kernel(
         w_raw, tab, qb_raw, rewards = {}, {}, {}, {}
 
         def load_w(a, b):
-            w_raw[a, b] = keep.tile([P, PACK, K_PASS], F32, name="w_raw_%d_%d" % (a, b))
+            w_raw[a, b] = ring.tile([P, PACK, K_PASS], F32, name="w_raw", bufs=4)
             rows = w1[a * K_PASS : (a + 1) * K_PASS, b * K_PASS : (b + 1) * K_PASS]
             nc.sync.dma_start(w_raw[a, b][:], rows.rearrange("(p j) c -> p j c", j=PACK))
 
@@ -63,7 +63,7 @@ def tile_list_twin_critic_targets_kernel(
 
         def load_tab_scales():
             for q in range(4):
-                nc.sync.dma_start(
+                nc.gpsimd.dma_start(
                     tab_sc[32 * q : 32 * q + 4 * K_PASSES, :], tab_scales[:, 4 * q : 4 * q + 4, :].bitcast(I32)
                 )
 
@@ -144,13 +144,13 @@ def tile_list_twin_critic_targets_kernel(
 
         def relu_out(b, u, tiles=range(PACK)):
             if (b, u) not in planes:
-                planes[b, u] = ring.tile([P, PACK, COLS], BF16, name="planes")
+                planes[b, u] = ring.tile([P, PACK, COLS], BF16, name="planes", bufs=4)
             for t in tiles:
                 nc.scalar.activation(planes[b, u][:, t, :], banks[b, u, t][:], RELU, bias=bias[:, b, t : t + 1])
 
         def interleave_h(b, u, engine, lo, hi):
             if (b, u) not in h_bf:
-                h_bf[b, u] = ring.tile([P, COLS * PACK], BF16, name="h_bf", align_bytes=64, bufs=2)
+                h_bf[b, u] = ring.tile([P, COLS * PACK], BF16, name="h_bf", align_bytes=64)
             dst = h_bf[b, u][:].rearrange("p (c i t) -> p c t i", i=4, t=PACK)
             src = planes[b, u][:].rearrange("p t (c i) -> p c t i", i=4)
             copy_on(engine, dst[:, lo:hi], src[:, lo:hi])
@@ -169,8 +169,8 @@ def tile_list_twin_critic_targets_kernel(
             src = qb_raw[b][:].rearrange("p t (c i) -> p c t i", i=4)
             copy_on(engine, dst[:, lo:hi], src[:, lo:hi])
 
-        def quantize_qb(b):
-            for lo, hi in ((b * N, b * N + 256), (b * N + 256, (b + 1) * N)):
+        def quantize_qb(ranges):
+            for lo, hi in ranges:
                 nc.vector.quantize_mx(
                     out=qb_codes[:, lo:hi].bitcast(FP8X4), scales=qb_sc[:, lo:hi], in_=qb_bf[:, lo * PACK : hi * PACK]
                 )
@@ -209,7 +209,7 @@ def tile_list_twin_critic_targets_kernel(
             nc.scalar.copy(ya_sb[i, u][:], ya[i, u][:])
 
         def smaller(i, u):
-            least[i, u] = ring.tile([P, COLS], F32, name="least")
+            least[i, u] = ring.tile([P, COLS], F32, name="least", bufs=4)
             nc.vector.tensor_tensor(least[i, u][:], yb[i, u][:], ya_sb[i, u][:], ALU.min)
 
         def finish(i, u):
@@ -219,154 +219,150 @@ def tile_list_twin_critic_targets_kernel(
             )
             nc.sync.dma_start(out[i * P : (i + 1) * P, u * COLS : (u + 1) * COLS], target[:])
 
-        load_tab(0)
-        load_w(0, 0)
         load_tab_scales()
-        load_tab(1)
+        load_w(0, 0)
+        load_tab(0)
         load_w(1, 0)
         load_w(2, 0)
+        load_tab(1)
         load_tab(2)
         load_w(0, 1)
         load_w(1, 1)
         load_w(2, 1)
         load_qb(0)
         load_rewards(0)
-        load_qb(1)
         load_qa()
         load_rewards(1)
         load_rewards(2)
-        gather_words(0, 1, 2)
+        load_qb(1)
+        gather_scales(0, 2)
+        cast_w(0, 0, "scalar", 0, 128)
         gather_words(0, 0, 1)
-        cast_w(0, 0, "scalar", 64, 128)
-        gather_scales(1, 2)
-        cast_w(0, 0, "vector", 0, 64)
-        gather_scales(0, 1)
+        gather_words(0, 1, 2)
+        cast_w(1, 0, "vector", 0, 128)
         quantize_w(0, 0)
-        gather_words(1, 0, 1)
+        cast_w(2, 0, "scalar", 0, 128)
+        quantize_w(1, 0)
         hidden_pass(0, 0, 0, [0])
         hidden_pass(0, 0, 0, [1])
-        cast_w(1, 0, "scalar", 0, 128)
         hidden_pass(0, 0, 0, [2])
+        gather_words(1, 0, 2)
         hidden_pass(0, 0, 0, [3])
-        gather_words(1, 1, 2)
         hidden_pass(0, 0, 1, [0])
         hidden_pass(0, 0, 1, [1])
         hidden_pass(0, 0, 1, [2])
         hidden_pass(0, 0, 1, [3])
-        cast_w(2, 0, "vector", 0, 80)
-        cast_w(2, 0, "scalar", 80, 128)
-        quantize_w(1, 0)
         quantize_w(2, 0)
         hidden_pass(1, 0, 1, [0])
+        gather_words(2, 0, 1)
         hidden_pass(1, 0, 1, [1])
         hidden_pass(1, 0, 1, [2])
-        gather_words(2, 0, 1)
         hidden_pass(1, 0, 1, [3])
         hidden_pass(1, 0, 0, [0])
         hidden_pass(1, 0, 0, [1])
-        hidden_pass(1, 0, 0, [2])
         gather_words(2, 1, 2)
+        cast_w(0, 1, "scalar", 96, 128)
+        hidden_pass(1, 0, 0, [2])
+        hidden_pass(1, 0, 0, [3])
         hidden_pass(2, 0, 0, [0])
         hidden_pass(2, 0, 0, [1])
-        relu_out(0, 0, [0])
+        cast_w(0, 1, "vector", 0, 96)
         hidden_pass(2, 0, 0, [2])
-        hidden_pass(1, 0, 0, [3])
-        cast_w(0, 1, "vector", 0, 128)
-        relu_out(0, 0, [1])
-        hidden_pass(2, 0, 0, [3])
+        relu_out(0, 0, [0])
         hidden_pass(2, 0, 1, [0])
-        relu_out(0, 0, [2])
         hidden_pass(2, 0, 1, [1])
+        relu_out(0, 0, [1])
         hidden_pass(2, 0, 1, [2])
+        cast_w(1, 1, "vector", 0, 128)
         hidden_pass(2, 0, 1, [3])
-        relu_out(0, 0, [3])
-        quantize_w(0, 1)
+        relu_out(0, 0, [2])
+        hidden_pass(2, 0, 0, [3])
         relu_out(0, 1, [0])
-        interleave_h(0, 0, "vector", 0, 128)
-        hidden_pass(0, 1, 0, [0])
+        quantize_w(0, 1)
+        relu_out(0, 0, [3])
+        quantize_w(1, 1)
         relu_out(0, 1, [1])
+        hidden_pass(0, 1, 0, [0])
+        cast_w(2, 1, "vector", 0, 128)
         hidden_pass(0, 1, 0, [1])
+        relu_out(0, 1, [2])
         hidden_pass(0, 1, 0, [2])
         hidden_pass(0, 1, 0, [3])
-        relu_out(0, 1, [2])
-        cast_w(1, 1, "vector", 0, 128)
-        hidden_pass(0, 1, 1, [0])
-        hidden_pass(0, 1, 1, [1])
-        relu_out(0, 1, [3])
-        hidden_pass(0, 1, 1, [2])
-        cast_w(2, 1, "scalar", 96, 128)
-        cast_w(2, 1, "vector", 0, 96)
-        hidden_pass(0, 1, 1, [3])
-        interleave_h(0, 1, "scalar", 80, 128)
-        quantize_w(1, 1)
-        cast_qb(0, "scalar", 0, 96)
-        quantize_w(2, 1)
         hidden_pass(1, 1, 0, [0])
+        relu_out(0, 1, [3])
         hidden_pass(1, 1, 0, [1])
-        interleave_h(0, 1, "vector", 0, 80)
+        cast_qb(0, "vector", 0, 24)
         hidden_pass(1, 1, 0, [2])
-        hidden_pass(2, 1, 0, [0])
-        hidden_pass(2, 1, 0, [1])
+        cast_qb(0, "scalar", 24, 96)
+        interleave_h(0, 0, "vector", 0, 128)
+        hidden_pass(1, 1, 0, [3])
+        hidden_pass(0, 1, 1, [0])
+        hidden_pass(1, 1, 1, [0])
+        hidden_pass(0, 1, 1, [1])
+        interleave_h(0, 1, "scalar", 0, 128)
+        hidden_pass(1, 1, 1, [1])
+        quantize_w(2, 1)
+        hidden_pass(0, 1, 1, [2])
+        hidden_pass(1, 1, 1, [2])
+        hidden_pass(0, 1, 1, [3])
         quantize_h(0, 0)
+        hidden_pass(1, 1, 1, [3])
+        hidden_pass(2, 1, 0, [0])
+        gather_rewards(0, 0, 2)
+        hidden_pass(2, 1, 0, [1])
         hidden_pass(2, 1, 0, [2])
         relu_out(1, 0, [0])
-        hidden_pass(1, 1, 0, [3])
-        gather_rewards(0, 1, 2)
         hidden_pass(2, 1, 0, [3])
-        relu_out(1, 0, [1])
-        hidden_pass(1, 1, 1, [0])
         hidden_pass(2, 1, 1, [0])
-        relu_out(1, 0, [2])
-        hidden_pass(1, 1, 1, [1])
+        relu_out(1, 0, [1])
         hidden_pass(2, 1, 1, [1])
-        quantize_qb(0)
-        cast_qb(1, "scalar", 0, 96)
-        hidden_pass(1, 1, 1, [2])
         hidden_pass(2, 1, 1, [2])
-        quantize_h(0, 1)
-        hidden_pass(1, 1, 1, [3])
         hidden_pass(2, 1, 1, [3])
-        gather_rewards(0, 0, 1)
+        relu_out(1, 0, [2])
+        quantize_h(0, 1)
         relu_out(1, 0, [3])
+        gather_rewards(1, 0, 1)
         relu_out(1, 1, [0])
-        quantize_qb(1)
-        interleave_h(1, 0, "scalar", 48, 128)
-        interleave_h(1, 0, "vector", 0, 48)
-        gather_rewards(1, 0, 2)
         relu_out(1, 1, [1])
+        interleave_h(1, 0, "vector", 0, 128)
         relu_out(1, 1, [2])
         relu_out(1, 1, [3])
+        gather_rewards(2, 0, 1)
+        cast_qb(1, "scalar", 0, 96)
         quantize_h(1, 0)
-        gather_rewards(2, 0, 2)
         interleave_h(1, 1, "scalar", 0, 128)
+        gather_rewards(1, 1, 2)
         critic_a(1, 0)
-        critic_b(2, 0)
-        critic_b(1, 0)
+        quantize_qb([(0, 512)])
         critic_a(2, 0)
+        quantize_qb([(512, 768)])
         copy_a(1, 0)
-        quantize_h(1, 1)
-        critic_a(0, 0)
+        gather_rewards(2, 1, 2)
+        critic_b(1, 0)
         copy_a(2, 0)
+        critic_b(2, 0)
+        quantize_h(1, 1)
         critic_b(0, 0)
         smaller(1, 0)
-        copy_a(0, 0)
-        critic_a(0, 1)
+        critic_a(0, 0)
         smaller(2, 0)
+        critic_a(0, 1)
+        copy_a(0, 0)
         critic_b(0, 1)
-        copy_a(0, 1)
-        smaller(0, 0)
-        critic_a(1, 1)
-        finish(2, 0)
-        critic_b(1, 1)
-        copy_a(1, 1)
-        finish(0, 0)
-        critic_b(2, 1)
-        smaller(0, 1)
-        critic_a(2, 1)
         finish(1, 0)
+        copy_a(0, 1)
+        critic_b(2, 1)
+        finish(2, 0)
+        critic_a(1, 1)
+        smaller(0, 0)
+        critic_a(2, 1)
+        copy_a(1, 1)
+        smaller(0, 1)
+        critic_b(1, 1)
         copy_a(2, 1)
+        finish(0, 0)
         finish(0, 1)
-        smaller(2, 1)
         smaller(1, 1)
-        finish(2, 1)
+        smaller(2, 1)
         finish(1, 1)
+        finish(2, 1)

@@ -18,13 +18,20 @@ ALU = mybir.AluOpType
 
 P = 128
 PACK = 4
-K_PASS = P * PACK
-K_PASSES = K // K_PASS
-H_PASSES = H // K_PASS
+PASS = P * PACK
+K_PASSES = K // PASS
+H_PASSES = H // PASS
 COLS = 512
 HALVES = S // COLS
 N_TILES = N // P
+QUADRANTS = 4
+SCALE_ROWS = 4
 LIST_COLS = COLS // 16
+RUN = 4
+PSUM_BANKS = 8
+
+W_VECTOR_PART = {(0, 0): 0, (1, 0): 64, (2, 0): 64, (0, 1): 96, (1, 1): 128, (2, 1): 64}
+H_VECTOR_PART = {(0, 0): 96, (0, 1): 48, (1, 0): 96}
 
 
 def tile_list_twin_critic_targets_kernel(
@@ -34,27 +41,25 @@ def tile_list_twin_critic_targets_kernel(
     with ExitStack() as ctx:
         keep = ctx.enter_context(tc.tile_pool(name="keep", bufs=1))
         ring = ctx.enter_context(tc.tile_pool(name="ring", bufs=3))
-        psum = ctx.enter_context(tc.psum_pool(name="psum", bufs=8))
+        psum = ctx.enter_context(tc.psum_pool(name="psum", bufs=PSUM_BANKS))
 
         offsets = keep.tile([P, S // 16], U16, name="offsets")
         nc.sync.dma_start(offsets[:], offs)
 
         tab_sc = keep.tile([P, T // 4], I32, name="tab_sc", align_bytes=64)
         qa_sc = keep.tile([P, H_PASSES, N // 4], I32, name="qa_sc", align_bytes=64)
-        warm = keep.tile([P, 8], F32, name="warm")
-        warm2 = keep.tile([P, 8], F32, name="warm2")
         nc.vector.memset(tab_sc[:], 0)
-        nc.vector.memset(warm[:], 0.0)
         nc.vector.memset(qa_sc[:], 0)
         bias = keep.tile([P, H_PASSES, PACK], F32, name="bias")
         nc.scalar.dma_start(bias[:], b1.rearrange("(b p t) -> p b t", p=P, t=PACK))
-        nc.scalar.activation(warm2[:], warm[:], RELU)
+        discount = keep.tile([P, N_TILES], F32, name="discount")
+        qa = keep.tile([P, H_PASSES, N // 2], I32, name="qa", align_bytes=64)
 
         w_raw, tab, qb_raw, rewards = {}, {}, {}, {}
 
         def load_w(a, b):
-            w_raw[a, b] = ring.tile([P, PACK, K_PASS], F32, name="w_raw", bufs=4)
-            rows = w1[a * K_PASS : (a + 1) * K_PASS, b * K_PASS : (b + 1) * K_PASS]
+            w_raw[a, b] = ring.tile([P, PACK, PASS], F32, name="w_raw", bufs=4)
+            rows = w1[a * PASS : (a + 1) * PASS, b * PASS : (b + 1) * PASS]
             nc.sync.dma_start(w_raw[a, b][:], rows.rearrange("(p j) c -> p j c", j=PACK))
 
         def load_tab(a):
@@ -62,26 +67,22 @@ def tile_list_twin_critic_targets_kernel(
             nc.sync.dma_start(tab[a][:], tab_words[a].rearrange("p t i -> p (t i)").bitcast(I32))
 
         def load_tab_scales():
-            for q in range(4):
-                nc.gpsimd.dma_start(
-                    tab_sc[32 * q : 32 * q + 4 * K_PASSES, :], tab_scales[:, 4 * q : 4 * q + 4, :].bitcast(I32)
+            for q in range(QUADRANTS):
+                nc.sync.dma_start(
+                    tab_sc[32 * q : 32 * q + SCALE_ROWS * K_PASSES, :],
+                    tab_scales[:, SCALE_ROWS * q : SCALE_ROWS * (q + 1), :].bitcast(I32),
                 )
 
         def load_qb(b):
             qb_raw[b] = keep.tile([P, PACK, N], F32, name="qb_raw_%d" % b)
-            nc.sync.dma_start(
-                qb_raw[b][:], qb[b * K_PASS : (b + 1) * K_PASS, :].rearrange("(p j) n -> p j n", j=PACK)
-            )
+            nc.sync.dma_start(qb_raw[b][:], qb[b * PASS : (b + 1) * PASS, :].rearrange("(p t) n -> p t n", t=PACK))
 
-        discount = keep.tile([P, N_TILES], F32, name="discount")
-        qa = keep.tile([P, H_PASSES, N // 2], I32, name="qa", align_bytes=64)
-
-        def load_qa():
+        def load_qa_and_discount():
             nc.sync.dma_start(qa[:], qa_words.rearrange("b p c -> p b c").bitcast(I32))
-            for q in range(4):
+            for q in range(QUADRANTS):
                 nc.sync.dma_start(
-                    qa_sc[32 * q : 32 * q + 4, :, :],
-                    qa_scales[:, 4 * q : 4 * q + 4, :].rearrange("b r n -> r b n").bitcast(I32),
+                    qa_sc[32 * q : 32 * q + SCALE_ROWS, :, :],
+                    qa_scales[:, SCALE_ROWS * q : SCALE_ROWS * (q + 1), :].rearrange("b r n -> r b n").bitcast(I32),
                 )
             with nc.allow_non_contiguous_dma(reason="one discount a partition"):
                 nc.sync.dma_start(discount[:], disc.rearrange("(i p) -> p i", p=P))
@@ -90,41 +91,42 @@ def tile_list_twin_critic_targets_kernel(
             rewards[i] = keep.tile([P, T], F32, name="rewards_%d" % i, align_bytes=64)
             nc.sync.dma_start(rewards[i][:], gT[i * P : (i + 1) * P, :])
 
-        w_bf, w_codes, w_sc = {}, {}, {}
-        banks, planes, h_bf, h_codes, h_sc = {}, {}, {}, {}, {}
         v_sc = keep.tile([P, S], U8, name="v_sc", align_bytes=64)
         v_codes = [keep.tile([P, S], U32, name="v_codes_%d" % a, align_bytes=64) for a in range(K_PASSES)]
         picked = [keep.tile([P, S], F32, name="picked_%d" % i) for i in range(N_TILES)]
 
-        def gather(dst, window, lo, hi):
-            picks = offsets[:, lo * LIST_COLS : hi * LIST_COLS]
-            nc.vector.tensor_copy(dst[:, lo * COLS : hi * COLS], window.indirect(picks))
+        def gather(dst, window, first, last):
+            picks = offsets[:, first * LIST_COLS : last * LIST_COLS]
+            nc.vector.tensor_copy(dst[:, first * COLS : last * COLS], window.indirect(picks))
 
-        def gather_scales(lo, hi):
-            gather(v_sc, tab_sc[:].bitcast(U8), lo, hi)
+        def gather_scales():
+            gather(v_sc, tab_sc[:].bitcast(U8), 0, HALVES)
 
-        def gather_words(a, lo, hi):
-            gather(v_codes[a], tab[a][:].bitcast(U32), lo, hi)
+        def gather_words(a, first=0, last=HALVES):
+            gather(v_codes[a], tab[a][:].bitcast(U32), first, last)
 
-        def gather_rewards(i, lo, hi):
-            gather(picked[i], rewards[i][:], lo, hi)
+        def gather_rewards(i, first=0, last=HALVES):
+            gather(picked[i], rewards[i][:], first, last)
 
-        def copy_on(engine, dst, src):
-            if engine == "vector":
-                nc.vector.tensor_copy(dst, src)
-            else:
-                nc.scalar.copy(dst, src)
+        def half(u):
+            return slice(u * COLS, (u + 1) * COLS)
 
-        def cast_w(a, b, engine, lo, hi):
-            if (a, b) not in w_bf:
-                w_bf[a, b] = ring.tile([P, PACK * K_PASS], BF16, name="w_bf", align_bytes=64)
+        w_bf, w_codes, w_sc = {}, {}, {}
+        banks, h_rows, h_bf, h_codes, h_sc = {}, {}, {}, {}, {}
+
+        def round_w(a, b):
+            w_bf[a, b] = ring.tile([P, PACK * PASS], BF16, name="w_bf", align_bytes=64)
             dst = w_bf[a, b][:].rearrange("p (t m j) -> p m j t", t=PACK, j=PACK)
             src = w_raw[a, b][:].rearrange("p j (m t) -> p m j t", t=PACK)
-            copy_on(engine, dst[:, lo:hi], src[:, lo:hi])
+            cut = W_VECTOR_PART[a, b]
+            if cut > 0:
+                nc.vector.tensor_copy(dst[:, 0:cut], src[:, 0:cut])
+            if cut < P:
+                nc.scalar.copy(dst[:, cut:P], src[:, cut:P])
 
         def quantize_w(a, b):
-            w_codes[a, b] = keep.tile([P, K_PASS], U32, name="w_codes_%d_%d" % (a, b), align_bytes=64)
-            w_sc[a, b] = keep.tile([P, K_PASS], U8, name="w_sc_%d_%d" % (a, b), align_bytes=64)
+            w_codes[a, b] = keep.tile([P, PASS], U32, name="w_codes_%d_%d" % (a, b), align_bytes=64)
+            w_sc[a, b] = keep.tile([P, PASS], U8, name="w_sc_%d_%d" % (a, b), align_bytes=64)
             nc.vector.quantize_mx(out=w_codes[a, b][:].bitcast(FP8X4), scales=w_sc[a, b][:], in_=w_bf[a, b][:])
 
         def hidden_pass(a, b, u, tiles=range(PACK)):
@@ -136,24 +138,37 @@ def tile_list_twin_critic_targets_kernel(
                     out=banks[b, u, t][:],
                     lhsT=w_codes[a, b][:, cols].bitcast(FP8X4),
                     lhsT_scale=w_sc[a, b][:, cols],
-                    rhs=v_codes[a][:, u * COLS : (u + 1) * COLS].bitcast(FP8X4),
-                    rhs_scale=v_sc[4 * a : P, u * COLS : (u + 1) * COLS],
+                    rhs=v_codes[a][:, half(u)].bitcast(FP8X4),
+                    rhs_scale=v_sc[SCALE_ROWS * a : P, half(u)],
                     start=(a == 0),
                     stop=(a == K_PASSES - 1),
                 )
 
         def relu_out(b, u, tiles=range(PACK)):
-            if (b, u) not in planes:
-                planes[b, u] = ring.tile([P, PACK, COLS], BF16, name="planes", bufs=4)
+            if (b, u) not in h_rows:
+                h_rows[b, u] = ring.tile([P, PACK, COLS], BF16, name="h_rows", bufs=H_PASSES * HALVES)
             for t in tiles:
-                nc.scalar.activation(planes[b, u][:, t, :], banks[b, u, t][:], RELU, bias=bias[:, b, t : t + 1])
+                nc.scalar.activation(h_rows[b, u][:, t, :], banks[b, u, t][:], RELU, bias=bias[:, b, t : t + 1])
 
-        def interleave_h(b, u, engine, lo, hi):
+        def interleave_views(grouped, rows):
+            dst = grouped.rearrange("p (c i t) -> p c t i", i=RUN, t=PACK)
+            src = rows.rearrange("p t (c i) -> p c t i", i=RUN)
+            return dst, src
+
+        def h_views(b, u):
             if (b, u) not in h_bf:
                 h_bf[b, u] = ring.tile([P, COLS * PACK], BF16, name="h_bf", align_bytes=64)
-            dst = h_bf[b, u][:].rearrange("p (c i t) -> p c t i", i=4, t=PACK)
-            src = planes[b, u][:].rearrange("p t (c i) -> p c t i", i=4)
-            copy_on(engine, dst[:, lo:hi], src[:, lo:hi])
+            return interleave_views(h_bf[b, u][:], h_rows[b, u][:])
+
+        def interleave_h_vector(b, u):
+            dst, src = h_views(b, u)
+            cut = H_VECTOR_PART[b, u]
+            nc.vector.tensor_copy(dst[:, 0:cut], src[:, 0:cut])
+
+        def interleave_h_scalar(b, u):
+            dst, src = h_views(b, u)
+            cut = H_VECTOR_PART.get((b, u), 0)
+            nc.scalar.copy(dst[:, cut:P], src[:, cut:P])
 
         def quantize_h(b, u):
             h_codes[b, u] = keep.tile([P, COLS], U32, name="h_codes_%d_%d" % (b, u), align_bytes=64)
@@ -164,45 +179,44 @@ def tile_list_twin_critic_targets_kernel(
         qb_codes = keep.tile([P, H_PASSES * N], U32, name="qb_codes", align_bytes=64)
         qb_sc = keep.tile([P, H_PASSES * N], U8, name="qb_sc", align_bytes=64)
 
-        def cast_qb(b, engine, lo, hi):
-            dst = qb_bf[:, b * N * PACK : (b + 1) * N * PACK].rearrange("p (c i t) -> p c t i", i=4, t=PACK)
-            src = qb_raw[b][:].rearrange("p t (c i) -> p c t i", i=4)
-            copy_on(engine, dst[:, lo:hi], src[:, lo:hi])
+        def qb_views(b):
+            return interleave_views(qb_bf[:, b * N * PACK : (b + 1) * N * PACK], qb_raw[b][:])
 
-        def quantize_qb(ranges):
-            for lo, hi in ranges:
-                nc.vector.quantize_mx(
-                    out=qb_codes[:, lo:hi].bitcast(FP8X4), scales=qb_sc[:, lo:hi], in_=qb_bf[:, lo * PACK : hi * PACK]
-                )
+        def quantize_qb(lo, hi):
+            nc.vector.quantize_mx(
+                out=qb_codes[:, lo:hi].bitcast(FP8X4), scales=qb_sc[:, lo:hi], in_=qb_bf[:, lo * PACK : hi * PACK]
+            )
 
         ya, yb, ya_sb, least = {}, {}, {}, {}
 
-        def critic_a(i, u):
-            ya[i, u] = psum.tile([P, COLS], F32, name="bank")
+        def critic(weights, u):
+            y = psum.tile([P, COLS], F32, name="bank")
             for b in range(H_PASSES):
+                codes, scales = weights(b)
                 nc.tensor.matmul_mx(
-                    out=ya[i, u][:],
-                    lhsT=qa[:, b, :].bitcast(U8)[:, 2 * i * P : 2 * (i + 1) * P].bitcast(FP4X4),
-                    lhsT_scale=qa_sc[:, b, :].bitcast(U8)[:, i * P : (i + 1) * P],
+                    out=y[:],
+                    lhsT=codes,
+                    lhsT_scale=scales,
                     rhs=h_codes[b, u][:].bitcast(FP8X4),
                     rhs_scale=h_sc[b, u][:],
                     start=(b == 0),
                     stop=(b == H_PASSES - 1),
                 )
+            return y
+
+        def critic_a(i, u):
+            def weights(b):
+                codes = qa[:, b, :].bitcast(U8)[:, 2 * i * P : 2 * (i + 1) * P].bitcast(FP4X4)
+                return codes, qa_sc[:, b, :].bitcast(U8)[:, i * P : (i + 1) * P]
+
+            ya[i, u] = critic(weights, u)
 
         def critic_b(i, u):
-            yb[i, u] = psum.tile([P, COLS], F32, name="bank")
-            for b in range(H_PASSES):
+            def weights(b):
                 cols = slice(b * N + i * P, b * N + (i + 1) * P)
-                nc.tensor.matmul_mx(
-                    out=yb[i, u][:],
-                    lhsT=qb_codes[:, cols].bitcast(FP8X4),
-                    lhsT_scale=qb_sc[:, cols],
-                    rhs=h_codes[b, u][:].bitcast(FP8X4),
-                    rhs_scale=h_sc[b, u][:],
-                    start=(b == 0),
-                    stop=(b == H_PASSES - 1),
-                )
+                return qb_codes[:, cols].bitcast(FP8X4), qb_sc[:, cols]
+
+            yb[i, u] = critic(weights, u)
 
         def copy_a(i, u):
             ya_sb[i, u] = ring.tile([P, COLS], F32, name="ya_sb")
@@ -215,152 +229,108 @@ def tile_list_twin_critic_targets_kernel(
         def finish(i, u):
             target = ring.tile([P, COLS], F32, name="target", bufs=4)
             nc.vector.scalar_tensor_tensor(
-                target[:], least[i, u][:], discount[:, i : i + 1], picked[i][:, u * COLS : (u + 1) * COLS], ALU.mult, ALU.add
+                target[:], least[i, u][:], discount[:, i : i + 1], picked[i][:, half(u)], ALU.mult, ALU.add
             )
-            nc.sync.dma_start(out[i * P : (i + 1) * P, u * COLS : (u + 1) * COLS], target[:])
+            nc.sync.dma_start(out[i * P : (i + 1) * P, half(u)], target[:])
 
+        load_tab(0)
         load_tab_scales()
         load_w(0, 0)
-        load_tab(0)
         load_w(1, 0)
-        load_w(2, 0)
         load_tab(1)
+        load_w(2, 0)
         load_tab(2)
-        load_w(0, 1)
-        load_w(1, 1)
-        load_w(2, 1)
-        load_qb(0)
+        for a in range(K_PASSES):
+            load_w(a, 1)
         load_rewards(0)
-        load_qa()
-        load_rewards(1)
-        load_rewards(2)
+        load_qb(0)
         load_qb(1)
-        gather_scales(0, 2)
-        cast_w(0, 0, "scalar", 0, 128)
-        gather_words(0, 0, 1)
-        gather_words(0, 1, 2)
-        cast_w(1, 0, "vector", 0, 128)
+        load_rewards(1)
+        load_qa_and_discount()
+        load_rewards(2)
+
+
+        gather_words(0)
+        round_w(0, 0)
+        gather_scales()
+        round_w(1, 0)
         quantize_w(0, 0)
-        cast_w(2, 0, "scalar", 0, 128)
         quantize_w(1, 0)
-        hidden_pass(0, 0, 0, [0])
-        hidden_pass(0, 0, 0, [1])
-        hidden_pass(0, 0, 0, [2])
-        gather_words(1, 0, 2)
-        hidden_pass(0, 0, 0, [3])
-        hidden_pass(0, 0, 1, [0])
-        hidden_pass(0, 0, 1, [1])
-        hidden_pass(0, 0, 1, [2])
-        hidden_pass(0, 0, 1, [3])
+        hidden_pass(0, 0, 0)
+        gather_words(1)
+        hidden_pass(0, 0, 1)
+        round_w(2, 0)
+        hidden_pass(1, 0, 0)
         quantize_w(2, 0)
-        hidden_pass(1, 0, 1, [0])
+        hidden_pass(1, 0, 1)
         gather_words(2, 0, 1)
-        hidden_pass(1, 0, 1, [1])
-        hidden_pass(1, 0, 1, [2])
-        hidden_pass(1, 0, 1, [3])
-        hidden_pass(1, 0, 0, [0])
-        hidden_pass(1, 0, 0, [1])
         gather_words(2, 1, 2)
-        cast_w(0, 1, "scalar", 96, 128)
-        hidden_pass(1, 0, 0, [2])
-        hidden_pass(1, 0, 0, [3])
-        hidden_pass(2, 0, 0, [0])
-        hidden_pass(2, 0, 0, [1])
-        cast_w(0, 1, "vector", 0, 96)
-        hidden_pass(2, 0, 0, [2])
-        relu_out(0, 0, [0])
-        hidden_pass(2, 0, 1, [0])
-        hidden_pass(2, 0, 1, [1])
-        relu_out(0, 0, [1])
-        hidden_pass(2, 0, 1, [2])
-        cast_w(1, 1, "vector", 0, 128)
-        hidden_pass(2, 0, 1, [3])
-        relu_out(0, 0, [2])
-        hidden_pass(2, 0, 0, [3])
-        relu_out(0, 1, [0])
+        hidden_pass(2, 0, 0)
+        round_w(0, 1)
+        relu_out(0, 0)
+        hidden_pass(2, 0, 1)
+
         quantize_w(0, 1)
-        relu_out(0, 0, [3])
+        round_w(1, 1)
+        hidden_pass(0, 1, 0)
+        relu_out(0, 1, range(0, 2))
+        interleave_h_vector(0, 0)
+        round_w(2, 1)
+        relu_out(0, 1, range(2, PACK))
+        hidden_pass(0, 1, 1)
         quantize_w(1, 1)
-        relu_out(0, 1, [1])
-        hidden_pass(0, 1, 0, [0])
-        cast_w(2, 1, "vector", 0, 128)
-        hidden_pass(0, 1, 0, [1])
-        relu_out(0, 1, [2])
-        hidden_pass(0, 1, 0, [2])
-        hidden_pass(0, 1, 0, [3])
-        hidden_pass(1, 1, 0, [0])
-        relu_out(0, 1, [3])
-        hidden_pass(1, 1, 0, [1])
-        cast_qb(0, "vector", 0, 24)
-        hidden_pass(1, 1, 0, [2])
-        cast_qb(0, "scalar", 24, 96)
-        interleave_h(0, 0, "vector", 0, 128)
-        hidden_pass(1, 1, 0, [3])
-        hidden_pass(0, 1, 1, [0])
-        hidden_pass(1, 1, 1, [0])
-        hidden_pass(0, 1, 1, [1])
-        interleave_h(0, 1, "scalar", 0, 128)
-        hidden_pass(1, 1, 1, [1])
         quantize_w(2, 1)
-        hidden_pass(0, 1, 1, [2])
-        hidden_pass(1, 1, 1, [2])
-        hidden_pass(0, 1, 1, [3])
+        interleave_h_scalar(0, 0)
+        gather_rewards(0)
+        interleave_h_scalar(0, 1)
+        for u in range(HALVES):
+            for t in range(PACK):
+                hidden_pass(1, 1, u, [t])
+                hidden_pass(2, 1, u, [t])
+        relu_out(1, 0)
+        nc.vector.tensor_copy(*qb_views(0))
+        interleave_h_vector(0, 1)
         quantize_h(0, 0)
-        hidden_pass(1, 1, 1, [3])
-        hidden_pass(2, 1, 0, [0])
-        gather_rewards(0, 0, 2)
-        hidden_pass(2, 1, 0, [1])
-        hidden_pass(2, 1, 0, [2])
-        relu_out(1, 0, [0])
-        hidden_pass(2, 1, 0, [3])
-        hidden_pass(2, 1, 1, [0])
-        relu_out(1, 0, [1])
-        hidden_pass(2, 1, 1, [1])
-        hidden_pass(2, 1, 1, [2])
-        hidden_pass(2, 1, 1, [3])
-        relu_out(1, 0, [2])
         quantize_h(0, 1)
-        relu_out(1, 0, [3])
-        gather_rewards(1, 0, 1)
-        relu_out(1, 1, [0])
-        relu_out(1, 1, [1])
-        interleave_h(1, 0, "vector", 0, 128)
-        relu_out(1, 1, [2])
-        relu_out(1, 1, [3])
-        gather_rewards(2, 0, 1)
-        cast_qb(1, "scalar", 0, 96)
+        interleave_h_vector(1, 0)
+        interleave_h_scalar(1, 0)
+        relu_out(1, 1)
+        gather_rewards(1)
+        nc.scalar.copy(*qb_views(1))
         quantize_h(1, 0)
-        interleave_h(1, 1, "scalar", 0, 128)
-        gather_rewards(1, 1, 2)
-        critic_a(1, 0)
-        quantize_qb([(0, 512)])
-        critic_a(2, 0)
-        quantize_qb([(512, 768)])
-        copy_a(1, 0)
-        gather_rewards(2, 1, 2)
-        critic_b(1, 0)
-        copy_a(2, 0)
-        critic_b(2, 0)
-        quantize_h(1, 1)
-        critic_b(0, 0)
-        smaller(1, 0)
+        interleave_h_scalar(1, 1)
+
+        gather_rewards(2, 0, 1)
         critic_a(0, 0)
-        smaller(2, 0)
-        critic_a(0, 1)
+        quantize_qb(0, 512)
+        critic_a(1, 0)
+        quantize_qb(512, H_PASSES * N)
         copy_a(0, 0)
-        critic_b(0, 1)
-        finish(1, 0)
-        copy_a(0, 1)
-        critic_b(2, 1)
-        finish(2, 0)
-        critic_a(1, 1)
+        gather_rewards(2, 1, 2)
+        critic_b(0, 0)
+        copy_a(1, 0)
+        critic_b(1, 0)
+        quantize_h(1, 1)
+        critic_b(2, 0)
+
         smaller(0, 0)
+        critic_a(2, 0)
+        smaller(1, 0)
+        critic_a(0, 1)
+        copy_a(2, 0)
+        critic_b(0, 1)
+        finish(0, 0)
+        copy_a(0, 1)
+        critic_a(1, 1)
+        finish(1, 0)
         critic_a(2, 1)
+        smaller(2, 0)
         copy_a(1, 1)
-        smaller(0, 1)
         critic_b(1, 1)
         copy_a(2, 1)
-        finish(0, 0)
+        smaller(0, 1)
+        critic_b(2, 1)
+        finish(2, 0)
         finish(0, 1)
         smaller(1, 1)
         smaller(2, 1)

@@ -51,7 +51,6 @@ def tile_list_twin_critic_targets_kernel(
         nc.vector.memset(tab_sc[:], 0)
         nc.vector.memset(qa_sc[:], 0)
         bias = keep.tile([P, H_PASSES, PACK], F32, name="bias")
-        nc.scalar.dma_start(bias[:], b1.rearrange("(b p t) -> p b t", p=P, t=PACK))
         discount = keep.tile([P, N_TILES], F32, name="discount")
         qa = keep.tile([P, H_PASSES, N // 2], I32, name="qa", align_bytes=64)
 
@@ -68,7 +67,7 @@ def tile_list_twin_critic_targets_kernel(
 
         def load_tab_scales():
             for q in range(QUADRANTS):
-                nc.sync.dma_start(
+                (nc.sync if q % 2 == 0 else nc.scalar).dma_start(
                     tab_sc[32 * q : 32 * q + SCALE_ROWS * K_PASSES, :],
                     tab_scales[:, SCALE_ROWS * q : SCALE_ROWS * (q + 1), :].bitcast(I32),
                 )
@@ -238,6 +237,7 @@ def tile_list_twin_critic_targets_kernel(
         load_w(0, 0)
         load_w(1, 0)
         load_tab(1)
+        nc.sync.dma_start(bias[:], b1.rearrange("(b p t) -> p b t", p=P, t=PACK))
         load_w(2, 0)
         load_tab(2)
         for a in range(K_PASSES):

@@ -14,6 +14,7 @@ U8 = mybir.dt.uint8
 FP8X4 = mybir.dt.float8_e4m3fn_x4
 FP4X4 = mybir.dt.float4_e2m1fn_x4
 RELU = mybir.ActivationFunctionType.Relu
+COPY = mybir.ActivationFunctionType.Copy
 ALU = mybir.AluOpType
 
 P = 128
@@ -30,8 +31,8 @@ LIST_COLS = COLS // 16
 RUN = 4
 PSUM_BANKS = 8
 
-W_VECTOR_PART = {(0, 0): 0, (1, 0): 64, (2, 0): 64, (0, 1): 96, (1, 1): 128, (2, 1): 64}
-H_VECTOR_PART = {(0, 0): 96, (0, 1): 48, (1, 0): 96}
+W_VECTOR_PART = {(0, 0): 0, (1, 0): 64, (2, 0): 64, (0, 1): 128, (1, 1): 128, (2, 1): 128}
+H_VECTOR_PART = {(0, 1): 128, (1, 0): 128}
 
 
 def tile_list_twin_critic_targets_kernel(
@@ -57,7 +58,10 @@ def tile_list_twin_critic_targets_kernel(
         w_raw, tab, qb_raw, rewards = {}, {}, {}, {}
 
         def load_w(a, b):
-            w_raw[a, b] = ring.tile([P, PACK, PASS], F32, name="w_raw", bufs=4)
+            if (a, b) == (2, 1):
+                w_raw[a, b] = keep.tile([P, PACK, PASS], F32, name="w_raw_last", tag="w_raw_last", align_bytes=64)
+            else:
+                w_raw[a, b] = ring.tile([P, PACK, PASS], F32, name="w_raw", bufs=4)
             rows = w1[a * PASS : (a + 1) * PASS, b * PASS : (b + 1) * PASS]
             nc.sync.dma_start(w_raw[a, b][:], rows.rearrange("(p j) c -> p j c", j=PACK))
 
@@ -73,7 +77,7 @@ def tile_list_twin_critic_targets_kernel(
                 )
 
         def load_qb(b):
-            qb_raw[b] = keep.tile([P, PACK, N], F32, name="qb_raw_%d" % b)
+            qb_raw[b] = keep.tile([P, PACK, N], F32, name="qb_raw", tag="qb_raw_%d" % b, align_bytes=64)
             nc.sync.dma_start(qb_raw[b][:], qb[b * PASS : (b + 1) * PASS, :].rearrange("(p t) n -> p t n", t=PACK))
 
         def load_qa_and_discount():
@@ -83,8 +87,6 @@ def tile_list_twin_critic_targets_kernel(
                     qa_sc[32 * q : 32 * q + SCALE_ROWS, :, :],
                     qa_scales[:, SCALE_ROWS * q : SCALE_ROWS * (q + 1), :].rearrange("b r n -> r b n").bitcast(I32),
                 )
-            with nc.allow_non_contiguous_dma(reason="one discount a partition"):
-                nc.sync.dma_start(discount[:], disc.rearrange("(i p) -> p i", p=P))
 
         def load_rewards(i):
             rewards[i] = keep.tile([P, T], F32, name="rewards_%d" % i, align_bytes=64)
@@ -92,7 +94,6 @@ def tile_list_twin_critic_targets_kernel(
 
         v_sc = keep.tile([P, S], U8, name="v_sc", align_bytes=64)
         v_codes = [keep.tile([P, S], U32, name="v_codes_%d" % a, align_bytes=64) for a in range(K_PASSES)]
-        picked = [keep.tile([P, S], F32, name="picked_%d" % i) for i in range(N_TILES)]
 
         def gather(dst, window, first, last):
             picks = offsets[:, first * LIST_COLS : last * LIST_COLS]
@@ -104,8 +105,6 @@ def tile_list_twin_critic_targets_kernel(
         def gather_words(a, first=0, last=HALVES):
             gather(v_codes[a], tab[a][:].bitcast(U32), first, last)
 
-        def gather_rewards(i, first=0, last=HALVES):
-            gather(picked[i], rewards[i][:], first, last)
 
         def half(u):
             return slice(u * COLS, (u + 1) * COLS)
@@ -114,7 +113,10 @@ def tile_list_twin_critic_targets_kernel(
         banks, h_rows, h_bf, h_codes, h_sc = {}, {}, {}, {}, {}
 
         def round_w(a, b):
-            w_bf[a, b] = ring.tile([P, PACK * PASS], BF16, name="w_bf", align_bytes=64)
+            if (a, b) == (2, 1):
+                w_bf[a, b] = keep.tile([P, PACK * PASS], BF16, name="w_last", tag="w_last", align_bytes=64)
+            else:
+                w_bf[a, b] = ring.tile([P, PACK * PASS], BF16, name="w_bf", align_bytes=64)
             dst = w_bf[a, b][:].rearrange("p (t m j) -> p m j t", t=PACK, j=PACK)
             src = w_raw[a, b][:].rearrange("p j (m t) -> p m j t", t=PACK)
             cut = W_VECTOR_PART[a, b]
@@ -145,7 +147,7 @@ def tile_list_twin_critic_targets_kernel(
 
         def relu_out(b, u, tiles=range(PACK)):
             if (b, u) not in h_rows:
-                h_rows[b, u] = ring.tile([P, PACK, COLS], BF16, name="h_rows", bufs=H_PASSES * HALVES)
+                h_rows[b, u] = keep.tile([P, PACK, COLS], BF16, name="h_rows", tag="h_rows_%d_%d" % (b, u), align_bytes=64)
             for t in tiles:
                 nc.scalar.activation(h_rows[b, u][:, t, :], banks[b, u, t][:], RELU, bias=bias[:, b, t : t + 1])
 
@@ -156,7 +158,8 @@ def tile_list_twin_critic_targets_kernel(
 
         def h_views(b, u):
             if (b, u) not in h_bf:
-                h_bf[b, u] = ring.tile([P, COLS * PACK], BF16, name="h_bf", align_bytes=64)
+                tag = {(0, 1): "h_bf_1_0"}.get((b, u), "h_bf_%d_%d" % (b, u))
+                h_bf[b, u] = keep.tile([P, COLS * PACK], BF16, name="h_bf", tag=tag, align_bytes=64)
             return interleave_views(h_bf[b, u][:], h_rows[b, u][:])
 
         def interleave_h_vector(b, u):
@@ -164,29 +167,31 @@ def tile_list_twin_critic_targets_kernel(
             cut = H_VECTOR_PART[b, u]
             nc.vector.tensor_copy(dst[:, 0:cut], src[:, 0:cut])
 
-        def interleave_h_scalar(b, u):
+        def interleave_h_scalar(b, u, lo=0, hi=P):
             dst, src = h_views(b, u)
-            cut = H_VECTOR_PART.get((b, u), 0)
-            nc.scalar.copy(dst[:, cut:P], src[:, cut:P])
+            nc.scalar.copy(dst[:, lo:hi], src[:, lo:hi])
 
         def quantize_h(b, u):
-            h_codes[b, u] = keep.tile([P, COLS], U32, name="h_codes_%d_%d" % (b, u), align_bytes=64)
+            tag = {(0, 0): "w_last"}.get((b, u), "h_codes_%d_%d" % (b, u))
+            h_codes[b, u] = keep.tile([P, COLS], U32, name="h_codes", tag=tag, align_bytes=64)
             h_sc[b, u] = keep.tile([P, COLS], U8, name="h_sc_%d_%d" % (b, u), align_bytes=64)
             nc.vector.quantize_mx(out=h_codes[b, u][:].bitcast(FP8X4), scales=h_sc[b, u][:], in_=h_bf[b, u][:])
 
-        qb_bf = keep.tile([P, H_PASSES * N * PACK], BF16, name="qb_bf", align_bytes=64)
+        qb_tile = []
         qb_codes = keep.tile([P, H_PASSES * N], U32, name="qb_codes", align_bytes=64)
         qb_sc = keep.tile([P, H_PASSES * N], U8, name="qb_sc", align_bytes=64)
 
         def qb_views(b):
-            return interleave_views(qb_bf[:, b * N * PACK : (b + 1) * N * PACK], qb_raw[b][:])
+            if b == 0:
+                qb_tile.append(keep.tile([P, H_PASSES * N * PACK], BF16, name="qb_bf", tag="w_raw_last", align_bytes=64))
+            return interleave_views(qb_tile[0][:, b * N * PACK : (b + 1) * N * PACK], qb_raw[b][:])
 
         def quantize_qb(lo, hi):
             nc.vector.quantize_mx(
-                out=qb_codes[:, lo:hi].bitcast(FP8X4), scales=qb_sc[:, lo:hi], in_=qb_bf[:, lo * PACK : hi * PACK]
+                out=qb_codes[:, lo:hi].bitcast(FP8X4), scales=qb_sc[:, lo:hi], in_=qb_tile[0][:, lo * PACK : hi * PACK]
             )
 
-        ya, yb, ya_sb, least = {}, {}, {}, {}
+        ya, yb, ya_sb, least, scaled = {}, {}, {}, {}, {}
 
         def critic(weights, u):
             y = psum.tile([P, COLS], F32, name="bank")
@@ -222,32 +227,36 @@ def tile_list_twin_critic_targets_kernel(
             nc.scalar.copy(ya_sb[i, u][:], ya[i, u][:])
 
         def smaller(i, u):
-            least[i, u] = ring.tile([P, COLS], F32, name="least", bufs=4)
+            least[i, u] = keep.tile([P, COLS], F32, name="least", tag="least_%d_%d" % (i, u), align_bytes=64)
             nc.vector.tensor_tensor(least[i, u][:], yb[i, u][:], ya_sb[i, u][:], ALU.min)
+
+        def discounted(i, u):
+            scaled[i, u] = ring.tile([P, COLS], F32, name="scaled", bufs=6)
+            nc.scalar.activation(scaled[i, u][:], least[i, u][:], COPY, scale=discount[:, i : i + 1])
 
         def finish(i, u):
             target = ring.tile([P, COLS], F32, name="target", bufs=4)
-            nc.vector.scalar_tensor_tensor(
-                target[:], least[i, u][:], discount[:, i : i + 1], picked[i][:, half(u)], ALU.mult, ALU.add
-            )
+            picks = offsets[:, u * LIST_COLS : (u + 1) * LIST_COLS]
+            nc.vector.tensor_tensor(target[:], rewards[i][:].indirect(picks), scaled[i, u][:], ALU.add)
             nc.sync.dma_start(out[i * P : (i + 1) * P, half(u)], target[:])
 
         load_tab(0)
         load_tab_scales()
+        nc.scalar.dma_start(bias[:], b1.rearrange("(b p t) -> p b t", p=P, t=PACK))
+        with nc.allow_non_contiguous_dma(reason="one discount a partition"):
+            nc.scalar.dma_start(discount[:], disc.rearrange("(i p) -> p i", p=P))
         load_w(0, 0)
         load_w(1, 0)
         load_tab(1)
-        nc.sync.dma_start(bias[:], b1.rearrange("(b p t) -> p b t", p=P, t=PACK))
         load_w(2, 0)
         load_tab(2)
         for a in range(K_PASSES):
             load_w(a, 1)
-        load_rewards(0)
         load_qb(0)
         load_qb(1)
-        load_rewards(1)
         load_qa_and_discount()
-        load_rewards(2)
+        for i in range(N_TILES):
+            load_rewards(i)
 
 
         gather_words(0)
@@ -271,68 +280,46 @@ def tile_list_twin_critic_targets_kernel(
         hidden_pass(2, 0, 1)
 
         quantize_w(0, 1)
-        round_w(1, 1)
+        relu_out(0, 1)
         hidden_pass(0, 1, 0)
-        relu_out(0, 1, range(0, 2))
-        interleave_h_vector(0, 0)
-        round_w(2, 1)
-        relu_out(0, 1, range(2, PACK))
-        hidden_pass(0, 1, 1)
+        round_w(1, 1)
         quantize_w(1, 1)
-        quantize_w(2, 1)
         interleave_h_scalar(0, 0)
-        gather_rewards(0)
-        interleave_h_scalar(0, 1)
-        for u in range(HALVES):
-            for t in range(PACK):
-                hidden_pass(1, 1, u, [t])
-                hidden_pass(2, 1, u, [t])
+        hidden_pass(1, 1, 0)
+        round_w(2, 1)
+        quantize_w(2, 1)
+        hidden_pass(2, 1, 0)
+        for a in range(K_PASSES):
+            hidden_pass(a, 1, 1)
         relu_out(1, 0)
-        nc.vector.tensor_copy(*qb_views(0))
-        interleave_h_vector(0, 1)
-        quantize_h(0, 0)
-        quantize_h(0, 1)
-        interleave_h_vector(1, 0)
-        interleave_h_scalar(1, 0)
         relu_out(1, 1)
-        gather_rewards(1)
-        nc.scalar.copy(*qb_views(1))
-        quantize_h(1, 0)
-        interleave_h_scalar(1, 1)
-
-        gather_rewards(2, 0, 1)
-        critic_a(0, 0)
+        quantize_h(0, 0)
+        qb_dst, qb_src = qb_views(0)
+        nc.scalar.copy(qb_dst[:, 0:48], qb_src[:, 0:48])
+        nc.vector.tensor_copy(qb_dst[:, 48:96], qb_src[:, 48:96])
+        nc.vector.tensor_copy(*qb_views(1))
+        interleave_h_vector(1, 0)
         quantize_qb(0, 512)
-        critic_a(1, 0)
+        quantize_h(1, 0)
         quantize_qb(512, H_PASSES * N)
-        copy_a(0, 0)
-        gather_rewards(2, 1, 2)
-        critic_b(0, 0)
-        copy_a(1, 0)
-        critic_b(1, 0)
+        interleave_h_vector(0, 1)
+        interleave_h_scalar(1, 1, 0, P // 2)
+        for i in range(N_TILES):
+            critic_a(i, 0)
+            critic_b(i, 0)
+            copy_a(i, 0)
+            smaller(i, 0)
+        interleave_h_scalar(1, 1, P // 2, P)
+        quantize_h(0, 1)
         quantize_h(1, 1)
-        critic_b(2, 0)
-
-        smaller(0, 0)
-        critic_a(2, 0)
-        smaller(1, 0)
-        critic_a(0, 1)
-        copy_a(2, 0)
-        critic_b(0, 1)
-        finish(0, 0)
-        copy_a(0, 1)
-        critic_a(1, 1)
-        finish(1, 0)
-        critic_a(2, 1)
-        smaller(2, 0)
-        copy_a(1, 1)
-        critic_b(1, 1)
-        copy_a(2, 1)
-        smaller(0, 1)
-        critic_b(2, 1)
-        finish(2, 0)
-        finish(0, 1)
-        smaller(1, 1)
-        smaller(2, 1)
-        finish(1, 1)
-        finish(2, 1)
+        for i in range(N_TILES):
+            discounted(i, 0)
+            finish(i, 0)
+        for i in range(N_TILES):
+            critic_a(i, 1)
+            critic_b(i, 1)
+            copy_a(i, 1)
+            smaller(i, 1)
+        for i in range(N_TILES):
+            discounted(i, 1)
+            finish(i, 1)

@@ -22,6 +22,7 @@ PACK = 4
 PASS = P * PACK
 K_PASSES = K // PASS
 H_PASSES = H // PASS
+LAST = K_PASSES - 1
 COLS = 512
 HALVES = S // COLS
 N_TILES = N // P
@@ -30,9 +31,8 @@ SCALE_ROWS = 4
 LIST_COLS = COLS // 16
 RUN = 4
 PSUM_BANKS = 8
-
-W_VECTOR_PART = {(0, 0): 0, (1, 0): 64, (2, 0): 64, (0, 1): 128, (1, 1): 128, (2, 1): 128}
-H_VECTOR_PART = {(0, 1): 128, (1, 0): 128}
+QB_FIRST = 512
+QB_SCALAR_COLS = 192
 
 
 def tile_list_twin_critic_targets_kernel(
@@ -57,13 +57,15 @@ def tile_list_twin_critic_targets_kernel(
 
         w_raw, tab, qb_raw, rewards = {}, {}, {}, {}
 
-        def load_w(a, b):
-            if (a, b) == (2, 1):
-                w_raw[a, b] = keep.tile([P, PACK, PASS], F32, name="w_raw_last", tag="w_raw_last", align_bytes=64)
-            else:
-                w_raw[a, b] = ring.tile([P, PACK, PASS], F32, name="w_raw", bufs=4)
-            rows = w1[a * PASS : (a + 1) * PASS, b * PASS : (b + 1) * PASS]
-            nc.sync.dma_start(w_raw[a, b][:], rows.rearrange("(p j) c -> p j c", j=PACK))
+        def load_w(a, b, pieces=1):
+            width = PASS // pieces
+            w_raw[a, b] = []
+            for n in range(pieces):
+                tag = "w_raw_%d_%d_%d" % (a, b, n)
+                piece = keep.tile([P, PACK, width], F32, name="w_raw", tag=tag, align_bytes=64)
+                rows = w1[a * PASS : (a + 1) * PASS, b * PASS + n * width : b * PASS + (n + 1) * width]
+                nc.sync.dma_start(piece[:], rows.rearrange("(p j) c -> p j c", j=PACK))
+                w_raw[a, b].append(piece)
 
         def load_tab(a):
             tab[a] = keep.tile([P, T], I32, name="tab_%d" % a, align_bytes=64)
@@ -71,21 +73,27 @@ def tile_list_twin_critic_targets_kernel(
 
         def load_tab_scales():
             for q in range(QUADRANTS):
-                (nc.sync if q % 2 == 0 else nc.scalar).dma_start(
+                queue = nc.sync if q % 2 == 0 else nc.scalar
+                queue.dma_start(
                     tab_sc[32 * q : 32 * q + SCALE_ROWS * K_PASSES, :],
                     tab_scales[:, SCALE_ROWS * q : SCALE_ROWS * (q + 1), :].bitcast(I32),
                 )
 
+        def load_bias_and_discount():
+            nc.scalar.dma_start(bias[:], b1.rearrange("(b p t) -> p b t", p=P, t=PACK))
+            with nc.allow_non_contiguous_dma(reason="one discount a partition"):
+                nc.scalar.dma_start(discount[:], disc.rearrange("(i p) -> p i", p=P))
+
         def load_qb(b):
-            qb_raw[b] = keep.tile([P, PACK, N], F32, name="qb_raw", tag="qb_raw_%d" % b, align_bytes=64)
+            qb_raw[b] = keep.tile([P, PACK, N], F32, name="qb_raw_%d" % b)
             nc.sync.dma_start(qb_raw[b][:], qb[b * PASS : (b + 1) * PASS, :].rearrange("(p t) n -> p t n", t=PACK))
 
-        def load_qa_and_discount():
+        def load_qa():
             nc.sync.dma_start(qa[:], qa_words.rearrange("b p c -> p b c").bitcast(I32))
             for q in range(QUADRANTS):
                 nc.sync.dma_start(
                     qa_sc[32 * q : 32 * q + SCALE_ROWS, :, :],
-                    qa_scales[:, SCALE_ROWS * q : SCALE_ROWS * (q + 1), :].rearrange("b r n -> r b n").bitcast(I32),
+                    qa_scales[:, SCALE_ROWS * q : SCALE_ROWS * (q + 1), :].rearrange("b s n -> s b n").bitcast(I32),
                 )
 
         def load_rewards(i):
@@ -95,16 +103,15 @@ def tile_list_twin_critic_targets_kernel(
         v_sc = keep.tile([P, S], U8, name="v_sc", align_bytes=64)
         v_codes = [keep.tile([P, S], U32, name="v_codes_%d" % a, align_bytes=64) for a in range(K_PASSES)]
 
-        def gather(dst, window, first, last):
-            picks = offsets[:, first * LIST_COLS : last * LIST_COLS]
-            nc.vector.tensor_copy(dst[:, first * COLS : last * COLS], window.indirect(picks))
+        def picks(first, last):
+            return offsets[:, first * LIST_COLS : last * LIST_COLS]
 
         def gather_scales():
-            gather(v_sc, tab_sc[:].bitcast(U8), 0, HALVES)
+            nc.vector.tensor_copy(v_sc[:], tab_sc[:].bitcast(U8).indirect(picks(0, HALVES)))
 
         def gather_words(a, first=0, last=HALVES):
-            gather(v_codes[a], tab[a][:].bitcast(U32), first, last)
-
+            window = tab[a][:].bitcast(U32)
+            nc.vector.tensor_copy(v_codes[a][:, first * COLS : last * COLS], window.indirect(picks(first, last)))
 
         def half(u):
             return slice(u * COLS, (u + 1) * COLS)
@@ -112,26 +119,26 @@ def tile_list_twin_critic_targets_kernel(
         w_bf, w_codes, w_sc = {}, {}, {}
         banks, h_rows, h_bf, h_codes, h_sc = {}, {}, {}, {}, {}
 
-        def round_w(a, b):
-            if (a, b) == (2, 1):
-                w_bf[a, b] = keep.tile([P, PACK * PASS], BF16, name="w_last", tag="w_last", align_bytes=64)
+        def round_w(a, b, copies):
+            if (a, b) == (LAST, 1):
+                w_bf[a, b] = keep.tile([P, PACK * PASS], BF16, name="w_bf_last", tag="w_bf_last", align_bytes=64)
             else:
                 w_bf[a, b] = ring.tile([P, PACK * PASS], BF16, name="w_bf", align_bytes=64)
             dst = w_bf[a, b][:].rearrange("p (t m j) -> p m j t", t=PACK, j=PACK)
-            src = w_raw[a, b][:].rearrange("p j (m t) -> p m j t", t=PACK)
-            cut = W_VECTOR_PART[a, b]
-            if cut > 0:
-                nc.vector.tensor_copy(dst[:, 0:cut], src[:, 0:cut])
-            if cut < P:
-                nc.scalar.copy(dst[:, cut:P], src[:, cut:P])
+            share = P // len(copies)
+            per_piece = P // len(w_raw[a, b])
+            for n, copy in enumerate(copies):
+                piece, first = divmod(n * share, per_piece)
+                src = w_raw[a, b][piece][:].rearrange("p j (m t) -> p m j t", t=PACK)
+                copy(dst[:, n * share : (n + 1) * share], src[:, first : first + share])
 
         def quantize_w(a, b):
             w_codes[a, b] = keep.tile([P, PASS], U32, name="w_codes_%d_%d" % (a, b), align_bytes=64)
             w_sc[a, b] = keep.tile([P, PASS], U8, name="w_sc_%d_%d" % (a, b), align_bytes=64)
             nc.vector.quantize_mx(out=w_codes[a, b][:].bitcast(FP8X4), scales=w_sc[a, b][:], in_=w_bf[a, b][:])
 
-        def hidden_pass(a, b, u, tiles=range(PACK)):
-            for t in tiles:
+        def hidden_pass(a, b, u):
+            for t in range(PACK):
                 if a == 0:
                     banks[b, u, t] = psum.tile([P, COLS], F32, name="bank")
                 cols = slice(t * P, (t + 1) * P)
@@ -142,13 +149,12 @@ def tile_list_twin_critic_targets_kernel(
                     rhs=v_codes[a][:, half(u)].bitcast(FP8X4),
                     rhs_scale=v_sc[SCALE_ROWS * a : P, half(u)],
                     start=(a == 0),
-                    stop=(a == K_PASSES - 1),
+                    stop=(a == LAST),
                 )
 
-        def relu_out(b, u, tiles=range(PACK)):
-            if (b, u) not in h_rows:
-                h_rows[b, u] = keep.tile([P, PACK, COLS], BF16, name="h_rows", tag="h_rows_%d_%d" % (b, u), align_bytes=64)
-            for t in tiles:
+        def relu_out(b, u):
+            h_rows[b, u] = keep.tile([P, PACK, COLS], BF16, name="h_rows_%d_%d" % (b, u), align_bytes=64)
+            for t in range(PACK):
                 nc.scalar.activation(h_rows[b, u][:, t, :], banks[b, u, t][:], RELU, bias=bias[:, b, t : t + 1])
 
         def interleave_views(grouped, rows):
@@ -156,47 +162,44 @@ def tile_list_twin_critic_targets_kernel(
             src = rows.rearrange("p t (c i) -> p c t i", i=RUN)
             return dst, src
 
-        def h_views(b, u):
-            if (b, u) not in h_bf:
-                tag = {(0, 1): "h_bf_1_0"}.get((b, u), "h_bf_%d_%d" % (b, u))
-                h_bf[b, u] = keep.tile([P, COLS * PACK], BF16, name="h_bf", tag=tag, align_bytes=64)
+        def h_views(b, u, tag):
+            h_bf[b, u] = keep.tile([P, COLS * PACK], BF16, name="h_bf", tag=tag, align_bytes=64)
             return interleave_views(h_bf[b, u][:], h_rows[b, u][:])
 
-        def interleave_h_vector(b, u):
-            dst, src = h_views(b, u)
-            cut = H_VECTOR_PART[b, u]
-            nc.vector.tensor_copy(dst[:, 0:cut], src[:, 0:cut])
-
-        def interleave_h_scalar(b, u, lo=0, hi=P):
-            dst, src = h_views(b, u)
-            nc.scalar.copy(dst[:, lo:hi], src[:, lo:hi])
-
-        def quantize_h(b, u):
-            tag = {(0, 0): "w_last"}.get((b, u), "h_codes_%d_%d" % (b, u))
+        def quantize_h(b, u, tag):
             h_codes[b, u] = keep.tile([P, COLS], U32, name="h_codes", tag=tag, align_bytes=64)
             h_sc[b, u] = keep.tile([P, COLS], U8, name="h_sc_%d_%d" % (b, u), align_bytes=64)
             nc.vector.quantize_mx(out=h_codes[b, u][:].bitcast(FP8X4), scales=h_sc[b, u][:], in_=h_bf[b, u][:])
 
-        qb_tile = []
         qb_codes = keep.tile([P, H_PASSES * N], U32, name="qb_codes", align_bytes=64)
         qb_sc = keep.tile([P, H_PASSES * N], U8, name="qb_sc", align_bytes=64)
 
-        def qb_views(b):
-            if b == 0:
-                qb_tile.append(keep.tile([P, H_PASSES * N * PACK], BF16, name="qb_bf", tag="w_raw_last", align_bytes=64))
-            return interleave_views(qb_tile[0][:, b * N * PACK : (b + 1) * N * PACK], qb_raw[b][:])
+        def round_qb():
+            qb_bf = keep.tile([P, H_PASSES * N * PACK], BF16, name="qb_bf", tag="w_raw_2_1_1", align_bytes=64)
+            dst, src = interleave_views(qb_bf[:, 0 : N * PACK], qb_raw[0][:])
+            cut = QB_SCALAR_COLS // RUN
+            nc.scalar.copy(dst[:, 0:cut], src[:, 0:cut])
+            nc.vector.tensor_copy(dst[:, cut : N // RUN], src[:, cut : N // RUN])
+            nc.vector.tensor_copy(*interleave_views(qb_bf[:, N * PACK : 2 * N * PACK], qb_raw[1][:]))
+            return qb_bf
 
-        def quantize_qb(lo, hi):
+        def quantize_qb(qb_bf, lo, hi):
             nc.vector.quantize_mx(
-                out=qb_codes[:, lo:hi].bitcast(FP8X4), scales=qb_sc[:, lo:hi], in_=qb_tile[0][:, lo * PACK : hi * PACK]
+                out=qb_codes[:, lo:hi].bitcast(FP8X4), scales=qb_sc[:, lo:hi], in_=qb_bf[:, lo * PACK : hi * PACK]
             )
 
-        ya, yb, ya_sb, least, scaled = {}, {}, {}, {}, {}
+        def qa_weights(i, b):
+            codes = qa[:, b, :].bitcast(U8)[:, 2 * i * P : 2 * (i + 1) * P].bitcast(FP4X4)
+            return codes, qa_sc[:, b, :].bitcast(U8)[:, i * P : (i + 1) * P]
 
-        def critic(weights, u):
+        def qb_weights(i, b):
+            cols = slice(b * N + i * P, b * N + (i + 1) * P)
+            return qb_codes[:, cols].bitcast(FP8X4), qb_sc[:, cols]
+
+        def critic(weights, i, u):
             y = psum.tile([P, COLS], F32, name="bank")
             for b in range(H_PASSES):
-                codes, scales = weights(b)
+                codes, scales = weights(i, b)
                 nc.tensor.matmul_mx(
                     out=y[:],
                     lhsT=codes,
@@ -208,118 +211,88 @@ def tile_list_twin_critic_targets_kernel(
                 )
             return y
 
-        def critic_a(i, u):
-            def weights(b):
-                codes = qa[:, b, :].bitcast(U8)[:, 2 * i * P : 2 * (i + 1) * P].bitcast(FP4X4)
-                return codes, qa_sc[:, b, :].bitcast(U8)[:, i * P : (i + 1) * P]
+        least = {}
 
-            ya[i, u] = critic(weights, u)
-
-        def critic_b(i, u):
-            def weights(b):
-                cols = slice(b * N + i * P, b * N + (i + 1) * P)
-                return qb_codes[:, cols].bitcast(FP8X4), qb_sc[:, cols]
-
-            yb[i, u] = critic(weights, u)
-
-        def copy_a(i, u):
-            ya_sb[i, u] = ring.tile([P, COLS], F32, name="ya_sb")
-            nc.scalar.copy(ya_sb[i, u][:], ya[i, u][:])
-
-        def smaller(i, u):
-            least[i, u] = keep.tile([P, COLS], F32, name="least", tag="least_%d_%d" % (i, u), align_bytes=64)
-            nc.vector.tensor_tensor(least[i, u][:], yb[i, u][:], ya_sb[i, u][:], ALU.min)
-
-        def discounted(i, u):
-            scaled[i, u] = ring.tile([P, COLS], F32, name="scaled", bufs=6)
-            nc.scalar.activation(scaled[i, u][:], least[i, u][:], COPY, scale=discount[:, i : i + 1])
+        def smaller_critic(i, u):
+            ya = critic(qa_weights, i, u)
+            yb = critic(qb_weights, i, u)
+            ya_sb = ring.tile([P, COLS], F32, name="ya_sb")
+            nc.scalar.copy(ya_sb[:], ya[:])
+            least[i, u] = keep.tile([P, COLS], F32, name="least_%d_%d" % (i, u), align_bytes=64)
+            nc.vector.tensor_tensor(least[i, u][:], yb[:], ya_sb[:], ALU.min)
 
         def finish(i, u):
+            scaled = ring.tile([P, COLS], F32, name="scaled", bufs=N_TILES * HALVES)
+            nc.scalar.activation(scaled[:], least[i, u][:], COPY, scale=discount[:, i : i + 1])
             target = ring.tile([P, COLS], F32, name="target", bufs=4)
-            picks = offsets[:, u * LIST_COLS : (u + 1) * LIST_COLS]
-            nc.vector.tensor_tensor(target[:], rewards[i][:].indirect(picks), scaled[i, u][:], ALU.add)
+            nc.vector.tensor_tensor(target[:], rewards[i][:].indirect(picks(u, u + 1)), scaled[:], ALU.add)
             nc.sync.dma_start(out[i * P : (i + 1) * P, half(u)], target[:])
 
         load_tab(0)
         load_tab_scales()
-        nc.scalar.dma_start(bias[:], b1.rearrange("(b p t) -> p b t", p=P, t=PACK))
-        with nc.allow_non_contiguous_dma(reason="one discount a partition"):
-            nc.scalar.dma_start(discount[:], disc.rearrange("(i p) -> p i", p=P))
+        load_bias_and_discount()
         load_w(0, 0)
         load_w(1, 0)
         load_tab(1)
-        load_w(2, 0)
-        load_tab(2)
-        for a in range(K_PASSES):
+        load_w(LAST, 0)
+        load_tab(LAST)
+        for a in range(LAST):
             load_w(a, 1)
-        load_qb(0)
-        load_qb(1)
-        load_qa_and_discount()
+        load_w(LAST, 1, 2)
+        for b in range(H_PASSES):
+            load_qb(b)
+        load_qa()
         for i in range(N_TILES):
             load_rewards(i)
 
-
+        on_vector, on_scalar = nc.vector.tensor_copy, nc.scalar.copy
         gather_words(0)
-        round_w(0, 0)
+        round_w(0, 0, [on_scalar])
         gather_scales()
-        round_w(1, 0)
+        round_w(1, 0, [on_vector, on_scalar])
         quantize_w(0, 0)
         quantize_w(1, 0)
-        hidden_pass(0, 0, 0)
         gather_words(1)
-        hidden_pass(0, 0, 1)
-        round_w(2, 0)
-        hidden_pass(1, 0, 0)
-        quantize_w(2, 0)
-        hidden_pass(1, 0, 1)
-        gather_words(2, 0, 1)
-        gather_words(2, 1, 2)
-        hidden_pass(2, 0, 0)
-        round_w(0, 1)
-        relu_out(0, 0)
-        hidden_pass(2, 0, 1)
+        round_w(LAST, 0, [on_vector, on_scalar])
+        quantize_w(LAST, 0)
+        for a in range(LAST):
+            for u in range(HALVES):
+                hidden_pass(a, 0, u)
+        for u in range(HALVES):
+            gather_words(LAST, u, u + 1)
+        for u in range(HALVES):
+            hidden_pass(LAST, 0, u)
+            relu_out(0, u)
 
-        quantize_w(0, 1)
-        relu_out(0, 1)
-        hidden_pass(0, 1, 0)
-        round_w(1, 1)
-        quantize_w(1, 1)
-        interleave_h_scalar(0, 0)
-        hidden_pass(1, 1, 0)
-        round_w(2, 1)
-        quantize_w(2, 1)
-        hidden_pass(2, 1, 0)
-        for a in range(K_PASSES):
-            hidden_pass(a, 1, 1)
-        relu_out(1, 0)
-        relu_out(1, 1)
-        quantize_h(0, 0)
-        qb_dst, qb_src = qb_views(0)
-        nc.scalar.copy(qb_dst[:, 0:48], qb_src[:, 0:48])
-        nc.vector.tensor_copy(qb_dst[:, 48:96], qb_src[:, 48:96])
-        nc.vector.tensor_copy(*qb_views(1))
-        interleave_h_vector(1, 0)
-        quantize_qb(0, 512)
-        quantize_h(1, 0)
-        quantize_qb(512, H_PASSES * N)
-        interleave_h_vector(0, 1)
-        interleave_h_scalar(1, 1, 0, P // 2)
+        for a in range(LAST):
+            round_w(a, 1, [on_vector])
+            quantize_w(a, 1)
+        round_w(LAST, 1, [on_vector, on_vector])
+        quantize_w(LAST, 1)
+        nc.scalar.copy(*h_views(0, 0, "h_bf_0_0"))
+        for u in range(HALVES):
+            for a in range(K_PASSES):
+                hidden_pass(a, 1, u)
+        for u in range(HALVES):
+            relu_out(1, u)
+
+        quantize_h(0, 0, "w_bf_last")
+        qb_bf = round_qb()
+        nc.vector.tensor_copy(*h_views(1, 0, "h_bf_vector"))
+        quantize_qb(qb_bf, 0, QB_FIRST)
+        quantize_h(1, 0, "h_codes_1_0")
+        quantize_qb(qb_bf, QB_FIRST, H_PASSES * N)
+
+        nc.vector.tensor_copy(*h_views(0, 1, "h_bf_vector"))
+        nc.scalar.copy(*h_views(1, 1, "h_bf_1_1"))
+
         for i in range(N_TILES):
-            critic_a(i, 0)
-            critic_b(i, 0)
-            copy_a(i, 0)
-            smaller(i, 0)
-        interleave_h_scalar(1, 1, P // 2, P)
-        quantize_h(0, 1)
-        quantize_h(1, 1)
+            smaller_critic(i, 0)
+        for b in range(H_PASSES):
+            quantize_h(b, 1, "h_codes_%d_1" % b)
         for i in range(N_TILES):
-            discounted(i, 0)
             finish(i, 0)
         for i in range(N_TILES):
-            critic_a(i, 1)
-            critic_b(i, 1)
-            copy_a(i, 1)
-            smaller(i, 1)
+            smaller_critic(i, 1)
         for i in range(N_TILES):
-            discounted(i, 1)
             finish(i, 1)

@@ -29,7 +29,8 @@ N_TILES = N // P
 QUADRANTS = 4
 SCALE_ROWS = 4
 LIST_COLS = COLS // 16
-RUN = 4
+RUN_F32 = 4
+RUN_BF16 = 8
 PSUM_BANKS = 8
 QB_FIRST = 512
 QB_SCALAR_COLS = 192
@@ -157,14 +158,14 @@ def tile_list_twin_critic_targets_kernel(
             for t in range(PACK):
                 nc.scalar.activation(h_rows[b, u][:, t, :], banks[b, u, t][:], RELU, bias=bias[:, b, t : t + 1])
 
-        def interleave_views(grouped, rows):
-            dst = grouped.rearrange("p (c i t) -> p c t i", i=RUN, t=PACK)
-            src = rows.rearrange("p t (c i) -> p c t i", i=RUN)
+        def interleave_views(grouped, rows, run):
+            dst = grouped.rearrange("p (c i t) -> p c t i", i=run, t=PACK)
+            src = rows.rearrange("p t (c i) -> p c t i", i=run)
             return dst, src
 
         def h_views(b, u, tag):
             h_bf[b, u] = keep.tile([P, COLS * PACK], BF16, name="h_bf", tag=tag, align_bytes=64)
-            return interleave_views(h_bf[b, u][:], h_rows[b, u][:])
+            return interleave_views(h_bf[b, u][:], h_rows[b, u][:], RUN_BF16)
 
         def quantize_h(b, u, tag):
             h_codes[b, u] = keep.tile([P, COLS], U32, name="h_codes", tag=tag, align_bytes=64)
@@ -176,11 +177,11 @@ def tile_list_twin_critic_targets_kernel(
 
         def round_qb():
             qb_bf = keep.tile([P, H_PASSES * N * PACK], BF16, name="qb_bf", tag="w_raw_2_1_1", align_bytes=64)
-            dst, src = interleave_views(qb_bf[:, 0 : N * PACK], qb_raw[0][:])
-            cut = QB_SCALAR_COLS // RUN
+            dst, src = interleave_views(qb_bf[:, 0 : N * PACK], qb_raw[0][:], RUN_F32)
+            cut = QB_SCALAR_COLS // RUN_F32
             nc.scalar.copy(dst[:, 0:cut], src[:, 0:cut])
-            nc.vector.tensor_copy(dst[:, cut : N // RUN], src[:, cut : N // RUN])
-            nc.vector.tensor_copy(*interleave_views(qb_bf[:, N * PACK : 2 * N * PACK], qb_raw[1][:]))
+            nc.vector.tensor_copy(dst[:, cut : N // RUN_F32], src[:, cut : N // RUN_F32])
+            nc.vector.tensor_copy(*interleave_views(qb_bf[:, N * PACK : 2 * N * PACK], qb_raw[1][:], RUN_F32))
             return qb_bf
 
         def quantize_qb(qb_bf, lo, hi):

@@ -1,6 +1,7 @@
 from contextlib import ExitStack
 
 import concourse.mybir as mybir
+from concourse.masks import make_identity
 
 K, T, S, H, N = 1536, 2048, 1024, 1024, 384
 FLOPS = 2 * K * H * S + 2 * 2 * H * N * S
@@ -51,8 +52,12 @@ def tile_list_twin_critic_targets_kernel(
         tab_sc = keep.tile([P, T // 4], I32, name="tab_sc", align_bytes=64)
         qa_sc = keep.tile([P, H_PASSES, N // 4], I32, name="qa_sc", align_bytes=64)
         nc.vector.memset(tab_sc[:], 0)
+        bias_rows = keep.tile([P, PASS], F32, name="bias_rows", tag="least_0_0", align_bytes=64)
+        disc_rows = keep.tile([P, P], F32, name="disc_rows", tag="least_1_0", align_bytes=64)
+        nc.vector.memset(bias_rows[:], 0.0)
+        nc.vector.memset(disc_rows[:], 0.0)
         nc.vector.memset(qa_sc[:], 0)
-        bias = keep.tile([P, H_PASSES, PACK], F32, name="bias")
+        bias = keep.tile([P, PACK, H_PASSES], F32, name="bias")
         discount = keep.tile([P, N_TILES], F32, name="discount")
         qa = keep.tile([P, H_PASSES, N // 2], I32, name="qa", align_bytes=64)
 
@@ -81,9 +86,17 @@ def tile_list_twin_critic_targets_kernel(
                 )
 
         def load_bias_and_discount():
-            nc.scalar.dma_start(bias[:], b1.rearrange("(b p t) -> p b t", p=P, t=PACK))
-            with nc.allow_non_contiguous_dma(reason="one discount a partition"):
-                nc.scalar.dma_start(discount[:], disc.rearrange("(i p) -> p i", p=P))
+            identity = keep.tile([P, P], F32, name="identity", tag="least_2_0", align_bytes=64)
+            make_identity(nc, identity[:])
+            nc.scalar.dma_start(bias_rows[0:H_PASSES, :], b1.rearrange("(b c) -> b c", b=H_PASSES))
+            nc.scalar.dma_start(disc_rows[0:N_TILES, :], disc.rearrange("(i p) -> i p", i=N_TILES))
+            turned = psum.tile([P, PACK, P], F32, name="bank")
+            for t in range(PACK):
+                nc.tensor.transpose(turned[:, t, :], bias_rows[:, t:PASS:PACK], identity[:])
+            nc.scalar.copy(bias[:], turned[:, :, 0:H_PASSES])
+            turned = psum.tile([P, P], F32, name="bank")
+            nc.tensor.transpose(turned[:], disc_rows[:], identity[:])
+            nc.scalar.copy(discount[:], turned[:, 0:N_TILES])
 
         def load_qb(b):
             qb_raw[b] = keep.tile([P, PACK, N], F32, name="qb_raw_%d" % b)
@@ -156,7 +169,7 @@ def tile_list_twin_critic_targets_kernel(
         def relu_out(b, u):
             h_rows[b, u] = keep.tile([P, PACK, COLS], BF16, name="h_rows_%d_%d" % (b, u), align_bytes=64)
             for t in range(PACK):
-                nc.scalar.activation(h_rows[b, u][:, t, :], banks[b, u, t][:], RELU, bias=bias[:, b, t : t + 1])
+                nc.scalar.activation(h_rows[b, u][:, t, :], banks[b, u, t][:], RELU, bias=bias[:, t, b : b + 1])
 
         def interleave_views(grouped, rows, run):
             dst = grouped.rearrange("p (c i t) -> p c t i", i=run, t=PACK)
@@ -219,7 +232,7 @@ def tile_list_twin_critic_targets_kernel(
             yb = critic(qb_weights, i, u)
             ya_sb = ring.tile([P, COLS], F32, name="ya_sb")
             nc.scalar.copy(ya_sb[:], ya[:])
-            least[i, u] = keep.tile([P, COLS], F32, name="least_%d_%d" % (i, u), align_bytes=64)
+            least[i, u] = keep.tile([P, COLS], F32, name="least", tag="least_%d_%d" % (i, u), align_bytes=64)
             nc.vector.tensor_tensor(least[i, u][:], yb[:], ya_sb[:], ALU.min)
 
         def finish(i, u):

@@ -151,8 +151,8 @@ def tile_list_twin_critic_targets_kernel(
             w_sc[a, b] = keep.tile([P, PASS], U8, name="w_sc_%d_%d" % (a, b), align_bytes=64)
             nc.vector.quantize_mx(out=w_codes[a, b][:].bitcast(FP8X4), scales=w_sc[a, b][:], in_=w_bf[a, b][:])
 
-        def hidden_pass(a, b, u):
-            for t in range(PACK):
+        def hidden_pass(a, b, u, slots=range(PACK), closing=LAST):
+            for t in slots:
                 if a == 0:
                     banks[b, u, t] = psum.tile([P, COLS], F32, name="bank")
                 cols = slice(t * P, (t + 1) * P)
@@ -163,7 +163,7 @@ def tile_list_twin_critic_targets_kernel(
                     rhs=v_codes[a][:, half(u)].bitcast(FP8X4),
                     rhs_scale=v_sc[SCALE_ROWS * a : P, half(u)],
                     start=(a == 0),
-                    stop=(a == LAST),
+                    stop=(a == closing),
                 )
 
         def relu_out(b, u):
@@ -185,15 +185,25 @@ def tile_list_twin_critic_targets_kernel(
             h_sc[b, u] = keep.tile([P, COLS], U8, name="h_sc_%d_%d" % (b, u), align_bytes=64)
             nc.vector.quantize_mx(out=h_codes[b, u][:].bitcast(FP8X4), scales=h_sc[b, u][:], in_=h_bf[b, u][:])
 
+        def interleave_part(b, u, n, copy, tag):
+            part = keep.tile([P, COLS * PACK // 2], BF16, name="h_part", tag=tag, align_bytes=64)
+            cols = slice(n * COLS // 2, (n + 1) * COLS // 2)
+            copy(*interleave_views(part[:], h_rows[b, u][:, :, cols], RUN_BF16))
+            return part, cols
+
+        def quantize_parts(b, u, parts):
+            h_codes[b, u] = keep.tile([P, COLS], U32, name="h_codes", tag="h_codes_%d_%d" % (b, u), align_bytes=64)
+            h_sc[b, u] = keep.tile([P, COLS], U8, name="h_sc_%d_%d" % (b, u), align_bytes=64)
+            for part, cols in parts:
+                nc.vector.quantize_mx(out=h_codes[b, u][:, cols].bitcast(FP8X4), scales=h_sc[b, u][:, cols], in_=part[:])
+
         qb_codes = keep.tile([P, H_PASSES * N], U32, name="qb_codes", align_bytes=64)
         qb_sc = keep.tile([P, H_PASSES * N], U8, name="qb_sc", align_bytes=64)
 
         def round_qb():
             qb_bf = keep.tile([P, H_PASSES * N * PACK], BF16, name="qb_bf", tag="w_raw_2_1_1", align_bytes=64)
             dst, src = interleave_views(qb_bf[:, 0 : N * PACK], qb_raw[0][:], RUN_F32)
-            cut = QB_SCALAR_COLS // RUN_F32
-            nc.scalar.copy(dst[:, 0:cut], src[:, 0:cut])
-            nc.vector.tensor_copy(dst[:, cut : N // RUN_F32], src[:, cut : N // RUN_F32])
+            nc.vector.tensor_copy(dst, src)
             nc.vector.tensor_copy(*interleave_views(qb_bf[:, N * PACK : 2 * N * PACK], qb_raw[1][:], RUN_F32))
             return qb_bf
 
@@ -210,30 +220,29 @@ def tile_list_twin_critic_targets_kernel(
             cols = slice(b * N + i * P, b * N + (i + 1) * P)
             return qb_codes[:, cols].bitcast(FP8X4), qb_sc[:, cols]
 
-        def critic(weights, i, u):
-            y = psum.tile([P, COLS], F32, name="bank")
-            for b in range(H_PASSES):
-                codes, scales = weights(i, b)
-                nc.tensor.matmul_mx(
-                    out=y[:],
-                    lhsT=codes,
-                    lhsT_scale=scales,
-                    rhs=h_codes[b, u][:].bitcast(FP8X4),
-                    rhs_scale=h_sc[b, u][:],
-                    start=(b == 0),
-                    stop=(b == H_PASSES - 1),
-                )
-            return y
+        sums, least = {}, {}
 
-        least = {}
+        def critic_passes(b, u):
+            for i in range(N_TILES):
+                for name, weights in (("a", qa_weights), ("b", qb_weights)):
+                    if b == 0:
+                        sums[name, i, u] = psum.tile([P, COLS], F32, name="bank")
+                    codes, scales = weights(i, b)
+                    nc.tensor.matmul_mx(
+                        out=sums[name, i, u][:],
+                        lhsT=codes,
+                        lhsT_scale=scales,
+                        rhs=h_codes[b, u][:].bitcast(FP8X4),
+                        rhs_scale=h_sc[b, u][:],
+                        start=(b == 0),
+                        stop=(b == H_PASSES - 1),
+                    )
 
         def smaller_critic(i, u):
-            ya = critic(qa_weights, i, u)
-            yb = critic(qb_weights, i, u)
-            ya_sb = ring.tile([P, COLS], F32, name="ya_sb")
-            nc.scalar.copy(ya_sb[:], ya[:])
+            ya_sb = keep.tile([P, COLS], F32, name="ya_sb", tag="ya_sb_%d" % i if u == 1 or i > 0 else "ya_first", align_bytes=64)
+            nc.scalar.copy(ya_sb[:], sums["a", i, u][:])
             least[i, u] = keep.tile([P, COLS], F32, name="least", tag="least_%d_%d" % (i, u), align_bytes=64)
-            nc.vector.tensor_tensor(least[i, u][:], yb[:], ya_sb[:], ALU.min)
+            nc.vector.tensor_tensor(least[i, u][:], sums["b", i, u][:], ya_sb[:], ALU.min)
 
         def finish(i, u):
             scaled = ring.tile([P, COLS], F32, name="scaled", bufs=N_TILES * HALVES)
@@ -263,7 +272,7 @@ def tile_list_twin_critic_targets_kernel(
         gather_words(0)
         round_w(0, 0, [on_scalar])
         gather_scales()
-        round_w(1, 0, [on_vector, on_scalar])
+        round_w(1, 0, [on_scalar])
         quantize_w(0, 0)
         quantize_w(1, 0)
         gather_words(1)
@@ -282,30 +291,39 @@ def tile_list_twin_critic_targets_kernel(
             round_w(a, 1, [on_vector])
             quantize_w(a, 1)
         round_w(LAST, 1, [on_vector, on_vector])
+        early = [interleave_part(0, 1, 0, on_vector, "w_raw_2_1_0")]
         quantize_w(LAST, 1)
         nc.scalar.copy(*h_views(0, 0, "h_bf_0_0"))
-        for u in range(HALVES):
-            for a in range(K_PASSES):
-                hidden_pass(a, 1, u)
+        for a in range(K_PASSES):
+            hidden_pass(a, 1, 0)
+        hidden_pass(0, 1, 1, closing=1)
+        for t in range(PACK):
+            for a in (LAST, 1):
+                hidden_pass(a, 1, 1, [t], closing=1)
+        qb_bf = round_qb()
         for u in range(HALVES):
             relu_out(1, u)
 
         quantize_h(0, 0, "w_bf_last")
-        qb_bf = round_qb()
-        nc.vector.tensor_copy(*h_views(1, 0, "h_bf_vector"))
         quantize_qb(qb_bf, 0, QB_FIRST)
-        quantize_h(1, 0, "h_codes_1_0")
+        nc.vector.tensor_copy(*h_views(1, 0, "h_bf_vector"))
         quantize_qb(qb_bf, QB_FIRST, H_PASSES * N)
+        quantize_h(1, 0, "h_codes_1_0")
+        early.append(interleave_part(0, 1, 1, on_vector, "w_raw_2_1_1"))
+        quantize_parts(0, 1, early)
+        for b in range(H_PASSES):
+            critic_passes(b, 0)
 
-        nc.vector.tensor_copy(*h_views(0, 1, "h_bf_vector"))
-        nc.scalar.copy(*h_views(1, 1, "h_bf_1_1"))
-
+        parts = [interleave_part(1, 1, 0, on_scalar, "h_part_0")]
         for i in range(N_TILES):
             smaller_critic(i, 0)
-        for b in range(H_PASSES):
-            quantize_h(b, 1, "h_codes_%d_1" % b)
-        for i in range(N_TILES):
+        finish(0, 0)
+        parts.append(interleave_part(1, 1, 1, on_scalar, "ya_first"))
+        quantize_parts(1, 1, parts)
+        for i in range(1, N_TILES):
             finish(i, 0)
+        for b in range(H_PASSES):
+            critic_passes(b, 1)
         for i in range(N_TILES):
             smaller_critic(i, 1)
         for i in range(N_TILES):

@@ -191,11 +191,11 @@ def tile_list_twin_critic_targets_kernel(
             copy(*interleave_views(part[:], h_rows[b, u][:, :, cols], RUN_BF16))
             return part, cols
 
-        def quantize_parts(b, u, parts):
-            h_codes[b, u] = keep.tile([P, COLS], U32, name="h_codes", tag="h_codes_%d_%d" % (b, u), align_bytes=64)
-            h_sc[b, u] = keep.tile([P, COLS], U8, name="h_sc_%d_%d" % (b, u), align_bytes=64)
-            for part, cols in parts:
-                nc.vector.quantize_mx(out=h_codes[b, u][:, cols].bitcast(FP8X4), scales=h_sc[b, u][:, cols], in_=part[:])
+        def quantize_part(b, u, part, cols):
+            if (b, u) not in h_codes:
+                h_codes[b, u] = keep.tile([P, COLS], U32, name="h_codes", tag="h_codes_%d_%d" % (b, u), align_bytes=64)
+                h_sc[b, u] = keep.tile([P, COLS], U8, name="h_sc_%d_%d" % (b, u), align_bytes=64)
+            nc.vector.quantize_mx(out=h_codes[b, u][:, cols].bitcast(FP8X4), scales=h_sc[b, u][:, cols], in_=part[:])
 
         qb_codes = keep.tile([P, H_PASSES * N], U32, name="qb_codes", align_bytes=64)
         qb_sc = keep.tile([P, H_PASSES * N], U8, name="qb_sc", align_bytes=64)
@@ -203,7 +203,9 @@ def tile_list_twin_critic_targets_kernel(
         def round_qb():
             qb_bf = keep.tile([P, H_PASSES * N * PACK], BF16, name="qb_bf", tag="w_raw_2_1_1", align_bytes=64)
             dst, src = interleave_views(qb_bf[:, 0 : N * PACK], qb_raw[0][:], RUN_F32)
-            nc.vector.tensor_copy(dst, src)
+            cut = QB_SCALAR_COLS // RUN_F32
+            nc.scalar.copy(dst[:, 0:cut], src[:, 0:cut])
+            nc.vector.tensor_copy(dst[:, cut : N // RUN_F32], src[:, cut : N // RUN_F32])
             nc.vector.tensor_copy(*interleave_views(qb_bf[:, N * PACK : 2 * N * PACK], qb_raw[1][:], RUN_F32))
             return qb_bf
 
@@ -291,7 +293,7 @@ def tile_list_twin_critic_targets_kernel(
             round_w(a, 1, [on_vector])
             quantize_w(a, 1)
         round_w(LAST, 1, [on_vector, on_vector])
-        early = [interleave_part(0, 1, 0, on_vector, "w_raw_2_1_0")]
+        early = interleave_part(0, 1, 0, on_vector, "w_raw_2_1_0")
         quantize_w(LAST, 1)
         nc.scalar.copy(*h_views(0, 0, "h_bf_0_0"))
         for a in range(K_PASSES):
@@ -305,21 +307,21 @@ def tile_list_twin_critic_targets_kernel(
             relu_out(1, u)
 
         quantize_h(0, 0, "w_bf_last")
+        quantize_part(0, 1, *early)
         quantize_qb(qb_bf, 0, QB_FIRST)
         nc.vector.tensor_copy(*h_views(1, 0, "h_bf_vector"))
         quantize_qb(qb_bf, QB_FIRST, H_PASSES * N)
         quantize_h(1, 0, "h_codes_1_0")
-        early.append(interleave_part(0, 1, 1, on_vector, "w_raw_2_1_1"))
-        quantize_parts(0, 1, early)
+        late = interleave_part(0, 1, 1, on_vector, "w_raw_2_1_1")
         for b in range(H_PASSES):
             critic_passes(b, 0)
 
-        parts = [interleave_part(1, 1, 0, on_scalar, "h_part_0")]
+        quantize_part(1, 1, *interleave_part(1, 1, 0, on_scalar, "h_part_0"))
+        quantize_part(0, 1, *late)
         for i in range(N_TILES):
             smaller_critic(i, 0)
         finish(0, 0)
-        parts.append(interleave_part(1, 1, 1, on_scalar, "ya_first"))
-        quantize_parts(1, 1, parts)
+        quantize_part(1, 1, *interleave_part(1, 1, 1, on_scalar, "ya_first"))
         for i in range(1, N_TILES):
             finish(i, 0)
         for b in range(H_PASSES):

@@ -246,12 +246,16 @@ def tile_list_twin_critic_targets_kernel(
             least[i, u] = keep.tile([P, COLS], F32, name="least", tag="least_%d_%d" % (i, u), align_bytes=64)
             nc.vector.tensor_tensor(least[i, u][:], sums["b", i, u][:], ya_sb[:], ALU.min)
 
-        def finish(i, u):
+        def finish(i, u, pieces=1):
             scaled = ring.tile([P, COLS], F32, name="scaled", bufs=N_TILES * HALVES)
             nc.scalar.activation(scaled[:], least[i, u][:], COPY, scale=discount[:, i : i + 1])
-            target = ring.tile([P, COLS], F32, name="target", bufs=4)
-            nc.vector.tensor_tensor(target[:], rewards[i][:].indirect(picks(u, u + 1)), scaled[:], ALU.add)
-            nc.sync.dma_start(out[i * P : (i + 1) * P, half(u)], target[:])
+            width = COLS // pieces
+            for n in range(pieces):
+                first = u * COLS + n * width
+                picked = rewards[i][:].indirect(offsets[:, first // 16 : (first + width) // 16])
+                target = ring.tile([P, width], F32, name="target", bufs=4)
+                nc.vector.tensor_tensor(target[:], picked, scaled[:, n * width : (n + 1) * width], ALU.add)
+                nc.sync.dma_start(out[i * P : (i + 1) * P, first : first + width], target[:])
 
         load_tab(0)
         load_tab_scales()
@@ -322,11 +326,14 @@ def tile_list_twin_critic_targets_kernel(
             smaller_critic(i, 0)
         finish(0, 0)
         quantize_part(1, 1, *interleave_part(1, 1, 1, on_scalar, "ya_first"))
-        for i in range(1, N_TILES):
+        last = N_TILES - 1
+        for i in range(1, last):
             finish(i, 0)
         for b in range(H_PASSES):
             critic_passes(b, 1)
         for i in range(N_TILES):
             smaller_critic(i, 1)
-        for i in range(N_TILES):
+        for i in range(last):
             finish(i, 1)
+        finish(last, 0)
+        finish(last, 1, 2)

@@ -34,7 +34,7 @@ RUN_F32 = 4
 RUN_BF16 = 8
 PSUM_BANKS = 8
 QB_FIRST = 512
-QB_SCALAR_COLS = 192
+QB_SCALAR_COLS = 128
 
 
 def tile_list_twin_critic_targets_kernel(
@@ -99,7 +99,7 @@ def tile_list_twin_critic_targets_kernel(
             nc.scalar.copy(discount[:], turned[:, 0:N_TILES])
 
         def load_qb(b):
-            qb_raw[b] = keep.tile([P, PACK, N], F32, name="qb_raw_%d" % b)
+            qb_raw[b] = keep.tile([P, PACK, N], F32, name="qb_raw", tag="qb_raw_%d" % b, align_bytes=64)
             nc.sync.dma_start(qb_raw[b][:], qb[b * PASS : (b + 1) * PASS, :].rearrange("(p t) n -> p t n", t=PACK))
 
         def load_qa():
@@ -146,10 +146,14 @@ def tile_list_twin_critic_targets_kernel(
                 src = w_raw[a, b][piece][:].rearrange("p j (m t) -> p m j t", t=PACK)
                 copy(dst[:, n * share : (n + 1) * share], src[:, first : first + share])
 
-        def quantize_w(a, b):
+        def quantize_w(a, b, calls=1):
             w_codes[a, b] = keep.tile([P, PASS], U32, name="w_codes_%d_%d" % (a, b), align_bytes=64)
             w_sc[a, b] = keep.tile([P, PASS], U8, name="w_sc_%d_%d" % (a, b), align_bytes=64)
-            nc.vector.quantize_mx(out=w_codes[a, b][:].bitcast(FP8X4), scales=w_sc[a, b][:], in_=w_bf[a, b][:])
+            width = PASS // calls
+            for first in range(0, PASS, width):
+                cols = slice(first, first + width)
+                values = w_bf[a, b][:, first * PACK : (first + width) * PACK]
+                nc.vector.quantize_mx(out=w_codes[a, b][:, cols].bitcast(FP8X4), scales=w_sc[a, b][:, cols], in_=values)
 
         def hidden_pass(a, b, u, slots=range(PACK), closing=LAST):
             for t in slots:
@@ -201,12 +205,8 @@ def tile_list_twin_critic_targets_kernel(
         qb_sc = keep.tile([P, H_PASSES * N], U8, name="qb_sc", align_bytes=64)
 
         def round_qb():
-            qb_bf = keep.tile([P, H_PASSES * N * PACK], BF16, name="qb_bf", tag="w_raw_2_1_1", align_bytes=64)
-            dst, src = interleave_views(qb_bf[:, 0 : N * PACK], qb_raw[0][:], RUN_F32)
-            cut = QB_SCALAR_COLS // RUN_F32
-            nc.scalar.copy(dst[:, 0:cut], src[:, 0:cut])
-            nc.vector.tensor_copy(dst[:, cut : N // RUN_F32], src[:, cut : N // RUN_F32])
-            nc.vector.tensor_copy(*interleave_views(qb_bf[:, N * PACK : 2 * N * PACK], qb_raw[1][:], RUN_F32))
+            qb_bf = keep.tile([P, H_PASSES * N * PACK], BF16, name="qb_bf", tag="w_raw_1_1_0", align_bytes=64)
+            nc.vector.tensor_copy(*interleave_views(qb_bf[:, 0 : N * PACK], qb_raw[0][:], RUN_F32))
             return qb_bf
 
         def quantize_qb(qb_bf, lo, hi):
@@ -224,21 +224,24 @@ def tile_list_twin_critic_targets_kernel(
 
         sums, least = {}, {}
 
-        def critic_passes(b, u):
+        def critic_passes(b, u, lo=0, hi=COLS):
             for i in range(N_TILES):
                 for name, weights in (("a", qa_weights), ("b", qb_weights)):
                     if b == 0:
                         sums[name, i, u] = psum.tile([P, COLS], F32, name="bank")
                     codes, scales = weights(i, b)
-                    nc.tensor.matmul_mx(
-                        out=sums[name, i, u][:],
-                        lhsT=codes,
-                        lhsT_scale=scales,
-                        rhs=h_codes[b, u][:].bitcast(FP8X4),
-                        rhs_scale=h_sc[b, u][:],
-                        start=(b == 0),
-                        stop=(b == H_PASSES - 1),
-                    )
+                    width = P if name == "a" and hi - lo < COLS else hi - lo
+                    for first in range(lo, hi, width):
+                        cols = slice(first, first + width)
+                        nc.tensor.matmul_mx(
+                            out=sums[name, i, u][:, cols],
+                            lhsT=codes,
+                            lhsT_scale=scales,
+                            rhs=h_codes[b, u][:, cols].bitcast(FP8X4),
+                            rhs_scale=h_sc[b, u][:, cols],
+                            start=(b == 0),
+                            stop=(b == H_PASSES - 1 and first + width == COLS),
+                        )
 
         def smaller_critic(i, u):
             ya_sb = keep.tile([P, COLS], F32, name="ya_sb", tag="ya_sb_%d" % i if u == 1 or i > 0 else "ya_first", align_bytes=64)
@@ -297,8 +300,7 @@ def tile_list_twin_critic_targets_kernel(
             round_w(a, 1, [on_vector])
             quantize_w(a, 1)
         round_w(LAST, 1, [on_vector, on_vector])
-        early = interleave_part(0, 1, 0, on_vector, "w_raw_2_1_0")
-        quantize_w(LAST, 1)
+        quantize_w(LAST, 1, 2)
         nc.scalar.copy(*h_views(0, 0, "h_bf_0_0"))
         for a in range(K_PASSES):
             hidden_pass(a, 1, 0)
@@ -310,30 +312,31 @@ def tile_list_twin_critic_targets_kernel(
         for u in range(HALVES):
             relu_out(1, u)
 
-        quantize_h(0, 0, "w_bf_last")
-        quantize_part(0, 1, *early)
-        quantize_qb(qb_bf, 0, QB_FIRST)
+        quantize_h(0, 0, "qb_raw_0")
+        quantize_qb(qb_bf, 0, 256)
+        nc.vector.tensor_copy(*interleave_views(qb_bf[:, N * PACK : 2 * N * PACK], qb_raw[1][:], RUN_F32))
         nc.vector.tensor_copy(*h_views(1, 0, "h_bf_vector"))
-        quantize_qb(qb_bf, QB_FIRST, H_PASSES * N)
+        quantize_qb(qb_bf, 256, 512)
         quantize_h(1, 0, "h_codes_1_0")
-        late = interleave_part(0, 1, 1, on_vector, "w_raw_2_1_1")
+        quantize_qb(qb_bf, 512, 768)
+        nc.vector.tensor_copy(*h_views(0, 1, "h_bf_vector"))
         for b in range(H_PASSES):
             critic_passes(b, 0)
 
-        quantize_part(1, 1, *interleave_part(1, 1, 0, on_scalar, "h_part_0"))
-        quantize_part(0, 1, *late)
-        for i in range(N_TILES):
-            smaller_critic(i, 0)
-        finish(0, 0)
-        quantize_part(1, 1, *interleave_part(1, 1, 1, on_scalar, "ya_first"))
+        smaller_critic(0, 0)
+        smaller_critic(1, 0)
+        quantize_h(0, 1, "ya_first")
+        smaller_critic(2, 0)
         last = N_TILES - 1
-        for i in range(1, last):
-            finish(i, 0)
-        for b in range(H_PASSES):
-            critic_passes(b, 1)
-        for i in range(N_TILES):
-            smaller_critic(i, 1)
+        critic_passes(0, 1)
         for i in range(last):
-            finish(i, 1)
+            finish(i, 0)
+            quantize_part(1, 1, *interleave_part(1, 1, i, on_scalar, "ya_sb_%d" % (i + 1)))
+            critic_passes(1, 1, i * COLS // 2, (i + 1) * COLS // 2)
         finish(last, 0)
+        smaller_critic(0, 1)
+        smaller_critic(1, 1)
+        finish(0, 1)
+        smaller_critic(last, 1)
+        finish(1, 1)
         finish(last, 1, 2)

@@ -138,12 +138,12 @@ def tile_list_twin_critic_targets_kernel(
                 w_bf[a, b] = keep.tile([P, PACK * PASS], BF16, name="w_bf_last", tag="w_bf_last", align_bytes=64)
             else:
                 w_bf[a, b] = ring.tile([P, PACK * PASS], BF16, name="w_bf", align_bytes=64)
-            dst = w_bf[a, b][:].rearrange("p (t m j) -> p m j t", t=PACK, j=PACK)
+            dst = w_bf[a, b][:].rearrange("p (s e m j) -> p m s j e", s=2, e=2, j=PACK)
             share = P // len(copies)
             per_piece = P // len(w_raw[a, b])
             for n, copy in enumerate(copies):
                 piece, first = divmod(n * share, per_piece)
-                src = w_raw[a, b][piece][:].rearrange("p j (m t) -> p m j t", t=PACK)
+                src = w_raw[a, b][piece][:].rearrange("p j (m s e) -> p m s j e", s=2, e=2)
                 copy(dst[:, n * share : (n + 1) * share], src[:, first : first + share])
 
         def quantize_w(a, b, calls=1):
@@ -176,8 +176,8 @@ def tile_list_twin_critic_targets_kernel(
                 nc.scalar.activation(h_rows[b, u][:, t, :], banks[b, u, t][:], RELU, bias=bias[:, t, b : b + 1])
 
         def interleave_views(grouped, rows, run):
-            dst = grouped.rearrange("p (c i t) -> p c t i", i=run, t=PACK)
-            src = rows.rearrange("p t (c i) -> p c t i", i=run)
+            dst = grouped.rearrange("p (c i s e) -> p c s i e", i=run, s=2, e=2)
+            src = rows.rearrange("p (s e) (c i) -> p c s i e", i=run, e=2)
             return dst, src
 
         def h_views(b, u, tag):
@@ -224,9 +224,10 @@ def tile_list_twin_critic_targets_kernel(
 
         sums, least = {}, {}
 
-        def critic_passes(b, u, lo=0, hi=COLS):
-            for i in range(N_TILES):
-                for name, weights in (("a", qa_weights), ("b", qb_weights)):
+        def critic_passes(b, u, lo=0, hi=COLS, names="ab", tiles=range(N_TILES)):
+            for i in tiles:
+                for name in names:
+                    weights = qa_weights if name == "a" else qb_weights
                     if b == 0:
                         sums[name, i, u] = psum.tile([P, COLS], F32, name="bank")
                     codes, scales = weights(i, b)
@@ -249,16 +250,17 @@ def tile_list_twin_critic_targets_kernel(
             least[i, u] = keep.tile([P, COLS], F32, name="least", tag="least_%d_%d" % (i, u), align_bytes=64)
             nc.vector.tensor_tensor(least[i, u][:], sums["b", i, u][:], ya_sb[:], ALU.min)
 
-        def finish(i, u, pieces=1):
+        def finish(i, u, widths=(COLS,)):
             scaled = ring.tile([P, COLS], F32, name="scaled", bufs=N_TILES * HALVES)
             nc.scalar.activation(scaled[:], least[i, u][:], COPY, scale=discount[:, i : i + 1])
-            width = COLS // pieces
-            for n in range(pieces):
-                first = u * COLS + n * width
+            start = 0
+            for width in widths:
+                first = u * COLS + start
                 picked = rewards[i][:].indirect(offsets[:, first // 16 : (first + width) // 16])
                 target = ring.tile([P, width], F32, name="target", bufs=4)
-                nc.vector.tensor_tensor(target[:], picked, scaled[:, n * width : (n + 1) * width], ALU.add)
+                nc.vector.tensor_tensor(target[:], picked, scaled[:, start : start + width], ALU.add)
                 nc.sync.dma_start(out[i * P : (i + 1) * P, first : first + width], target[:])
+                start = start + width
 
         load_tab(0)
         load_tab_scales()
@@ -315,15 +317,24 @@ def tile_list_twin_critic_targets_kernel(
         quantize_h(0, 0, "qb_raw_0")
         quantize_qb(qb_bf, 0, 256)
         nc.vector.tensor_copy(*interleave_views(qb_bf[:, N * PACK : 2 * N * PACK], qb_raw[1][:], RUN_F32))
-        nc.vector.tensor_copy(*h_views(1, 0, "h_bf_vector"))
+        parts = [interleave_part(1, 0, n, on_vector, "h_part_%d" % n) for n in range(2)]
+        critic_passes(0, 0, tiles=range(2))
+        critic_passes(0, 0, names="a", tiles=[2])
+        for part in parts:
+            quantize_part(1, 0, *part)
+        for n in range(2):
+            critic_passes(1, 0, n * COLS // 2, (n + 1) * COLS // 2, names="a")
         quantize_qb(qb_bf, 256, 512)
-        quantize_h(1, 0, "h_codes_1_0")
+        critic_passes(1, 0, names="b", tiles=[0])
+        critic_passes(0, 0, names="b", tiles=[2])
         quantize_qb(qb_bf, 512, 768)
-        nc.vector.tensor_copy(*h_views(0, 1, "h_bf_vector"))
-        for b in range(H_PASSES):
-            critic_passes(b, 0)
+        critic_passes(1, 0, names="b", tiles=[1, 2])
+        dst, src = h_views(0, 1, "h_part_1")
+        cut = COLS // RUN_BF16 // 2
+        nc.vector.tensor_copy(dst[:, 0:cut], src[:, 0:cut])
 
         smaller_critic(0, 0)
+        nc.vector.tensor_copy(dst[:, cut : 2 * cut], src[:, cut : 2 * cut])
         smaller_critic(1, 0)
         quantize_h(0, 1, "ya_first")
         smaller_critic(2, 0)
@@ -339,4 +350,4 @@ def tile_list_twin_critic_targets_kernel(
         finish(0, 1)
         smaller_critic(last, 1)
         finish(1, 1)
-        finish(last, 1, 2)
+        finish(last, 1, (384, 128))

@@ -33,8 +33,11 @@ LIST_COLS = COLS // 16
 RUN_F32 = 4
 RUN_BF16 = 8
 PSUM_BANKS = 8
-QB_FIRST = 512
-QB_SCALAR_COLS = 128
+PARTS = 2
+PART = COLS // PARTS
+QB_CALL = 256
+H_SCALAR_COLS = 128
+LAST_PIECES = (384, 128)
 
 
 def tile_list_twin_critic_targets_kernel(
@@ -134,10 +137,7 @@ def tile_list_twin_critic_targets_kernel(
         banks, h_rows, h_bf, h_codes, h_sc = {}, {}, {}, {}, {}
 
         def round_w(a, b, copies):
-            if (a, b) == (LAST, 1):
-                w_bf[a, b] = keep.tile([P, PACK * PASS], BF16, name="w_bf_last", tag="w_bf_last", align_bytes=64)
-            else:
-                w_bf[a, b] = ring.tile([P, PACK * PASS], BF16, name="w_bf", align_bytes=64)
+            w_bf[a, b] = ring.tile([P, PACK * PASS], BF16, name="w_bf", align_bytes=64)
             dst = w_bf[a, b][:].rearrange("p (s e m j) -> p m s j e", s=2, e=2, j=PACK)
             share = P // len(copies)
             per_piece = P // len(w_raw[a, b])
@@ -189,30 +189,36 @@ def tile_list_twin_critic_targets_kernel(
             h_sc[b, u] = keep.tile([P, COLS], U8, name="h_sc_%d_%d" % (b, u), align_bytes=64)
             nc.vector.quantize_mx(out=h_codes[b, u][:].bitcast(FP8X4), scales=h_sc[b, u][:], in_=h_bf[b, u][:])
 
-        def interleave_part(b, u, n, copy, tag):
-            part = keep.tile([P, COLS * PACK // 2], BF16, name="h_part", tag=tag, align_bytes=64)
-            cols = slice(n * COLS // 2, (n + 1) * COLS // 2)
-            copy(*interleave_views(part[:], h_rows[b, u][:, :, cols], RUN_BF16))
-            return part, cols
+        def part_cols(n):
+            return slice(n * PART, (n + 1) * PART)
 
-        def quantize_part(b, u, part, cols):
-            if (b, u) not in h_codes:
-                h_codes[b, u] = keep.tile([P, COLS], U32, name="h_codes", tag="h_codes_%d_%d" % (b, u), align_bytes=64)
+        def interleave_part(b, u, n, copy, tag):
+            part = keep.tile([P, PART * PACK], BF16, name="h_part", tag=tag, align_bytes=64)
+            copy(*interleave_views(part[:], h_rows[b, u][:, :, part_cols(n)], RUN_BF16))
+            return part
+
+        def quantize_part(b, u, n, part):
+            if n == 0:
+                h_codes[b, u] = keep.tile([P, COLS], U32, name="h_codes_%d_%d" % (b, u), align_bytes=64)
                 h_sc[b, u] = keep.tile([P, COLS], U8, name="h_sc_%d_%d" % (b, u), align_bytes=64)
+            cols = part_cols(n)
             nc.vector.quantize_mx(out=h_codes[b, u][:, cols].bitcast(FP8X4), scales=h_sc[b, u][:, cols], in_=part[:])
 
         qb_codes = keep.tile([P, H_PASSES * N], U32, name="qb_codes", align_bytes=64)
         qb_sc = keep.tile([P, H_PASSES * N], U8, name="qb_sc", align_bytes=64)
 
-        def round_qb():
-            qb_bf = keep.tile([P, H_PASSES * N * PACK], BF16, name="qb_bf", tag="w_raw_1_1_0", align_bytes=64)
-            nc.vector.tensor_copy(*interleave_views(qb_bf[:, 0 : N * PACK], qb_raw[0][:], RUN_F32))
-            return qb_bf
+        qb_bf = {}
 
-        def quantize_qb(qb_bf, lo, hi):
-            nc.vector.quantize_mx(
-                out=qb_codes[:, lo:hi].bitcast(FP8X4), scales=qb_sc[:, lo:hi], in_=qb_bf[:, lo * PACK : hi * PACK]
-            )
+        def round_qb(b):
+            if b == 0:
+                qb_bf["all"] = keep.tile([P, H_PASSES * N * PACK], BF16, name="qb_bf", tag="w_raw_1_1_0", align_bytes=64)
+            grouped = qb_bf["all"][:, b * N * PACK : (b + 1) * N * PACK]
+            nc.vector.tensor_copy(*interleave_views(grouped, qb_raw[b][:], RUN_F32))
+
+        def quantize_qb(call):
+            lo, hi = call * QB_CALL, (call + 1) * QB_CALL
+            values = qb_bf["all"][:, lo * PACK : hi * PACK]
+            nc.vector.quantize_mx(out=qb_codes[:, lo:hi].bitcast(FP8X4), scales=qb_sc[:, lo:hi], in_=values)
 
         def qa_weights(i, b):
             codes = qa[:, b, :].bitcast(U8)[:, 2 * i * P : 2 * (i + 1) * P].bitcast(FP4X4)
@@ -224,15 +230,15 @@ def tile_list_twin_critic_targets_kernel(
 
         sums, least = {}, {}
 
-        def critic_passes(b, u, lo=0, hi=COLS, names="ab", tiles=range(N_TILES)):
+        def critic_passes(b, u, critics="ab", tiles=range(N_TILES), tokens=slice(0, COLS)):
+            span = tokens.stop - tokens.start
             for i in tiles:
-                for name in names:
-                    weights = qa_weights if name == "a" else qb_weights
+                for name in critics:
                     if b == 0:
                         sums[name, i, u] = psum.tile([P, COLS], F32, name="bank")
-                    codes, scales = weights(i, b)
-                    width = P if name == "a" and hi - lo < COLS else hi - lo
-                    for first in range(lo, hi, width):
+                    codes, scales = qa_weights(i, b) if name == "a" else qb_weights(i, b)
+                    width = P if name == "a" and span < COLS else span
+                    for first in range(tokens.start, tokens.stop, width):
                         cols = slice(first, first + width)
                         nc.tensor.matmul_mx(
                             out=sums[name, i, u][:, cols],
@@ -241,11 +247,11 @@ def tile_list_twin_critic_targets_kernel(
                             rhs=h_codes[b, u][:, cols].bitcast(FP8X4),
                             rhs_scale=h_sc[b, u][:, cols],
                             start=(b == 0),
-                            stop=(b == H_PASSES - 1 and first + width == COLS),
+                            stop=(b == H_PASSES - 1 and cols.stop == COLS),
                         )
 
         def smaller_critic(i, u):
-            ya_sb = keep.tile([P, COLS], F32, name="ya_sb", tag="ya_sb_%d" % i if u == 1 or i > 0 else "ya_first", align_bytes=64)
+            ya_sb = keep.tile([P, COLS], F32, name="ya_sb", tag="ya_sb_%d" % i, align_bytes=64)
             nc.scalar.copy(ya_sb[:], sums["a", i, u][:])
             least[i, u] = keep.tile([P, COLS], F32, name="least", tag="least_%d_%d" % (i, u), align_bytes=64)
             nc.vector.tensor_tensor(least[i, u][:], sums["b", i, u][:], ya_sb[:], ALU.min)
@@ -310,44 +316,45 @@ def tile_list_twin_critic_targets_kernel(
         for t in range(PACK):
             for a in (LAST, 1):
                 hidden_pass(a, 1, 1, [t], closing=1)
-        qb_bf = round_qb()
+        round_qb(0)
         for u in range(HALVES):
             relu_out(1, u)
 
-        quantize_h(0, 0, "qb_raw_0")
-        quantize_qb(qb_bf, 0, 256)
-        nc.vector.tensor_copy(*interleave_views(qb_bf[:, N * PACK : 2 * N * PACK], qb_raw[1][:], RUN_F32))
-        parts = [interleave_part(1, 0, n, on_vector, "h_part_%d" % n) for n in range(2)]
-        critic_passes(0, 0, tiles=range(2))
-        critic_passes(0, 0, names="a", tiles=[2])
-        for part in parts:
-            quantize_part(1, 0, *part)
-        for n in range(2):
-            critic_passes(1, 0, n * COLS // 2, (n + 1) * COLS // 2, names="a")
-        quantize_qb(qb_bf, 256, 512)
-        critic_passes(1, 0, names="b", tiles=[0])
-        critic_passes(0, 0, names="b", tiles=[2])
-        quantize_qb(qb_bf, 512, 768)
-        critic_passes(1, 0, names="b", tiles=[1, 2])
-        dst, src = h_views(0, 1, "h_part_1")
-        cut = COLS // RUN_BF16 // 2
-        nc.vector.tensor_copy(dst[:, 0:cut], src[:, 0:cut])
-
-        smaller_critic(0, 0)
-        nc.vector.tensor_copy(dst[:, cut : 2 * cut], src[:, cut : 2 * cut])
-        smaller_critic(1, 0)
-        quantize_h(0, 1, "ya_first")
-        smaller_critic(2, 0)
         last = N_TILES - 1
-        critic_passes(0, 1)
+        quantize_h(0, 0, "qb_raw_0")
+        quantize_qb(0)
+        round_qb(1)
+        parts = [interleave_part(1, 0, n, on_vector, "h_part_%d" % n) for n in range(PARTS)]
+        critic_passes(0, 0, tiles=range(last))
+        critic_passes(0, 0, "a", [last])
+        for n in range(PARTS):
+            quantize_part(1, 0, n, parts[n])
+        for n in range(PARTS):
+            critic_passes(1, 0, "a", tokens=part_cols(n))
+        quantize_qb(1)
+        critic_passes(1, 0, "b", [0])
+        critic_passes(0, 0, "b", [last])
+        quantize_qb(2)
+        critic_passes(1, 0, "b", range(1, N_TILES))
+
+        dst, src = h_views(0, 1, "h_part_1")
+        cut = H_SCALAR_COLS // RUN_BF16
+        nc.scalar.copy(dst[:, 0:cut], src[:, 0:cut])
+        nc.vector.tensor_copy(dst[:, cut : COLS // RUN_BF16], src[:, cut : COLS // RUN_BF16])
         for i in range(last):
-            finish(i, 0)
-            quantize_part(1, 1, *interleave_part(1, 1, i, on_scalar, "ya_sb_%d" % (i + 1)))
-            critic_passes(1, 1, i * COLS // 2, (i + 1) * COLS // 2)
+            smaller_critic(i, 0)
+        quantize_h(0, 1, "ya_sb_0")
+        smaller_critic(last, 0)
+        critic_passes(0, 1)
+
+        for n in range(PARTS):
+            finish(n, 0)
+            quantize_part(1, 1, n, interleave_part(1, 1, n, on_scalar, "ya_sb_%d" % (n + 1)))
+            critic_passes(1, 1, tokens=part_cols(n))
         finish(last, 0)
+
         smaller_critic(0, 1)
-        smaller_critic(1, 1)
-        finish(0, 1)
-        smaller_critic(last, 1)
-        finish(1, 1)
-        finish(last, 1, (384, 128))
+        for i in range(1, N_TILES):
+            smaller_critic(i, 1)
+            finish(i - 1, 1)
+        finish(last, 1, LAST_PIECES)

@@ -33,6 +33,7 @@ LIST_COLS = COLS // 16
 RUN_F32 = 4
 RUN_BF16 = 8
 PSUM_BANKS = 8
+ALIGN = 256
 PARTS = 2
 PART = COLS // PARTS
 QB_CALL = 256
@@ -52,17 +53,17 @@ def tile_list_twin_critic_targets_kernel(
         offsets = keep.tile([P, S // 16], U16, name="offsets")
         nc.sync.dma_start(offsets[:], offs)
 
-        tab_sc = keep.tile([P, T // 4], I32, name="tab_sc", align_bytes=64)
-        qa_sc = keep.tile([P, H_PASSES, N // 4], I32, name="qa_sc", align_bytes=64)
+        tab_sc = keep.tile([P, T // 4], I32, name="tab_sc", align_bytes=ALIGN)
+        qa_sc = keep.tile([P, H_PASSES, N // 4], I32, name="qa_sc", align_bytes=ALIGN)
         nc.vector.memset(tab_sc[:], 0)
-        bias_rows = keep.tile([P, PASS], F32, name="bias_rows", tag="least_0_0", align_bytes=64)
-        disc_rows = keep.tile([P, P], F32, name="disc_rows", tag="least_1_0", align_bytes=64)
+        bias_rows = keep.tile([P, PASS], F32, name="bias_rows", tag="least_0_0", align_bytes=ALIGN)
+        disc_rows = keep.tile([P, P], F32, name="disc_rows", tag="least_1_0", align_bytes=ALIGN)
         nc.vector.memset(bias_rows[:], 0.0)
         nc.vector.memset(disc_rows[:], 0.0)
         nc.vector.memset(qa_sc[:], 0)
         bias = keep.tile([P, PACK, H_PASSES], F32, name="bias")
         discount = keep.tile([P, N_TILES], F32, name="discount")
-        qa = keep.tile([P, H_PASSES, N // 2], I32, name="qa", align_bytes=64)
+        qa = keep.tile([P, H_PASSES, N // 2], I32, name="qa", align_bytes=ALIGN)
 
         w_raw, tab, qb_raw, rewards = {}, {}, {}, {}
 
@@ -71,13 +72,13 @@ def tile_list_twin_critic_targets_kernel(
             w_raw[a, b] = []
             for n in range(pieces):
                 tag = "w_raw_%d_%d_%d" % (a, b, n)
-                piece = keep.tile([P, PACK, width], F32, name="w_raw", tag=tag, align_bytes=64)
+                piece = keep.tile([P, PACK, width], F32, name="w_raw", tag=tag, align_bytes=ALIGN)
                 rows = w1[a * PASS : (a + 1) * PASS, b * PASS + n * width : b * PASS + (n + 1) * width]
                 nc.sync.dma_start(piece[:], rows.rearrange("(p j) c -> p j c", j=PACK))
                 w_raw[a, b].append(piece)
 
         def load_tab(a):
-            tab[a] = keep.tile([P, T], I32, name="tab_%d" % a, align_bytes=64)
+            tab[a] = keep.tile([P, T], I32, name="tab_%d" % a, align_bytes=ALIGN)
             nc.sync.dma_start(tab[a][:], tab_words[a].rearrange("p t i -> p (t i)").bitcast(I32))
 
         def load_tab_scales():
@@ -89,7 +90,7 @@ def tile_list_twin_critic_targets_kernel(
                 )
 
         def load_bias_and_discount():
-            identity = keep.tile([P, P], F32, name="identity", tag="least_2_0", align_bytes=64)
+            identity = keep.tile([P, P], F32, name="identity", tag="least_2_0", align_bytes=ALIGN)
             make_identity(nc, identity[:])
             nc.scalar.dma_start(bias_rows[0:H_PASSES, :], b1.rearrange("(b c) -> b c", b=H_PASSES))
             nc.scalar.dma_start(disc_rows[0:N_TILES, :], disc.rearrange("(i p) -> i p", i=N_TILES))
@@ -102,7 +103,7 @@ def tile_list_twin_critic_targets_kernel(
             nc.scalar.copy(discount[:], turned[:, 0:N_TILES])
 
         def load_qb(b):
-            qb_raw[b] = keep.tile([P, PACK, N], F32, name="qb_raw", tag="qb_raw_%d" % b, align_bytes=64)
+            qb_raw[b] = keep.tile([P, PACK, N], F32, name="qb_raw", tag="qb_raw_%d" % b, align_bytes=ALIGN)
             nc.sync.dma_start(qb_raw[b][:], qb[b * PASS : (b + 1) * PASS, :].rearrange("(p t) n -> p t n", t=PACK))
 
         def load_qa():
@@ -114,11 +115,11 @@ def tile_list_twin_critic_targets_kernel(
                 )
 
         def load_rewards(i):
-            rewards[i] = keep.tile([P, T], F32, name="rewards_%d" % i, align_bytes=64)
+            rewards[i] = keep.tile([P, T], F32, name="rewards_%d" % i, align_bytes=ALIGN)
             nc.sync.dma_start(rewards[i][:], gT[i * P : (i + 1) * P, :])
 
-        v_sc = keep.tile([P, S], U8, name="v_sc", align_bytes=64)
-        v_codes = [keep.tile([P, S], U32, name="v_codes_%d" % a, align_bytes=64) for a in range(K_PASSES)]
+        v_sc = keep.tile([P, S], U8, name="v_sc", align_bytes=ALIGN)
+        v_codes = [keep.tile([P, S], U32, name="v_codes_%d" % a, align_bytes=ALIGN) for a in range(K_PASSES)]
 
         def picks(first, last):
             return offsets[:, first * LIST_COLS : last * LIST_COLS]
@@ -137,7 +138,7 @@ def tile_list_twin_critic_targets_kernel(
         banks, h_rows, h_bf, h_codes, h_sc = {}, {}, {}, {}, {}
 
         def round_w(a, b, copies):
-            w_bf[a, b] = ring.tile([P, PACK * PASS], BF16, name="w_bf", align_bytes=64)
+            w_bf[a, b] = ring.tile([P, PACK * PASS], BF16, name="w_bf", align_bytes=ALIGN)
             dst = w_bf[a, b][:].rearrange("p (s e m j) -> p m s j e", s=2, e=2, j=PACK)
             share = P // len(copies)
             per_piece = P // len(w_raw[a, b])
@@ -147,8 +148,8 @@ def tile_list_twin_critic_targets_kernel(
                 copy(dst[:, n * share : (n + 1) * share], src[:, first : first + share])
 
         def quantize_w(a, b, calls=1):
-            w_codes[a, b] = keep.tile([P, PASS], U32, name="w_codes_%d_%d" % (a, b), align_bytes=64)
-            w_sc[a, b] = keep.tile([P, PASS], U8, name="w_sc_%d_%d" % (a, b), align_bytes=64)
+            w_codes[a, b] = keep.tile([P, PASS], U32, name="w_codes_%d_%d" % (a, b), align_bytes=ALIGN)
+            w_sc[a, b] = keep.tile([P, PASS], U8, name="w_sc_%d_%d" % (a, b), align_bytes=ALIGN)
             width = PASS // calls
             for first in range(0, PASS, width):
                 cols = slice(first, first + width)
@@ -171,7 +172,7 @@ def tile_list_twin_critic_targets_kernel(
                 )
 
         def relu_out(b, u):
-            h_rows[b, u] = keep.tile([P, PACK, COLS], BF16, name="h_rows_%d_%d" % (b, u), align_bytes=64)
+            h_rows[b, u] = keep.tile([P, PACK, COLS], BF16, name="h_rows_%d_%d" % (b, u), align_bytes=ALIGN)
             for t in range(PACK):
                 nc.scalar.activation(h_rows[b, u][:, t, :], banks[b, u, t][:], RELU, bias=bias[:, t, b : b + 1])
 
@@ -181,37 +182,37 @@ def tile_list_twin_critic_targets_kernel(
             return dst, src
 
         def h_views(b, u, tag):
-            h_bf[b, u] = keep.tile([P, COLS * PACK], BF16, name="h_bf", tag=tag, align_bytes=64)
+            h_bf[b, u] = keep.tile([P, COLS * PACK], BF16, name="h_bf", tag=tag, align_bytes=ALIGN)
             return interleave_views(h_bf[b, u][:], h_rows[b, u][:], RUN_BF16)
 
         def quantize_h(b, u, tag):
-            h_codes[b, u] = keep.tile([P, COLS], U32, name="h_codes", tag=tag, align_bytes=64)
-            h_sc[b, u] = keep.tile([P, COLS], U8, name="h_sc_%d_%d" % (b, u), align_bytes=64)
+            h_codes[b, u] = keep.tile([P, COLS], U32, name="h_codes", tag=tag, align_bytes=ALIGN)
+            h_sc[b, u] = keep.tile([P, COLS], U8, name="h_sc_%d_%d" % (b, u), align_bytes=ALIGN)
             nc.vector.quantize_mx(out=h_codes[b, u][:].bitcast(FP8X4), scales=h_sc[b, u][:], in_=h_bf[b, u][:])
 
         def part_cols(n):
             return slice(n * PART, (n + 1) * PART)
 
         def interleave_part(b, u, n, copy, tag):
-            part = keep.tile([P, PART * PACK], BF16, name="h_part", tag=tag, align_bytes=64)
+            part = keep.tile([P, PART * PACK], BF16, name="h_part", tag=tag, align_bytes=ALIGN)
             copy(*interleave_views(part[:], h_rows[b, u][:, :, part_cols(n)], RUN_BF16))
             return part
 
         def quantize_part(b, u, n, part):
             if n == 0:
-                h_codes[b, u] = keep.tile([P, COLS], U32, name="h_codes_%d_%d" % (b, u), align_bytes=64)
-                h_sc[b, u] = keep.tile([P, COLS], U8, name="h_sc_%d_%d" % (b, u), align_bytes=64)
+                h_codes[b, u] = keep.tile([P, COLS], U32, name="h_codes_%d_%d" % (b, u), align_bytes=ALIGN)
+                h_sc[b, u] = keep.tile([P, COLS], U8, name="h_sc_%d_%d" % (b, u), align_bytes=ALIGN)
             cols = part_cols(n)
             nc.vector.quantize_mx(out=h_codes[b, u][:, cols].bitcast(FP8X4), scales=h_sc[b, u][:, cols], in_=part[:])
 
-        qb_codes = keep.tile([P, H_PASSES * N], U32, name="qb_codes", align_bytes=64)
-        qb_sc = keep.tile([P, H_PASSES * N], U8, name="qb_sc", align_bytes=64)
+        qb_codes = keep.tile([P, H_PASSES * N], U32, name="qb_codes", align_bytes=ALIGN)
+        qb_sc = keep.tile([P, H_PASSES * N], U8, name="qb_sc", align_bytes=ALIGN)
 
         qb_bf = {}
 
         def round_qb(b):
             if b == 0:
-                qb_bf["all"] = keep.tile([P, H_PASSES * N * PACK], BF16, name="qb_bf", tag="w_raw_1_1_0", align_bytes=64)
+                qb_bf["all"] = keep.tile([P, H_PASSES * N * PACK], BF16, name="qb_bf", tag="w_raw_1_1_0", align_bytes=ALIGN)
             grouped = qb_bf["all"][:, b * N * PACK : (b + 1) * N * PACK]
             nc.vector.tensor_copy(*interleave_views(grouped, qb_raw[b][:], RUN_F32))
 
@@ -251,19 +252,19 @@ def tile_list_twin_critic_targets_kernel(
                         )
 
         def smaller_critic(i, u):
-            ya_sb = keep.tile([P, COLS], F32, name="ya_sb", tag="ya_sb_%d" % i, align_bytes=64)
+            ya_sb = keep.tile([P, COLS], F32, name="ya_sb", tag="ya_sb_%d" % i, align_bytes=ALIGN)
             nc.scalar.copy(ya_sb[:], sums["a", i, u][:])
-            least[i, u] = keep.tile([P, COLS], F32, name="least", tag="least_%d_%d" % (i, u), align_bytes=64)
+            least[i, u] = keep.tile([P, COLS], F32, name="least", tag="least_%d_%d" % (i, u), align_bytes=ALIGN)
             nc.vector.tensor_tensor(least[i, u][:], sums["b", i, u][:], ya_sb[:], ALU.min)
 
         def finish(i, u, widths=(COLS,)):
-            scaled = ring.tile([P, COLS], F32, name="scaled", bufs=N_TILES * HALVES)
+            scaled = ring.tile([P, COLS], F32, name="scaled", bufs=N_TILES * HALVES, align_bytes=ALIGN)
             nc.scalar.activation(scaled[:], least[i, u][:], COPY, scale=discount[:, i : i + 1])
             start = 0
             for width in widths:
                 first = u * COLS + start
                 picked = rewards[i][:].indirect(offsets[:, first // 16 : (first + width) // 16])
-                target = ring.tile([P, width], F32, name="target", bufs=4)
+                target = ring.tile([P, width], F32, name="target", bufs=4, align_bytes=ALIGN)
                 nc.vector.tensor_tensor(target[:], picked, scaled[:, start : start + width], ALU.add)
                 nc.sync.dma_start(out[i * P : (i + 1) * P, first : first + width], target[:])
                 start = start + width

@@ -140,12 +140,13 @@ def tile_list_twin_critic_targets_kernel(
         def round_w(a, b, copies):
             w_bf[a, b] = ring.tile([P, PACK * PASS], BF16, name="w_bf", align_bytes=ALIGN)
             dst = w_bf[a, b][:].rearrange("p (s e m j) -> p m s j e", s=2, e=2, j=PACK)
-            share = P // len(copies)
             per_piece = P // len(w_raw[a, b])
-            for n, copy in enumerate(copies):
-                piece, first = divmod(n * share, per_piece)
+            start = 0
+            for copy, share in copies:
+                piece, first = divmod(start, per_piece)
                 src = w_raw[a, b][piece][:].rearrange("p j (m s e) -> p m s j e", s=2, e=2)
-                copy(dst[:, n * share : (n + 1) * share], src[:, first : first + share])
+                copy(dst[:, start : start + share], src[:, first : first + share])
+                start = start + share
 
         def quantize_w(a, b, calls=1):
             w_codes[a, b] = keep.tile([P, PASS], U32, name="w_codes_%d_%d" % (a, b), align_bytes=ALIGN)
@@ -156,9 +157,9 @@ def tile_list_twin_critic_targets_kernel(
                 values = w_bf[a, b][:, first * PACK : (first + width) * PACK]
                 nc.vector.quantize_mx(out=w_codes[a, b][:, cols].bitcast(FP8X4), scales=w_sc[a, b][:, cols], in_=values)
 
-        def hidden_pass(a, b, u, slots=range(PACK), closing=LAST):
+        def hidden_pass(a, b, u, slots=range(PACK), opening=0, closing=LAST):
             for t in slots:
-                if a == 0:
+                if a == opening:
                     banks[b, u, t] = psum.tile([P, COLS], F32, name="bank")
                 cols = slice(t * P, (t + 1) * P)
                 nc.tensor.matmul_mx(
@@ -167,7 +168,7 @@ def tile_list_twin_critic_targets_kernel(
                     lhsT_scale=w_sc[a, b][:, cols],
                     rhs=v_codes[a][:, half(u)].bitcast(FP8X4),
                     rhs_scale=v_sc[SCALE_ROWS * a : P, half(u)],
-                    start=(a == 0),
+                    start=(a == opening),
                     stop=(a == closing),
                 )
 
@@ -270,9 +271,9 @@ def tile_list_twin_critic_targets_kernel(
                 start = start + width
 
         load_tab(0)
+        load_w(0, 0)
         load_tab_scales()
         load_bias_and_discount()
-        load_w(0, 0)
         load_w(1, 0)
         load_tab(1)
         load_w(LAST, 0)
@@ -288,27 +289,29 @@ def tile_list_twin_critic_targets_kernel(
 
         on_vector, on_scalar = nc.vector.tensor_copy, nc.scalar.copy
         gather_words(0)
-        round_w(0, 0, [on_scalar])
+        round_w(0, 0, [(on_scalar, P)])
         gather_scales()
-        round_w(1, 0, [on_scalar])
+        round_w(1, 0, [(on_vector, 96), (on_scalar, 32)])
         quantize_w(0, 0)
         quantize_w(1, 0)
-        gather_words(1)
-        round_w(LAST, 0, [on_vector, on_scalar])
+        for u in range(HALVES):
+            gather_words(1, u, u + 1)
+        round_w(LAST, 0, [(on_vector, 64), (on_scalar, 64)])
         quantize_w(LAST, 0)
-        for a in range(LAST):
-            for u in range(HALVES):
-                hidden_pass(a, 0, u)
+        for a in (0, 1):
+            hidden_pass(a, 0, 0)
+        for a in (1, 0):
+            hidden_pass(a, 0, 1, opening=1)
         for u in range(HALVES):
             gather_words(LAST, u, u + 1)
         for u in range(HALVES):
-            hidden_pass(LAST, 0, u)
+            hidden_pass(LAST, 0, u, opening=u)
             relu_out(0, u)
 
         for a in range(LAST):
-            round_w(a, 1, [on_vector])
+            round_w(a, 1, [(on_vector, P)])
             quantize_w(a, 1)
-        round_w(LAST, 1, [on_vector, on_vector])
+        round_w(LAST, 1, [(on_vector, 64), (on_vector, 64)])
         quantize_w(LAST, 1, 2)
         nc.scalar.copy(*h_views(0, 0, "h_bf_0_0"))
         for a in range(K_PASSES):

@@ -30,8 +30,8 @@ N_TILES = N // P
 QUADRANTS = 4
 SCALE_ROWS = 4
 LIST_COLS = COLS // 16
-RUN_F32 = 4
-RUN_BF16 = 8
+RUN_F32 = 2
+RUN_BF16 = 2
 PSUM_BANKS = 8
 ALIGN = 256
 PARTS = 2
@@ -178,8 +178,8 @@ def tile_list_twin_critic_targets_kernel(
                 nc.scalar.activation(h_rows[b, u][:, t, :], banks[b, u, t][:], RELU, bias=bias[:, t, b : b + 1])
 
         def interleave_views(grouped, rows, run):
-            dst = grouped.rearrange("p (c i s e) -> p c s i e", i=run, s=2, e=2)
-            src = rows.rearrange("p (s e) (c i) -> p c s i e", i=run, e=2)
+            dst = grouped.rearrange("p (c i t) -> p c t i", i=run, t=PACK)
+            src = rows.rearrange("p t (c i) -> p c t i", i=run)
             return dst, src
 
         def h_views(b, u, tag):
@@ -239,7 +239,7 @@ def tile_list_twin_critic_targets_kernel(
                     if b == 0:
                         sums[name, i, u] = psum.tile([P, COLS], F32, name="bank")
                     codes, scales = qa_weights(i, b) if name == "a" else qb_weights(i, b)
-                    width = P if name == "a" and span < COLS else span
+                    width = span
                     for first in range(tokens.start, tokens.stop, width):
                         cols = slice(first, first + width)
                         nc.tensor.matmul_mx(
@@ -312,7 +312,7 @@ def tile_list_twin_critic_targets_kernel(
             round_w(a, 1, [(on_vector, P)])
             quantize_w(a, 1)
         round_w(LAST, 1, [(on_vector, 64), (on_vector, 64)])
-        quantize_w(LAST, 1, 2)
+        quantize_w(LAST, 1, PACK)
         nc.scalar.copy(*h_views(0, 0, "h_bf_0_0"))
         for a in range(K_PASSES):
             hidden_pass(a, 1, 0)

@@ -53,7 +53,7 @@ def tile_list_twin_critic_targets_kernel(
         offsets = keep.tile([P, S // 16], U16, name="offsets")
         nc.sync.dma_start(offsets[:], offs)
 
-        tab_sc = keep.tile([P, T // 4], I32, name="tab_sc", align_bytes=ALIGN)
+        tab_sc = keep.tile([P, T // 4], I32, name="tab_sc", tag="tab_sc", align_bytes=ALIGN)
         qa_sc = keep.tile([P, H_PASSES, N // 4], I32, name="qa_sc", align_bytes=ALIGN)
         nc.vector.memset(tab_sc[:], 0)
         bias_rows = keep.tile([P, PASS], F32, name="bias_rows", tag="least_0_0", align_bytes=ALIGN)
@@ -199,9 +199,9 @@ def tile_list_twin_critic_targets_kernel(
             copy(*interleave_views(part[:], h_rows[b, u][:, :, part_cols(n)], RUN_BF16))
             return part
 
-        def quantize_part(b, u, n, part):
+        def quantize_part(b, u, n, part, tag=None):
             if n == 0:
-                h_codes[b, u] = keep.tile([P, COLS], U32, name="h_codes_%d_%d" % (b, u), align_bytes=ALIGN)
+                h_codes[b, u] = keep.tile([P, COLS], U32, name="h_codes", tag=tag or "h_codes_%d_%d" % (b, u), align_bytes=ALIGN)
                 h_sc[b, u] = keep.tile([P, COLS], U8, name="h_sc_%d_%d" % (b, u), align_bytes=ALIGN)
             cols = part_cols(n)
             nc.vector.quantize_mx(out=h_codes[b, u][:, cols].bitcast(FP8X4), scales=h_sc[b, u][:, cols], in_=part[:])
@@ -236,7 +236,7 @@ def tile_list_twin_critic_targets_kernel(
             span = tokens.stop - tokens.start
             for i in tiles:
                 for name in critics:
-                    if b == 0:
+                    if b == 0 and tokens.start == 0:
                         sums[name, i, u] = psum.tile([P, COLS], F32, name="bank")
                     codes, scales = qa_weights(i, b) if name == "a" else qb_weights(i, b)
                     width = span
@@ -248,7 +248,7 @@ def tile_list_twin_critic_targets_kernel(
                             lhsT_scale=scales,
                             rhs=h_codes[b, u][:, cols].bitcast(FP8X4),
                             rhs_scale=h_sc[b, u][:, cols],
-                            start=(b == 0),
+                            start=(b == 0 and first == 0),
                             stop=(b == H_PASSES - 1 and cols.stop == COLS),
                         )
 
@@ -341,15 +341,20 @@ def tile_list_twin_critic_targets_kernel(
         quantize_qb(2)
         critic_passes(1, 0, "b", range(1, N_TILES))
 
-        dst, src = h_views(0, 1, "h_part_1")
+        head = interleave_part(0, 1, 0, on_vector, "h_part_0")
+        tail = keep.tile([P, PART * PACK], BF16, name="h_part", tag="h_part_1", align_bytes=ALIGN)
+        dst, src = interleave_views(tail[:], h_rows[0, 1][:, :, part_cols(1)], RUN_BF16)
         cut = H_SCALAR_COLS // RUN_BF16
         nc.scalar.copy(dst[:, 0:cut], src[:, 0:cut])
-        nc.vector.tensor_copy(dst[:, cut : COLS // RUN_BF16], src[:, cut : COLS // RUN_BF16])
+        nc.vector.tensor_copy(dst[:, cut : PART // RUN_BF16], src[:, cut : PART // RUN_BF16])
+        quantize_part(0, 1, 0, head, "tab_sc")
         for i in range(last):
             smaller_critic(i, 0)
-        quantize_h(0, 1, "ya_sb_0")
+        critic_passes(0, 1, tokens=part_cols(0))
+        h_codes[0, 1] = keep.tile([P, COLS], U32, name="h_codes", tag="ya_sb_0", align_bytes=ALIGN)
+        quantize_part(0, 1, 1, tail)
         smaller_critic(last, 0)
-        critic_passes(0, 1)
+        critic_passes(0, 1, tokens=part_cols(1))
 
         for n in range(PARTS):
             finish(n, 0)

@@ -83,8 +83,7 @@ def tile_list_twin_critic_targets_kernel(
 
         def load_tab_scales():
             for q in range(QUADRANTS):
-                queue = nc.sync if q % 2 == 0 else nc.scalar
-                queue.dma_start(
+                nc.sync.dma_start(
                     tab_sc[32 * q : 32 * q + SCALE_ROWS * K_PASSES, :],
                     tab_scales[:, SCALE_ROWS * q : SCALE_ROWS * (q + 1), :].bitcast(I32),
                 )
@@ -92,8 +91,8 @@ def tile_list_twin_critic_targets_kernel(
         def load_bias_and_discount():
             identity = keep.tile([P, P], F32, name="identity", tag="least_2_0", align_bytes=ALIGN)
             make_identity(nc, identity[:])
-            nc.scalar.dma_start(bias_rows[0:H_PASSES, :], b1.rearrange("(b c) -> b c", b=H_PASSES))
-            nc.scalar.dma_start(disc_rows[0:N_TILES, :], disc.rearrange("(i p) -> i p", i=N_TILES))
+            nc.sync.dma_start(bias_rows[0:H_PASSES, :], b1.rearrange("(b c) -> b c", b=H_PASSES))
+            nc.sync.dma_start(disc_rows[0:N_TILES, :], disc.rearrange("(i p) -> i p", i=N_TILES))
             turned = psum.tile([P, PACK, P], F32, name="bank")
             for t in range(PACK):
                 nc.tensor.transpose(turned[:, t, :], bias_rows[:, t:PASS:PACK], identity[:])
@@ -273,8 +272,8 @@ def tile_list_twin_critic_targets_kernel(
         load_tab(0)
         load_w(0, 0)
         load_tab_scales()
-        load_bias_and_discount()
         load_w(1, 0)
+        load_bias_and_discount()
         load_tab(1)
         load_w(LAST, 0)
         load_tab(LAST)

@@ -55,7 +55,7 @@ def tile_list_twin_critic_targets_kernel(
 
         tab_sc = keep.tile([P, T // 4], I32, name="tab_sc", tag="tab_sc", align_bytes=ALIGN)
         qa_sc = keep.tile([P, H_PASSES, N // 4], I32, name="qa_sc", align_bytes=ALIGN)
-        nc.vector.memset(tab_sc[:], 0)
+        nc.gpsimd.memset(tab_sc[:], 0)
         bias_rows = keep.tile([P, PASS], F32, name="bias_rows", tag="least_0_0", align_bytes=ALIGN)
         disc_rows = keep.tile([P, P], F32, name="disc_rows", tag="least_1_0", align_bytes=ALIGN)
         nc.vector.memset(bias_rows[:], 0.0)
@@ -81,8 +81,8 @@ def tile_list_twin_critic_targets_kernel(
             tab[a] = keep.tile([P, T], I32, name="tab_%d" % a, align_bytes=ALIGN)
             nc.sync.dma_start(tab[a][:], tab_words[a].rearrange("p t i -> p (t i)").bitcast(I32))
 
-        def load_tab_scales():
-            for q in range(QUADRANTS):
+        def load_tab_scales(quadrants):
+            for q in quadrants:
                 nc.sync.dma_start(
                     tab_sc[32 * q : 32 * q + SCALE_ROWS * K_PASSES, :],
                     tab_scales[:, SCALE_ROWS * q : SCALE_ROWS * (q + 1), :].bitcast(I32),
@@ -270,8 +270,9 @@ def tile_list_twin_critic_targets_kernel(
                 start = start + width
 
         load_tab(0)
+        load_tab_scales(range(QUADRANTS // 2))
         load_w(0, 0)
-        load_tab_scales()
+        load_tab_scales(range(QUADRANTS // 2, QUADRANTS))
         load_w(1, 0)
         load_bias_and_discount()
         load_tab(1)
@@ -290,7 +291,7 @@ def tile_list_twin_critic_targets_kernel(
         gather_words(0)
         round_w(0, 0, [(on_scalar, P)])
         gather_scales()
-        round_w(1, 0, [(on_vector, 96), (on_scalar, 32)])
+        round_w(1, 0, [(on_vector, 64), (on_scalar, 64)])
         quantize_w(0, 0)
         quantize_w(1, 0)
         for u in range(HALVES):

@@ -30,7 +30,7 @@ N_TILES = N // P
 QUADRANTS = 4
 SCALE_ROWS = 4
 LIST_COLS = COLS // 16
-RUN_F32 = 2
+RUN_F32 = 4
 RUN_BF16 = 2
 PSUM_BANKS = 8
 ALIGN = 256
@@ -138,12 +138,12 @@ def tile_list_twin_critic_targets_kernel(
 
         def round_w(a, b, copies):
             w_bf[a, b] = ring.tile([P, PACK * PASS], BF16, name="w_bf", align_bytes=ALIGN)
-            dst = w_bf[a, b][:].rearrange("p (s e m j) -> p m s j e", s=2, e=2, j=PACK)
+            dst = w_bf[a, b][:].rearrange("p (t m j) -> p m j t", t=PACK, j=PACK)
             per_piece = P // len(w_raw[a, b])
             start = 0
             for copy, share in copies:
                 piece, first = divmod(start, per_piece)
-                src = w_raw[a, b][piece][:].rearrange("p j (m s e) -> p m s j e", s=2, e=2)
+                src = w_raw[a, b][piece][:].rearrange("p j (m t) -> p m j t", t=PACK)
                 copy(dst[:, start : start + share], src[:, first : first + share])
                 start = start + share
 

from contextlib import ExitStack

import concourse.mybir as mybir
from concourse.masks import make_identity

K, T, S, H, N = 1536, 2048, 1024, 1024, 384
FLOPS = 2 * K * H * S + 2 * 2 * H * N * S

F32 = mybir.dt.float32
BF16 = mybir.dt.bfloat16
I32 = mybir.dt.int32
U32 = mybir.dt.uint32
U16 = mybir.dt.uint16
U8 = mybir.dt.uint8
FP8X4 = mybir.dt.float8_e4m3fn_x4
FP4X4 = mybir.dt.float4_e2m1fn_x4
RELU = mybir.ActivationFunctionType.Relu
COPY = mybir.ActivationFunctionType.Copy
ALU = mybir.AluOpType

P = 128
PACK = 4
PASS = P * PACK
K_PASSES = K // PASS
H_PASSES = H // PASS
LAST = K_PASSES - 1
COLS = 512
HALVES = S // COLS
N_TILES = N // P
QUADRANTS = 4
SCALE_ROWS = 4
LIST_COLS = COLS // 16
RUN_F32 = 4
RUN_BF16 = 2
PSUM_BANKS = 8
ALIGN = 256
PARTS = 2
PART = COLS // PARTS
QB_CALL = 256
H_SCALAR_COLS = 128
LAST_PIECES = (384, 128)


def tile_list_twin_critic_targets_kernel(
    tc, tab_words, tab_scales, offs, w1, b1, qa_words, qa_scales, qb, disc, gT, out
):
    nc = tc.nc
    with ExitStack() as ctx:
        keep = ctx.enter_context(tc.tile_pool(name="keep", bufs=1))
        ring = ctx.enter_context(tc.tile_pool(name="ring", bufs=3))
        psum = ctx.enter_context(tc.psum_pool(name="psum", bufs=PSUM_BANKS))

        offsets = keep.tile([P, S // 16], U16, name="offsets")
        nc.sync.dma_start(offsets[:], offs)

        tab_sc = keep.tile([P, T // 4], I32, name="tab_sc", tag="tab_sc", align_bytes=ALIGN)
        qa_sc = keep.tile([P, H_PASSES, N // 4], I32, name="qa_sc", align_bytes=ALIGN)
        nc.gpsimd.memset(tab_sc[:], 0)
        bias_rows = keep.tile([P, PASS], F32, name="bias_rows", tag="least_0_0", align_bytes=ALIGN)
        disc_rows = keep.tile([P, P], F32, name="disc_rows", tag="least_1_0", align_bytes=ALIGN)
        nc.vector.memset(bias_rows[:], 0.0)
        nc.vector.memset(disc_rows[:], 0.0)
        nc.vector.memset(qa_sc[:], 0)
        bias = keep.tile([P, PACK, H_PASSES], F32, name="bias")
        discount = keep.tile([P, N_TILES], F32, name="discount")
        qa = keep.tile([P, H_PASSES, N // 2], I32, name="qa", align_bytes=ALIGN)

        w_raw, tab, qb_raw, rewards = {}, {}, {}, {}

        def load_w(a, b, pieces=1):
            width = PASS // pieces
            w_raw[a, b] = []
            for n in range(pieces):
                tag = "w_raw_%d_%d_%d" % (a, b, n)
                piece = keep.tile([P, PACK, width], F32, name="w_raw", tag=tag, align_bytes=ALIGN)
                rows = w1[a * PASS : (a + 1) * PASS, b * PASS + n * width : b * PASS + (n + 1) * width]
                nc.sync.dma_start(piece[:], rows.rearrange("(p j) c -> p j c", j=PACK))
                w_raw[a, b].append(piece)

        def load_tab(a):
            tab[a] = keep.tile([P, T], I32, name="tab_%d" % a, align_bytes=ALIGN)
            nc.sync.dma_start(tab[a][:], tab_words[a].rearrange("p t i -> p (t i)").bitcast(I32))

        def load_tab_scales(quadrants):
            for q in quadrants:
                nc.sync.dma_start(
                    tab_sc[32 * q : 32 * q + SCALE_ROWS * K_PASSES, :],
                    tab_scales[:, SCALE_ROWS * q : SCALE_ROWS * (q + 1), :].bitcast(I32),
                )

        def load_bias_and_discount():
            identity = keep.tile([P, P], F32, name="identity", tag="least_2_0", align_bytes=ALIGN)
            make_identity(nc, identity[:])
            nc.sync.dma_start(bias_rows[0:H_PASSES, :], b1.rearrange("(b c) -> b c", b=H_PASSES))
            nc.sync.dma_start(disc_rows[0:N_TILES, :], disc.rearrange("(i p) -> i p", i=N_TILES))
            turned = psum.tile([P, PACK, P], F32, name="bank")
            for t in range(PACK):
                nc.tensor.transpose(turned[:, t, :], bias_rows[:, t:PASS:PACK], identity[:])
            nc.scalar.copy(bias[:], turned[:, :, 0:H_PASSES])
            turned = psum.tile([P, P], F32, name="bank")
            nc.tensor.transpose(turned[:], disc_rows[:], identity[:])
            nc.scalar.copy(discount[:], turned[:, 0:N_TILES])

        def load_qb(b):
            qb_raw[b] = keep.tile([P, PACK, N], F32, name="qb_raw", tag="qb_raw_%d" % b, align_bytes=ALIGN)
            nc.sync.dma_start(qb_raw[b][:], qb[b * PASS : (b + 1) * PASS, :].rearrange("(p t) n -> p t n", t=PACK))

        def load_qa():
            nc.sync.dma_start(qa[:], qa_words.rearrange("b p c -> p b c").bitcast(I32))
            for q in range(QUADRANTS):
                nc.sync.dma_start(
                    qa_sc[32 * q : 32 * q + SCALE_ROWS, :, :],
                    qa_scales[:, SCALE_ROWS * q : SCALE_ROWS * (q + 1), :].rearrange("b s n -> s b n").bitcast(I32),
                )

        def load_rewards(i):
            rewards[i] = keep.tile([P, T], F32, name="rewards_%d" % i, align_bytes=ALIGN)
            nc.sync.dma_start(rewards[i][:], gT[i * P : (i + 1) * P, :])

        v_sc = keep.tile([P, S], U8, name="v_sc", align_bytes=ALIGN)
        v_codes = [keep.tile([P, S], U32, name="v_codes_%d" % a, align_bytes=ALIGN) for a in range(K_PASSES)]

        def picks(first, last):
            return offsets[:, first * LIST_COLS : last * LIST_COLS]

        def gather_scales():
            nc.vector.tensor_copy(v_sc[:], tab_sc[:].bitcast(U8).indirect(picks(0, HALVES)))

        def gather_words(a, first=0, last=HALVES):
            window = tab[a][:].bitcast(U32)
            nc.vector.tensor_copy(v_codes[a][:, first * COLS : last * COLS], window.indirect(picks(first, last)))

        def half(u):
            return slice(u * COLS, (u + 1) * COLS)

        w_bf, w_codes, w_sc = {}, {}, {}
        banks, h_rows, h_bf, h_codes, h_sc = {}, {}, {}, {}, {}

        def round_w(a, b, copies):
            w_bf[a, b] = ring.tile([P, PACK * PASS], BF16, name="w_bf", align_bytes=ALIGN)
            dst = w_bf[a, b][:].rearrange("p (t m j) -> p m j t", t=PACK, j=PACK)
            per_piece = P // len(w_raw[a, b])
            start = 0
            for copy, share in copies:
                piece, first = divmod(start, per_piece)
                src = w_raw[a, b][piece][:].rearrange("p j (m t) -> p m j t", t=PACK)
                copy(dst[:, start : start + share], src[:, first : first + share])
                start = start + share

        def quantize_w(a, b, calls=1):
            w_codes[a, b] = keep.tile([P, PASS], U32, name="w_codes_%d_%d" % (a, b), align_bytes=ALIGN)
            w_sc[a, b] = keep.tile([P, PASS], U8, name="w_sc_%d_%d" % (a, b), align_bytes=ALIGN)
            width = PASS // calls
            for first in range(0, PASS, width):
                cols = slice(first, first + width)
                values = w_bf[a, b][:, first * PACK : (first + width) * PACK]
                nc.vector.quantize_mx(out=w_codes[a, b][:, cols].bitcast(FP8X4), scales=w_sc[a, b][:, cols], in_=values)

        def hidden_pass(a, b, u, slots=range(PACK), opening=0, closing=LAST):
            for t in slots:
                if a == opening:
                    banks[b, u, t] = psum.tile([P, COLS], F32, name="bank")
                cols = slice(t * P, (t + 1) * P)
                nc.tensor.matmul_mx(
                    out=banks[b, u, t][:],
                    lhsT=w_codes[a, b][:, cols].bitcast(FP8X4),
                    lhsT_scale=w_sc[a, b][:, cols],
                    rhs=v_codes[a][:, half(u)].bitcast(FP8X4),
                    rhs_scale=v_sc[SCALE_ROWS * a : P, half(u)],
                    start=(a == opening),
                    stop=(a == closing),
                )

        def relu_out(b, u):
            h_rows[b, u] = keep.tile([P, PACK, COLS], BF16, name="h_rows_%d_%d" % (b, u), align_bytes=ALIGN)
            for t in range(PACK):
                nc.scalar.activation(h_rows[b, u][:, t, :], banks[b, u, t][:], RELU, bias=bias[:, t, b : b + 1])

        def interleave_views(grouped, rows, run):
            dst = grouped.rearrange("p (c i t) -> p c t i", i=run, t=PACK)
            src = rows.rearrange("p t (c i) -> p c t i", i=run)
            return dst, src

        def h_views(b, u, tag):
            h_bf[b, u] = keep.tile([P, COLS * PACK], BF16, name="h_bf", tag=tag, align_bytes=ALIGN)
            return interleave_views(h_bf[b, u][:], h_rows[b, u][:], RUN_BF16)

        def quantize_h(b, u, tag):
            h_codes[b, u] = keep.tile([P, COLS], U32, name="h_codes", tag=tag, align_bytes=ALIGN)
            h_sc[b, u] = keep.tile([P, COLS], U8, name="h_sc_%d_%d" % (b, u), align_bytes=ALIGN)
            nc.vector.quantize_mx(out=h_codes[b, u][:].bitcast(FP8X4), scales=h_sc[b, u][:], in_=h_bf[b, u][:])

        def part_cols(n):
            return slice(n * PART, (n + 1) * PART)

        def interleave_part(b, u, n, copy, tag):
            part = keep.tile([P, PART * PACK], BF16, name="h_part", tag=tag, align_bytes=ALIGN)
            copy(*interleave_views(part[:], h_rows[b, u][:, :, part_cols(n)], RUN_BF16))
            return part

        def quantize_part(b, u, n, part, tag=None):
            if n == 0:
                h_codes[b, u] = keep.tile([P, COLS], U32, name="h_codes", tag=tag or "h_codes_%d_%d" % (b, u), align_bytes=ALIGN)
                h_sc[b, u] = keep.tile([P, COLS], U8, name="h_sc_%d_%d" % (b, u), align_bytes=ALIGN)
            cols = part_cols(n)
            nc.vector.quantize_mx(out=h_codes[b, u][:, cols].bitcast(FP8X4), scales=h_sc[b, u][:, cols], in_=part[:])

        qb_codes = keep.tile([P, H_PASSES * N], U32, name="qb_codes", align_bytes=ALIGN)
        qb_sc = keep.tile([P, H_PASSES * N], U8, name="qb_sc", align_bytes=ALIGN)

        qb_bf = {}

        def round_qb(b):
            if b == 0:
                qb_bf["all"] = keep.tile([P, H_PASSES * N * PACK], BF16, name="qb_bf", tag="w_raw_1_1_0", align_bytes=ALIGN)
            grouped = qb_bf["all"][:, b * N * PACK : (b + 1) * N * PACK]
            nc.vector.tensor_copy(*interleave_views(grouped, qb_raw[b][:], RUN_F32))

        def quantize_qb(call):
            lo, hi = call * QB_CALL, (call + 1) * QB_CALL
            values = qb_bf["all"][:, lo * PACK : hi * PACK]
            nc.vector.quantize_mx(out=qb_codes[:, lo:hi].bitcast(FP8X4), scales=qb_sc[:, lo:hi], in_=values)

        def qa_weights(i, b):
            codes = qa[:, b, :].bitcast(U8)[:, 2 * i * P : 2 * (i + 1) * P].bitcast(FP4X4)
            return codes, qa_sc[:, b, :].bitcast(U8)[:, i * P : (i + 1) * P]

        def qb_weights(i, b):
            cols = slice(b * N + i * P, b * N + (i + 1) * P)
            return qb_codes[:, cols].bitcast(FP8X4), qb_sc[:, cols]

        sums, least = {}, {}

        def critic_passes(b, u, critics="ab", tiles=range(N_TILES), tokens=slice(0, COLS)):
            span = tokens.stop - tokens.start
            for i in tiles:
                for name in critics:
                    if b == 0 and tokens.start == 0:
                        sums[name, i, u] = psum.tile([P, COLS], F32, name="bank")
                    codes, scales = qa_weights(i, b) if name == "a" else qb_weights(i, b)
                    width = span
                    for first in range(tokens.start, tokens.stop, width):
                        cols = slice(first, first + width)
                        nc.tensor.matmul_mx(
                            out=sums[name, i, u][:, cols],
                            lhsT=codes,
                            lhsT_scale=scales,
                            rhs=h_codes[b, u][:, cols].bitcast(FP8X4),
                            rhs_scale=h_sc[b, u][:, cols],
                            start=(b == 0 and first == 0),
                            stop=(b == H_PASSES - 1 and cols.stop == COLS),
                        )

        def smaller_critic(i, u):
            ya_sb = keep.tile([P, COLS], F32, name="ya_sb", tag="ya_sb_%d" % i, align_bytes=ALIGN)
            nc.scalar.copy(ya_sb[:], sums["a", i, u][:])
            least[i, u] = keep.tile([P, COLS], F32, name="least", tag="least_%d_%d" % (i, u), align_bytes=ALIGN)
            nc.vector.tensor_tensor(least[i, u][:], sums["b", i, u][:], ya_sb[:], ALU.min)

        def finish(i, u, widths=(COLS,)):
            scaled = ring.tile([P, COLS], F32, name="scaled", bufs=N_TILES * HALVES, align_bytes=ALIGN)
            nc.scalar.activation(scaled[:], least[i, u][:], COPY, scale=discount[:, i : i + 1])
            start = 0
            for width in widths:
                first = u * COLS + start
                picked = rewards[i][:].indirect(offsets[:, first // 16 : (first + width) // 16])
                target = ring.tile([P, width], F32, name="target", bufs=4, align_bytes=ALIGN)
                nc.vector.tensor_tensor(target[:], picked, scaled[:, start : start + width], ALU.add)
                nc.sync.dma_start(out[i * P : (i + 1) * P, first : first + width], target[:])
                start = start + width

        load_tab(0)
        load_tab_scales(range(QUADRANTS // 2))
        load_w(0, 0)
        load_tab_scales(range(QUADRANTS // 2, QUADRANTS))
        load_w(1, 0)
        load_bias_and_discount()
        load_tab(1)
        load_w(LAST, 0)
        load_tab(LAST)
        for a in range(LAST):
            load_w(a, 1)
        load_w(LAST, 1, 2)
        for b in range(H_PASSES):
            load_qb(b)
        load_qa()
        for i in range(N_TILES):
            load_rewards(i)

        on_vector, on_scalar = nc.vector.tensor_copy, nc.scalar.copy
        gather_words(0)
        round_w(0, 0, [(on_scalar, P)])
        gather_scales()
        round_w(1, 0, [(on_vector, 64), (on_scalar, 64)])
        quantize_w(0, 0)
        quantize_w(1, 0)
        for u in range(HALVES):
            gather_words(1, u, u + 1)
        round_w(LAST, 0, [(on_vector, 64), (on_scalar, 64)])
        quantize_w(LAST, 0)
        for a in (0, 1):
            hidden_pass(a, 0, 0)
        for a in (1, 0):
            hidden_pass(a, 0, 1, opening=1)
        for u in range(HALVES):
            gather_words(LAST, u, u + 1)
        for u in range(HALVES):
            hidden_pass(LAST, 0, u, opening=u)
            relu_out(0, u)

        for a in range(LAST):
            round_w(a, 1, [(on_vector, P)])
            quantize_w(a, 1)
        round_w(LAST, 1, [(on_vector, 64), (on_vector, 64)])
        quantize_w(LAST, 1, PACK)
        nc.scalar.copy(*h_views(0, 0, "h_bf_0_0"))
        for a in range(K_PASSES):
            hidden_pass(a, 1, 0)
        hidden_pass(0, 1, 1, closing=1)
        for t in range(PACK):
            for a in (LAST, 1):
                hidden_pass(a, 1, 1, [t], closing=1)
        round_qb(0)
        for u in range(HALVES):
            relu_out(1, u)

        last = N_TILES - 1
        quantize_h(0, 0, "qb_raw_0")
        quantize_qb(0)
        round_qb(1)
        parts = [interleave_part(1, 0, n, on_vector, "h_part_%d" % n) for n in range(PARTS)]
        critic_passes(0, 0, tiles=range(last))
        critic_passes(0, 0, "a", [last])
        for n in range(PARTS):
            quantize_part(1, 0, n, parts[n])
        for n in range(PARTS):
            critic_passes(1, 0, "a", tokens=part_cols(n))
        quantize_qb(1)
        critic_passes(1, 0, "b", [0])
        critic_passes(0, 0, "b", [last])
        quantize_qb(2)
        critic_passes(1, 0, "b", range(1, N_TILES))

        head = interleave_part(0, 1, 0, on_vector, "h_part_0")
        tail = keep.tile([P, PART * PACK], BF16, name="h_part", tag="h_part_1", align_bytes=ALIGN)
        dst, src = interleave_views(tail[:], h_rows[0, 1][:, :, part_cols(1)], RUN_BF16)
        cut = H_SCALAR_COLS // RUN_BF16
        nc.scalar.copy(dst[:, 0:cut], src[:, 0:cut])
        nc.vector.tensor_copy(dst[:, cut : PART // RUN_BF16], src[:, cut : PART // RUN_BF16])
        quantize_part(0, 1, 0, head, "tab_sc")
        for i in range(last):
            smaller_critic(i, 0)
        critic_passes(0, 1, tokens=part_cols(0))
        h_codes[0, 1] = keep.tile([P, COLS], U32, name="h_codes", tag="ya_sb_0", align_bytes=ALIGN)
        quantize_part(0, 1, 1, tail)
        smaller_critic(last, 0)
        critic_passes(0, 1, tokens=part_cols(1))

        for n in range(PARTS):
            finish(n, 0)
            quantize_part(1, 1, n, interleave_part(1, 1, n, on_scalar, "ya_sb_%d" % (n + 1)))
            critic_passes(1, 1, tokens=part_cols(n))
        finish(last, 0)

        smaller_critic(0, 1)
        for i in range(1, N_TILES):
            smaller_critic(i, 1)
            finish(i - 1, 1)
        finish(last, 1, LAST_PIECES)
